import numpy as np
import ml_dtypes


def mxq(x, axis, fmt="e4m3"):
    dtype, down = {"e4m3": (ml_dtypes.float8_e4m3fn, 7), "e5m2": (ml_dtypes.float8_e5m2, 14)}[fmt]
    v = np.moveaxis(np.asarray(x, np.float32).astype(ml_dtypes.bfloat16).astype(np.float64), axis, -1)
    blocks = v.reshape(v.shape[:-1] + (-1, 32))
    amax = np.abs(blocks).max(-1, keepdims=True)
    byte = np.maximum(np.where(amax > 0, np.frexp(amax)[1] - 1 + 127, 0) - down, 1)
    scale = np.exp2(byte - 127.0)
    codes = (blocks / scale).astype(np.float32).astype(dtype).astype(np.float64)
    return np.moveaxis((codes * scale).reshape(v.shape), -1, axis)


WIDE = False


def mx_kscale(k):
    if not WIDE:
        return np.ones(k)
    levels = np.array([10, -10, 5, -5, 0])
    if k % 512:
        return np.exp2(np.random.permutation(np.resize(levels, k // 32))).repeat(32)
    a = np.empty((k // 512, 16))
    for p in range(k // 512):
        a[p, :8] = np.random.permutation(np.resize(levels, 8))
        for g in range(8):
            far = levels[np.abs(levels - a[p, g]) >= 10]
            a[p, g + 8] = far[np.random.randint(len(far))]
    return np.exp2(a.ravel()).repeat(32)


def f64(x):
    return np.asarray(x).astype(np.float64)


def striped(idx):
    return np.tile(idx.reshape(-1, 16).T, (8, 1)).astype(np.uint16)


def unstriped(offs):
    return offs[:16].T.reshape(-1).astype(np.int64)


E2M1 = np.array([0.0, 0.5, 1.0, 1.5, 2.0, 3.0, 4.0, 6.0, -0.0, -0.5, -1.0, -1.5, -2.0, -3.0, -4.0, -6.0])


def pack_weight(w, fmt):
    k, n = w.shape
    w = f64(np.asarray(w, np.float32).astype(ml_dtypes.bfloat16)).reshape(k // 32, 32, n)
    amax = np.abs(w).max(1)
    if fmt == "e4m3":
        byte = np.frexp(amax)[1] - 1 + 127 - 7
    else:
        mant, ex = np.frexp(amax / 6.0)
        byte = np.where(mant > 0.5, ex, ex - 1) + 127
    byte = np.clip(np.where(amax > 0, byte, 1), 1, 254)
    scaled = (w * np.exp2(127.0 - byte)[:, None, :]).reshape(k, n).astype(np.float32)
    by_word = np.ascontiguousarray(scaled.reshape(k // 512, 128, 4, n).transpose(0, 1, 3, 2))
    if fmt == "e4m3":
        words = by_word.astype(ml_dtypes.float8_e4m3fn).view(np.uint8)
    else:
        c = by_word.astype(ml_dtypes.float4_e2m1fn).view(np.uint8) & 0xF
        words = (c[..., 0::2] | (c[..., 1::2] << 4)).reshape(k // 512, 128, 2 * n)
    return np.ascontiguousarray(words), np.ascontiguousarray(byte.astype(np.uint8).reshape(k // 512, 16, n))


def unpack_weight(words, scales, fmt):
    g, _, n = scales.shape
    words = np.ascontiguousarray(words).reshape(g, 128, n, -1)
    if fmt == "e4m3":
        vals = words.view(ml_dtypes.float8_e4m3fn).astype(np.float64)
    else:
        nib = np.empty((g, 128, n, 4), np.uint8)
        nib[..., 0::2] = words & 0xF
        nib[..., 1::2] = words >> 4
        vals = E2M1[nib]
    vals = vals * np.repeat(np.exp2(scales.astype(np.float64) - 127.0), 8, axis=1)[..., None]
    return vals.transpose(0, 1, 3, 2).reshape(g * 512, n)


def gelu(v):
    return 0.5 * v * (1.0 + np.tanh(np.sqrt(2.0 / np.pi) * (v + 0.044715 * v**3)))


K, T, S, H, T2, P, N = 512, 4096, 1024, 1024, 2048, 1024, 512

def setup_inputs():
    n = np.random.standard_normal
    s = mx_kscale(K)[:, None]
    u = mx_kscale(H)[:, None]
    tab_words, tab_scales = pack_weight(n((K, T)) * s, "e4m3")
    w1_words, w1_scales = pack_weight(n((K, H)) / np.sqrt(K) / s, "e2m1")
    w3_words, w3_scales = pack_weight(1.5 * n((H, N)) / np.sqrt(H) / u, "e4m3")
    return {
        "tab_words": tab_words, "tab_scales": tab_scales,
        "offs": striped(np.random.permutation(T)[:S]),
        "offs2": striped(np.random.permutation(T2)[:S]),
        "offs3": striped(np.random.permutation(T2)[:P]),
        "offs4": striped(np.random.permutation(T2)[:P]),
        "page0": n((H, T2)).astype(np.float32),
        "wgs": np.exp(0.3 * n((128, S))).astype(np.float32),
        "w1_words": w1_words, "w1_scales": w1_scales,
        "w2": (n((K, H)) / np.sqrt(K) / s).astype(np.float32),
        "gain": (np.exp(0.3 * n(H)) * u[:, 0]).astype(np.float32),
        "w3_words": w3_words, "w3_scales": w3_scales,
    }

def reference(tab_words, tab_scales, offs, offs2, offs3, offs4, page0, wgs,
              w1_words, w1_scales, w2, gain, w3_words, w3_scales):
    v = unpack_weight(tab_words, tab_scales, "e4m3")[:, unstriped(offs)]
    w1 = unpack_weight(w1_words, w1_scales, "e2m1")
    w3 = unpack_weight(w3_words, w3_scales, "e4m3")
    a = w1.T @ v
    b = mxq(f64(w2), 0, "e4m3").T @ v
    h = a - np.tanh(b)
    page = f64(page0).copy()
    page[:, unstriped(offs2)] = np.tile(f64(wgs), (H // 128, 1)) * h
    x1 = page[:, unstriped(offs3)]
    x2 = page[:, unstriped(offs4)]
    z = f64(gain)[:, None] * (x1 / (1.0 + np.abs(x2)))
    return w3.T @ mxq(z, 0, "e4m3")

@@ -1,0 +1,315 @@
+from contextlib import ExitStack
+
+import concourse.mybir as mybir
+from concourse.masks import make_identity
+
+K, T, S, H, T2, M, N = 512, 4096, 1024, 1024, 2048, 1024, 512
+FLOPS = 2 * K * H * S * 2 + 2 * H * N * M
+
+F32 = mybir.dt.float32
+BF16 = mybir.dt.bfloat16
+I32 = mybir.dt.int32
+U32 = mybir.dt.uint32
+U16 = mybir.dt.uint16
+U8 = mybir.dt.uint8
+FP8X4 = mybir.dt.float8_e4m3fn_x4
+FP4X4 = mybir.dt.float4_e2m1fn_x4
+ACT = mybir.ActivationFunctionType
+MULT = mybir.AluOpType.mult
+
+P = 128
+PACK = 4
+PASS = P * PACK
+BLOCKS = H // PASS
+CHUNK = 256
+PAGE_BUFS = 5
+WG_PARTS = ((0, CHUNK), (CHUNK, 2 * CHUNK), (2 * CHUNK, S))
+PIECES = ((0, 512), (512, 768), (768, 1024))
+
+
+def entries(offsets, lo, hi):
+    return offsets[:, lo // 16 : hi // 16]
+
+
+def interleaved(dst, src):
+    return (
+        dst.rearrange("p (c i t) -> p c t i", i=4, t=PACK),
+        src.rearrange("p t (c i) -> p c t i", i=4),
+    )
+
+
+def tile_list_trie_leak_audit_kernel(
+    tc, tab_words, tab_scales, offs, offs2, offs3, offs4, page0, wgs,
+    w1_words, w1_scales, w2, gain, w3_words, w3_scales, out,
+):
+    nc = tc.nc
+    with ExitStack() as ctx:
+        lists = ctx.enter_context(tc.tile_pool(name="lists", bufs=1))
+        keep = ctx.enter_context(tc.tile_pool(name="keep", bufs=1))
+        work = ctx.enter_context(tc.tile_pool(name="work", bufs=1))
+        psum = ctx.enter_context(tc.psum_pool(name="psum", bufs=4))
+
+        idx = lists.tile([P, S // 16], U16)
+        idx2 = lists.tile([P, S // 16], U16)
+        idx3 = lists.tile([P, M // 16], U16)
+        idx4 = lists.tile([P, M // 16], U16)
+
+        tab_w = keep.tile([P, T], I32, align_bytes=64)
+        tab_s = keep.tile([P, T], U8, align_bytes=64)
+        w1_w = keep.tile([P, 2 * H], U8, align_bytes=64)
+        w1_s = keep.tile([P, H], U8, align_bytes=64)
+        w3_w = keep.tile([P, BLOCKS * N], I32, align_bytes=64)
+        w3_s = keep.tile([P, BLOCKS * N], U8, align_bytes=64)
+        v_w = keep.tile([P, S], U32, align_bytes=64)
+        v_s = keep.tile([P, S], U8, align_bytes=64)
+        wg = keep.tile([P, PACK, S], F32)
+        gain_sb = keep.tile([P, BLOCKS, PACK], F32)
+        ident = keep.tile([P, P], F32)
+        one = keep.tile([P, 1], F32)
+
+        nc.vector.memset(tab_s[:].bitcast(I32), 0)
+        nc.vector.memset(w1_s[:].bitcast(I32), 0)
+        nc.gpsimd.memset(w3_s[:].bitcast(I32), 0)
+        nc.gpsimd.memset(one[:], 1.0)
+        make_identity(nc, ident[:])
+
+        def load_w2(b):
+            raw = work.tile([P, PACK, PASS], F32, name="raw", tag="wide", bufs=2)
+            nc.sync.dma_start(
+                out=raw[:],
+                in_=w2.rearrange("(p j) c -> p j c", j=PACK)[:, :, b * PASS : (b + 1) * PASS],
+            )
+            return raw
+
+        def quantize_w2(raw, b, copy):
+            rounded = work.tile([P, PACK * PASS], BF16, name="rounded", tag="rounded", bufs=3, align_bytes=64)
+            copy(*interleaved(rounded[:], raw[:]))
+            codes = keep.tile([P, PASS], U32, name="w2_w%d" % b, align_bytes=64)
+            scales = keep.tile([P, PASS], U8, name="w2_s%d" % b, align_bytes=64)
+            nc.vector.quantize_mx(out=codes[:].bitcast(FP8X4), scales=scales[:], in_=rounded[:])
+            return codes, scales
+
+        def load_wg(part):
+            lo, hi = WG_PARTS[part]
+            rows = wgs.rearrange("(i t) c -> i t c", t=PACK)
+            for quadrant in (0, 2, 1, 3):
+                nc.sync.dma_start(
+                    out=wg[32 * quadrant : 32 * quadrant + 32, :, lo:hi], in_=rows[:, :, lo:hi]
+                )
+
+        def load_page(b, t):
+            page = work.tile([P, T2], F32, name="page", tag="page", bufs=PAGE_BUFS)
+            nc.sync.dma_start(
+                out=page[:],
+                in_=page0.rearrange("(b p t) c -> b t p c", b=BLOCKS, t=PACK)[b, t],
+            )
+            return page
+
+        for quadrant in range(4):
+            nc.sync.dma_start(
+                out=tab_s[32 * quadrant : 32 * quadrant + 4, :].bitcast(I32),
+                in_=tab_scales[0, 4 * quadrant : 4 * quadrant + 4, :].bitcast(I32),
+            )
+        nc.sync.dma_start(idx[:], offs)
+        w2_raw0 = load_w2(0)
+        nc.sync.dma_start(
+            out=tab_w[:], in_=tab_words[0].rearrange("p n t -> p (n t)").bitcast(I32)
+        )
+        nc.sync.dma_start(out=w1_w[:].bitcast(I32), in_=w1_words[0].bitcast(I32))
+        for quadrant in range(4):
+            nc.sync.dma_start(
+                out=w1_s[32 * quadrant : 32 * quadrant + 4, :].bitcast(I32),
+                in_=w1_scales[0, 4 * quadrant : 4 * quadrant + 4, :].bitcast(I32),
+            )
+        w2_raw1 = load_w2(1)
+        pages = {(0, 0): load_page(0, 0)}
+        nc.sync.dma_start(idx2[:], offs2)
+        load_wg(0)
+        pages[0, 1] = load_page(0, 1)
+        load_wg(1)
+        pages[0, 2] = load_page(0, 2)
+        pages[0, 3] = load_page(0, 3)
+        load_wg(2)
+        nc.sync.dma_start(idx4[:], offs4)
+        nc.sync.dma_start(idx3[:], offs3)
+        nc.sync.dma_start(
+            out=gain_sb[:], in_=gain.rearrange("(b p t) -> p b t", b=BLOCKS, t=PACK)
+        )
+        pages[1, 0] = load_page(1, 0)
+        for b in range(BLOCKS):
+            nc.sync.dma_start(
+                out=w3_w[:, b * N : (b + 1) * N],
+                in_=w3_words[b].rearrange("p n t -> p (n t)").bitcast(I32),
+            )
+        for quadrant in range(4):
+            nc.sync.dma_start(
+                out=w3_s[32 * quadrant : 32 * quadrant + 4, :].bitcast(I32).rearrange("r (b n) -> r b n", b=BLOCKS),
+                in_=w3_scales[:, 4 * quadrant : 4 * quadrant + 4, :].bitcast(I32).rearrange("b r n -> r b n"),
+            )
+
+        nc.vector.tensor_copy(v_s[:], tab_s[:].indirect(idx[:]))
+        w2_mx = [quantize_w2(w2_raw0, 0, nc.scalar.copy)]
+        for lo in range(0, S, S // 2):
+            hi = lo + S // 2
+            nc.vector.tensor_copy(
+                v_w[:, lo:hi], tab_w[:].bitcast(U32).indirect(entries(idx, lo, hi))
+            )
+        w2_mx.append(quantize_w2(w2_raw1, 1, nc.vector.tensor_copy))
+
+        def features(b, q, h, rows, copy_first):
+            first = work.tile([P, 2, PACK, P], F32, name="first", tag="first", bufs=2)
+            second = work.tile([P, 2, PACK, P], F32, name="second", tag="second%d" % (q % 2), align_bytes=64)
+            for u in range(2):
+                cols = slice(q * CHUNK + u * P, q * CHUNK + (u + 1) * P)
+                w2_w, w2_s = w2_mx[b]
+                acc2 = psum.tile([P, PASS], F32, name="acc2", tag="sums")
+                nc.tensor.matmul_mx(
+                    out=acc2[:],
+                    lhsT=v_w[:, cols].bitcast(FP8X4), lhsT_scale=v_s[:, cols],
+                    rhs=w2_w[:].bitcast(FP8X4), rhs_scale=w2_s[:],
+                    start=True, stop=True,
+                )
+                acc1 = psum.tile([P, PASS], F32, name="acc1", tag="sums")
+                nc.tensor.matmul_mx(
+                    out=acc1[:],
+                    lhsT=v_w[:, cols].bitcast(FP8X4), lhsT_scale=v_s[:, cols],
+                    rhs=w1_w[:, 2 * b * PASS : 2 * (b + 1) * PASS].bitcast(FP4X4),
+                    rhs_scale=w1_s[:, b * PASS : (b + 1) * PASS],
+                    start=True, stop=True,
+                )
+                nc.scalar.activation(
+                    second[:, u], acc2[:].rearrange("p (m t) -> p t m", t=PACK), ACT.Tanh, scale=-1.0
+                )
+                copy_first(first[:, u], acc1[:].rearrange("p (m t) -> p t m", t=PACK))
+            for t0 in range(0, PACK, rows):
+                turned = psum.tile([P, rows, CHUNK], F32, name="turned", tag="turned")
+                for e in range(rows):
+                    for u in range(2):
+                        dst = turned[:, e, u * P : (u + 1) * P]
+                        t = t0 + e
+                        nc.tensor.matmul(dst, first[:, u, t, :], ident[:], start=True, stop=False, is_transpose=True)
+                        nc.tensor.matmul(dst, second[:, u, t, :], ident[:], start=False, stop=True, is_transpose=True)
+                nc.scalar.copy(h[:, t0 : t0 + rows, q * CHUNK : (q + 1) * CHUNK], turned[:])
+
+        def scatter(b, t, h, lo, hi):
+            nc.vector.tensor_tensor(
+                pages[b, t][:].indirect(entries(idx2, lo, hi)),
+                h[:, t, lo:hi], wg[:, t, lo:hi], MULT,
+            )
+
+        def scatter_all(b, t, h):
+            scatter(b, t, h, 0, S)
+
+        def fetch_link(b, t):
+            damp = work.tile([P, M], F32, name="damp", tag="damp", bufs=4)
+            nc.vector.tensor_copy(damp[:], pages[b, t][:].indirect(idx4[:]))
+            return damp
+
+        def damping(damp, tag):
+            root = work.tile([P, M], F32, name="root", tag=tag, align_bytes=64)
+            nc.scalar.activation(root[:], damp[:], ACT.Abs)
+            nc.scalar.activation(root[:], root[:], ACT.Abs_reciprocal_sqrt, bias=one[:])
+            nc.scalar.activation(damp[:], root[:], ACT.Square)
+            return root
+
+        def fetch_node(b, t, damp, z, lo, hi, factor):
+            nc.scalar.activation(factor, damp[:, lo:hi], ACT.Copy, scale=gain_sb[:, b, t : t + 1])
+            nc.vector.tensor_tensor(
+                z[:, t, lo:hi], pages[b, t][:].indirect(entries(idx3, lo, hi)), factor, MULT
+            )
+
+        z_w = [keep.tile([P, M], U32, name="z_w%d" % b, align_bytes=64) for b in range(BLOCKS)]
+        z_s = [keep.tile([P, M], U8, name="z_s%d" % b, align_bytes=64) for b in range(BLOCKS)]
+
+        def quantize_z(b, z, lo, hi, copy, part):
+            copy(*interleaved(part, z[:, :, lo:hi]))
+            nc.vector.quantize_mx(out=z_w[b][:, lo:hi].bitcast(FP8X4), scales=z_s[b][:, lo:hi], in_=part)
+
+        def rounding_tile(lo, hi):
+            rounded = work.tile([P, PACK * PASS], BF16, name="rounded", tag="rounded", bufs=3, align_bytes=64)
+            return rounded[:, : PACK * (hi - lo)]
+
+        def scores_pass(b, banks, lo, hi):
+            for n in range(N // P):
+                cols = slice(b * N + n * P, b * N + (n + 1) * P)
+                nc.tensor.matmul_mx(
+                    out=banks[n][:, : hi - lo],
+                    lhsT=w3_w[:, cols].bitcast(FP8X4), lhsT_scale=w3_s[:, cols],
+                    rhs=z_w[b][:, lo:hi].bitcast(FP8X4), rhs_scale=z_s[b][:, lo:hi],
+                    start=(b == 0), stop=(b == BLOCKS - 1),
+                )
+
+        def score_banks(tag):
+            return [psum.tile([P, PASS], F32, name="scores", tag=tag) for n in range(N // P)]
+
+        out_rows = out.rearrange("(n p) m -> p n m", p=P)
+
+        def store(banks, first_n, last_n, lo, hi, copy, staged):
+            for n in range(first_n, last_n):
+                copy(staged[:, n - first_n, : hi - lo], banks[n][:, : hi - lo])
+            nc.sync.dma_start(
+                out=out_rows[:, first_n:last_n, lo:hi], in_=staged[:, : last_n - first_n, : hi - lo]
+            )
+
+        h0 = work.tile([P, PACK, S], F32, name="h0", tag="rows0", align_bytes=64)
+        for q in range(S // CHUNK):
+            if q == 0:
+                features(0, q, h0, 1, nc.vector.tensor_copy)
+            else:
+                features(0, q, h0, 2, nc.scalar.copy)
+            for t in range(PACK):
+                scatter(0, t, h0, q * CHUNK, (q + 1) * CHUNK)
+        h1 = work.tile([P, PACK, S], F32, name="h1", tag="rows1", align_bytes=64)
+        for q in range(S // CHUNK):
+            features(1, q, h1, 2, nc.scalar.copy)
+        damps = {(0, t): fetch_link(0, t) for t in range(PACK)}
+        scatter_all(1, 0, h1)
+
+        z0 = work.tile([P, PACK, M], F32, name="z0", tag="rows0", align_bytes=64)
+        for t in range(PACK):
+            damping(damps[0, t], "second1")
+            fetch_node(0, t, damps[0, t], z0, 0, M, damps[0, t][:])
+            damps[1, t] = fetch_link(1, t)
+            if t + 1 < PACK:
+                pages[1, t + 1] = load_page(1, t + 1)
+                scatter_all(1, t + 1, h1)
+
+        z1 = work.tile([P, PACK, M], F32, name="z1", tag="rows1", align_bytes=64)
+        (a_lo, a_hi), (b_lo, b_hi), (c_lo, c_hi) = PIECES
+        last = PACK - 1
+        for t in range(last):
+            damping(damps[1, t], "second1")
+            fetch_node(1, t, damps[1, t], z1, a_lo, a_hi, damps[1, t][:, a_lo:a_hi])
+        rounded0 = work.tile([P, PACK * M], BF16, name="rounded0", tag="second1", align_bytes=64)
+        quantize_z(0, z0, 0, M, nc.scalar.copy, rounded0[:])
+        root = damping(damps[1, last], "rows0")
+        fetch_node(1, last, damps[1, last], z1, a_lo, a_hi, damps[1, last][:, a_lo:a_hi])
+        banks_a = score_banks("sums")
+        banks_c = score_banks("turned")
+        scores_pass(0, banks_a, a_lo, a_hi)
+        scores_pass(0, banks_c, c_lo, c_hi)
+
+        width = b_hi - b_lo
+        for t in range(PACK):
+            fetch_node(1, t, damps[1, t], z1, b_lo, b_hi, root[:, t * width : (t + 1) * width])
+        quantize_z(1, z1, a_lo, a_hi, nc.scalar.copy, rounding_tile(a_lo, a_hi))
+        scores_pass(1, banks_a, a_lo, a_hi)
+        for t in range(last):
+            fetch_node(1, t, damps[1, t], z1, c_lo, c_hi, z1[:, t, a_lo : a_lo + width])
+        quantize_z(1, z1, b_lo, b_hi, nc.scalar.copy, rounding_tile(b_lo, b_hi))
+        fetch_node(1, last, damps[1, last], z1, c_lo, c_hi, z1[:, last, b_lo:b_hi])
+
+        staged_a = work.tile([P, PACK, PASS], F32, name="staged_a", tag="wide", bufs=2)
+        store(banks_a, 0, 4, a_lo, a_hi, nc.scalar.copy, staged_a)
+        banks_b = score_banks("sums")
+        for b in range(BLOCKS):
+            scores_pass(b, banks_b, b_lo, b_hi)
+        staged_b = work.tile([P, PACK, PASS], F32, name="staged_b", tag="wide", bufs=2)
+        store(banks_b, 0, 4, b_lo, b_hi, nc.scalar.copy, staged_b)
+
+        quantize_z(1, z1, c_lo, c_hi, nc.vector.tensor_copy, rounding_tile(c_lo, c_hi))
+        scores_pass(1, banks_c, c_lo, c_hi)
+        staged_c = work.tile([P, 2, c_hi - c_lo], F32, name="staged_c")
+        staged_d = work.tile([P, 2, c_hi - c_lo], F32, name="staged_d")
+        store(banks_c, 0, 2, c_lo, c_hi, nc.vector.tensor_copy, staged_c)
+        store(banks_c, 2, 4, c_lo, c_hi, nc.scalar.copy, staged_d)

@@ -23,8 +23,7 @@ PASS = P * PACK
 BLOCKS = H // PASS
 CHUNK = 256
 PAGE_BUFS = 5
-WG_PARTS = ((0, CHUNK), (CHUNK, 2 * CHUNK), (2 * CHUNK, S))
-PIECES = ((0, 512), (512, 768), (768, 1024))
+PIECES = ((0, 256), (256, 512), (512, 768), (768, 1024))
 
 
 def entries(offsets, lo, hi):
@@ -74,27 +73,27 @@ def tile_list_trie_leak_audit_kernel(
         make_identity(nc, ident[:])
 
         def load_w2(b):
-            raw = work.tile([P, PACK, PASS], F32, name="raw", tag="wide", bufs=2)
+            raw = work.tile([P, PACK, PASS], F32, name="raw", tag="wide", bufs=4)
             nc.sync.dma_start(
                 out=raw[:],
                 in_=w2.rearrange("(p j) c -> p j c", j=PACK)[:, :, b * PASS : (b + 1) * PASS],
             )
             return raw
 
-        def quantize_w2(raw, b, copy):
+        def quantize_w2(raw, b, copy, width):
             rounded = work.tile([P, PACK * PASS], BF16, name="rounded", tag="rounded", bufs=3, align_bytes=64)
-            copy(*interleaved(rounded[:], raw[:]))
+            for lo in range(0, PASS, width):
+                copy(*interleaved(rounded[:, PACK * lo : PACK * (lo + width)], raw[:, :, lo : lo + width]))
             codes = keep.tile([P, PASS], U32, name="w2_w%d" % b, align_bytes=64)
             scales = keep.tile([P, PASS], U8, name="w2_s%d" % b, align_bytes=64)
             nc.vector.quantize_mx(out=codes[:].bitcast(FP8X4), scales=scales[:], in_=rounded[:])
             return codes, scales
 
-        def load_wg(part):
-            lo, hi = WG_PARTS[part]
+        def load_wg(t0, t1, lo, hi):
             rows = wgs.rearrange("(i t) c -> i t c", t=PACK)
             for quadrant in (0, 2, 1, 3):
                 nc.sync.dma_start(
-                    out=wg[32 * quadrant : 32 * quadrant + 32, :, lo:hi], in_=rows[:, :, lo:hi]
+                    out=wg[32 * quadrant : 32 * quadrant + 32, t0:t1, lo:hi], in_=rows[:, t0:t1, lo:hi]
                 )
 
         def load_page(b, t):
@@ -105,10 +104,9 @@ def tile_list_trie_leak_audit_kernel(
             )
             return page
 
-        for quadrant in range(4):
+        for r in range(4):
             nc.sync.dma_start(
-                out=tab_s[32 * quadrant : 32 * quadrant + 4, :].bitcast(I32),
-                in_=tab_scales[0, 4 * quadrant : 4 * quadrant + 4, :].bitcast(I32),
+                out=tab_s[r:P:32, :].bitcast(I32), in_=tab_scales[0, r:16:4, :].bitcast(I32)
             )
         nc.sync.dma_start(idx[:], offs)
         w2_raw0 = load_w2(0)
@@ -116,20 +114,19 @@ def tile_list_trie_leak_audit_kernel(
             out=tab_w[:], in_=tab_words[0].rearrange("p n t -> p (n t)").bitcast(I32)
         )
         nc.sync.dma_start(out=w1_w[:].bitcast(I32), in_=w1_words[0].bitcast(I32))
-        for quadrant in range(4):
+        for r in range(4):
             nc.sync.dma_start(
-                out=w1_s[32 * quadrant : 32 * quadrant + 4, :].bitcast(I32),
-                in_=w1_scales[0, 4 * quadrant : 4 * quadrant + 4, :].bitcast(I32),
+                out=w1_s[r:P:32, :].bitcast(I32), in_=w1_scales[0, r:16:4, :].bitcast(I32)
             )
         w2_raw1 = load_w2(1)
         pages = {(0, 0): load_page(0, 0)}
         nc.sync.dma_start(idx2[:], offs2)
-        load_wg(0)
+        load_wg(0, 4, 0, CHUNK)
         pages[0, 1] = load_page(0, 1)
-        load_wg(1)
         pages[0, 2] = load_page(0, 2)
+        load_wg(0, 4, CHUNK, 2 * CHUNK)
         pages[0, 3] = load_page(0, 3)
-        load_wg(2)
+        load_wg(0, 4, S // 2, S)
         nc.sync.dma_start(idx4[:], offs4)
         nc.sync.dma_start(idx3[:], offs3)
         nc.sync.dma_start(
@@ -148,17 +145,17 @@ def tile_list_trie_leak_audit_kernel(
             )
 
         nc.vector.tensor_copy(v_s[:], tab_s[:].indirect(idx[:]))
-        w2_mx = [quantize_w2(w2_raw0, 0, nc.scalar.copy)]
+        w2_mx = [quantize_w2(w2_raw0, 0, nc.scalar.copy, PASS)]
         for lo in range(0, S, S // 2):
             hi = lo + S // 2
             nc.vector.tensor_copy(
                 v_w[:, lo:hi], tab_w[:].bitcast(U32).indirect(entries(idx, lo, hi))
             )
-        w2_mx.append(quantize_w2(w2_raw1, 1, nc.vector.tensor_copy))
 
-        def features(b, q, h, rows, copy_first):
+        def features(b, q, h, rows, span):
             first = work.tile([P, 2, PACK, P], F32, name="first", tag="first", bufs=2)
             second = work.tile([P, 2, PACK, P], F32, name="second", tag="second%d" % (q % 2), align_bytes=64)
+            sums = []
             for u in range(2):
                 cols = slice(q * CHUNK + u * P, q * CHUNK + (u + 1) * P)
                 w2_w, w2_s = w2_mx[b]
@@ -177,19 +174,21 @@ def tile_list_trie_leak_audit_kernel(
                     rhs_scale=w1_s[:, b * PASS : (b + 1) * PASS],
                     start=True, stop=True,
                 )
-                nc.scalar.activation(
-                    second[:, u], acc2[:].rearrange("p (m t) -> p t m", t=PACK), ACT.Tanh, scale=-1.0
-                )
-                copy_first(first[:, u], acc1[:].rearrange("p (m t) -> p t m", t=PACK))
-            for t0 in range(0, PACK, rows):
-                turned = psum.tile([P, rows, CHUNK], F32, name="turned", tag="turned")
-                for e in range(rows):
-                    for u in range(2):
-                        dst = turned[:, e, u * P : (u + 1) * P]
-                        t = t0 + e
-                        nc.tensor.matmul(dst, first[:, u, t, :], ident[:], start=True, stop=False, is_transpose=True)
-                        nc.tensor.matmul(dst, second[:, u, t, :], ident[:], start=False, stop=True, is_transpose=True)
-                nc.scalar.copy(h[:, t0 : t0 + rows, q * CHUNK : (q + 1) * CHUNK], turned[:])
+                sums.append([acc[:].rearrange("p (m t) -> p t m", t=PACK) for acc in (acc1, acc2)])
+            for s0 in range(0, PACK, span):
+                slots = slice(s0, s0 + span)
+                for u in range(2):
+                    nc.scalar.activation(second[:, u, slots], sums[u][1][:, slots], ACT.Tanh, scale=-1.0)
+                    nc.scalar.copy(first[:, u, slots], sums[u][0][:, slots])
+                for t0 in range(s0, s0 + span, rows):
+                    turned = psum.tile([P, rows, CHUNK], F32, name="turned", tag="turned")
+                    for e in range(rows):
+                        for u in range(2):
+                            dst = turned[:, e, u * P : (u + 1) * P]
+                            t = t0 + e
+                            nc.tensor.matmul(dst, first[:, u, t, :], ident[:], start=True, stop=False, is_transpose=True)
+                            nc.tensor.matmul(dst, second[:, u, t, :], ident[:], start=False, stop=True, is_transpose=True)
+                    nc.scalar.copy(h[:, t0 : t0 + rows, q * CHUNK : (q + 1) * CHUNK], turned[:])
 
         def scatter(b, t, h, lo, hi):
             nc.vector.tensor_tensor(
@@ -201,28 +200,28 @@ def tile_list_trie_leak_audit_kernel(
             scatter(b, t, h, 0, S)
 
         def fetch_link(b, t):
-            damp = work.tile([P, M], F32, name="damp", tag="damp", bufs=4)
+            damp = work.tile([P, M], F32, name="damp", tag="damp", bufs=PACK)
             nc.vector.tensor_copy(damp[:], pages[b, t][:].indirect(idx4[:]))
             return damp
 
-        def damping(damp, tag):
+        def damping(b, t, tag):
+            damp = damps[b, t]
             root = work.tile([P, M], F32, name="root", tag=tag, align_bytes=64)
             nc.scalar.activation(root[:], damp[:], ACT.Abs)
             nc.scalar.activation(root[:], root[:], ACT.Abs_reciprocal_sqrt, bias=one[:])
-            nc.scalar.activation(damp[:], root[:], ACT.Square)
-            return root
+            nc.scalar.activation(root[:], root[:], ACT.Square)
+            nc.scalar.activation(damp[:], root[:], ACT.Copy, scale=gain_sb[:, b, t : t + 1])
 
-        def fetch_node(b, t, damp, z, lo, hi, factor):
-            nc.scalar.activation(factor, damp[:, lo:hi], ACT.Copy, scale=gain_sb[:, b, t : t + 1])
+        def fetch_node(b, t, z, lo, hi):
             nc.vector.tensor_tensor(
-                z[:, t, lo:hi], pages[b, t][:].indirect(entries(idx3, lo, hi)), factor, MULT
+                z[:, t, :], pages[b, t][:].indirect(entries(idx3, lo, hi)), damps[b, t][:, lo:hi], MULT
             )
 
         z_w = [keep.tile([P, M], U32, name="z_w%d" % b, align_bytes=64) for b in range(BLOCKS)]
         z_s = [keep.tile([P, M], U8, name="z_s%d" % b, align_bytes=64) for b in range(BLOCKS)]
 
         def quantize_z(b, z, lo, hi, copy, part):
-            copy(*interleaved(part, z[:, :, lo:hi]))
+            copy(*interleaved(part, z))
             nc.vector.quantize_mx(out=z_w[b][:, lo:hi].bitcast(FP8X4), scales=z_s[b][:, lo:hi], in_=part)
 
         def rounding_tile(lo, hi):
@@ -254,62 +253,66 @@ def tile_list_trie_leak_audit_kernel(
         h0 = work.tile([P, PACK, S], F32, name="h0", tag="rows0", align_bytes=64)
         for q in range(S // CHUNK):
             if q == 0:
-                features(0, q, h0, 1, nc.vector.tensor_copy)
+                features(0, q, h0, 1, 2)
+                w2_mx.append(quantize_w2(w2_raw1, 1, nc.vector.tensor_copy, PASS))
             else:
-                features(0, q, h0, 2, nc.scalar.copy)
-            for t in range(PACK):
-                scatter(0, t, h0, q * CHUNK, (q + 1) * CHUNK)
+                features(0, q, h0, 2, PACK)
+            if q < 2:
+                for t in range(PACK):
+                    scatter(0, t, h0, q * CHUNK, (q + 1) * CHUNK)
+        for t in range(PACK):
+            scatter(0, t, h0, S // 2, S)
         h1 = work.tile([P, PACK, S], F32, name="h1", tag="rows1", align_bytes=64)
         for q in range(S // CHUNK):
-            features(1, q, h1, 2, nc.scalar.copy)
+            features(1, q, h1, 2, PACK)
         damps = {(0, t): fetch_link(0, t) for t in range(PACK)}
         scatter_all(1, 0, h1)
 
         z0 = work.tile([P, PACK, M], F32, name="z0", tag="rows0", align_bytes=64)
         for t in range(PACK):
-            damping(damps[0, t], "second1")
-            fetch_node(0, t, damps[0, t], z0, 0, M, damps[0, t][:])
+            damping(0, t, "second1")
+            fetch_node(0, t, z0[:], 0, M)
             damps[1, t] = fetch_link(1, t)
             if t + 1 < PACK:
                 pages[1, t + 1] = load_page(1, t + 1)
                 scatter_all(1, t + 1, h1)
 
-        z1 = work.tile([P, PACK, M], F32, name="z1", tag="rows1", align_bytes=64)
-        (a_lo, a_hi), (b_lo, b_hi), (c_lo, c_hi) = PIECES
+
         last = PACK - 1
+        lead = PIECES[1][1]
+        z = work.tile([P, PACK, lead], F32, name="z", tag="rows1", align_bytes=64)
         for t in range(last):
-            damping(damps[1, t], "second1")
-            fetch_node(1, t, damps[1, t], z1, a_lo, a_hi, damps[1, t][:, a_lo:a_hi])
+            damping(1, t, "second1")
+            fetch_node(1, t, z[:], 0, lead)
         rounded0 = work.tile([P, PACK * M], BF16, name="rounded0", tag="second1", align_bytes=64)
-        quantize_z(0, z0, 0, M, nc.scalar.copy, rounded0[:])
-        root = damping(damps[1, last], "rows0")
-        fetch_node(1, last, damps[1, last], z1, a_lo, a_hi, damps[1, last][:, a_lo:a_hi])
-        banks_a = score_banks("sums")
-        banks_c = score_banks("turned")
-        scores_pass(0, banks_a, a_lo, a_hi)
-        scores_pass(0, banks_c, c_lo, c_hi)
+        quantize_z(0, z0[:], 0, M, nc.scalar.copy, rounded0[:])
+        damping(1, last, "rows0")
+        ready = [z[:, :, lo:hi] for lo, hi in PIECES[:2]]
+        for part, (lo, hi) in zip(ready, PIECES):
+            fetch_node(1, last, part, lo, hi)
 
-        width = b_hi - b_lo
-        for t in range(PACK):
-            fetch_node(1, t, damps[1, t], z1, b_lo, b_hi, root[:, t * width : (t + 1) * width])
-        quantize_z(1, z1, a_lo, a_hi, nc.scalar.copy, rounding_tile(a_lo, a_hi))
-        scores_pass(1, banks_a, a_lo, a_hi)
-        for t in range(last):
-            fetch_node(1, t, damps[1, t], z1, c_lo, c_hi, z1[:, t, a_lo : a_lo + width])
-        quantize_z(1, z1, b_lo, b_hi, nc.scalar.copy, rounding_tile(b_lo, b_hi))
-        fetch_node(1, last, damps[1, last], z1, c_lo, c_hi, z1[:, last, b_lo:b_hi])
+        def finish(banks, lo, hi, engines):
+            share = N // P // len(engines)
+            for e, copy in enumerate(engines):
+                staged = work.tile([P, share, hi - lo], F32, name="staged", tag="wide", bufs=4)
+                store(banks, e * share, (e + 1) * share, lo, hi, copy, staged)
 
-        staged_a = work.tile([P, PACK, PASS], F32, name="staged_a", tag="wide", bufs=2)
-        store(banks_a, 0, 4, a_lo, a_hi, nc.scalar.copy, staged_a)
-        banks_b = score_banks("sums")
-        for b in range(BLOCKS):
-            scores_pass(b, banks_b, b_lo, b_hi)
-        staged_b = work.tile([P, PACK, PASS], F32, name="staged_b", tag="wide", bufs=2)
-        store(banks_b, 0, 4, b_lo, b_hi, nc.scalar.copy, staged_b)
-
-        quantize_z(1, z1, c_lo, c_hi, nc.vector.tensor_copy, rounding_tile(c_lo, c_hi))
-        scores_pass(1, banks_c, c_lo, c_hi)
-        staged_c = work.tile([P, 2, c_hi - c_lo], F32, name="staged_c")
-        staged_d = work.tile([P, 2, c_hi - c_lo], F32, name="staged_d")
-        store(banks_c, 0, 2, c_lo, c_hi, nc.vector.tensor_copy, staged_c)
-        store(banks_c, 2, 4, c_lo, c_hi, nc.scalar.copy, staged_d)
+        waiting = None
+        for i, (lo, hi) in enumerate(PIECES):
+            final = i == len(PIECES) - 1
+            if len(ready) == i + 1 < len(PIECES):
+                ahead_lo, ahead_hi = PIECES[i + 1]
+                ahead = work.tile(
+                    [P, PACK, ahead_hi - ahead_lo], F32, name="z", tag="rows%d" % (len(ready) % 2), align_bytes=64
+                )
+                for t in range(PACK):
+                    fetch_node(1, t, ahead[:], ahead_lo, ahead_hi)
+                ready.append(ahead[:])
+            banks = score_banks(("sums", "turned")[i % 2])
+            scores_pass(0, banks, lo, hi)
+            quantize_z(1, ready[i], lo, hi, nc.vector.tensor_copy if i >= 3 else nc.scalar.copy, rounding_tile(lo, hi))
+            scores_pass(1, banks, lo, hi)
+            if waiting:
+                finish(*waiting)
+            waiting = (banks, lo, hi, [nc.vector.tensor_copy, nc.scalar.copy] if final else [nc.scalar.copy])
+        finish(*waiting)

@@ -22,8 +22,8 @@ PACK = 4
 PASS = P * PACK
 BLOCKS = H // PASS
 CHUNK = 256
-PAGE_BUFS = 5
-PIECES = ((0, 256), (256, 512), (512, 768), (768, 1024))
+HALF = 512
+PIECES = ((0, 256), (256, 512), (512, 768), (768, 896), (896, 1024))
 
 
 def entries(offsets, lo, hi):
@@ -46,7 +46,7 @@ def tile_list_trie_leak_audit_kernel(
         lists = ctx.enter_context(tc.tile_pool(name="lists", bufs=1))
         keep = ctx.enter_context(tc.tile_pool(name="keep", bufs=1))
         work = ctx.enter_context(tc.tile_pool(name="work", bufs=1))
-        psum = ctx.enter_context(tc.psum_pool(name="psum", bufs=4))
+        psum = ctx.enter_context(tc.psum_pool(name="psum", bufs=1))
 
         idx = lists.tile([P, S // 16], U16)
         idx2 = lists.tile([P, S // 16], U16)
@@ -55,11 +55,11 @@ def tile_list_trie_leak_audit_kernel(
 
         tab_w = keep.tile([P, T], I32, align_bytes=64)
         tab_s = keep.tile([P, T], U8, align_bytes=64)
-        w1_w = keep.tile([P, 2 * H], U8, align_bytes=64)
+        w1_s_in = keep.tile([P, H], U8)
+        w1_w = keep.tile([P, H // 2], I32, align_bytes=64)
         w1_s = keep.tile([P, H], U8, align_bytes=64)
         w3_w = keep.tile([P, BLOCKS * N], I32, align_bytes=64)
         w3_s = keep.tile([P, BLOCKS * N], U8, align_bytes=64)
-        v_w = keep.tile([P, S], U32, align_bytes=64)
         v_s = keep.tile([P, S], U8, align_bytes=64)
         wg = keep.tile([P, PACK, S], F32)
         gain_sb = keep.tile([P, BLOCKS, PACK], F32)
@@ -67,72 +67,82 @@ def tile_list_trie_leak_audit_kernel(
         one = keep.tile([P, 1], F32)
 
         nc.vector.memset(tab_s[:].bitcast(I32), 0)
-        nc.vector.memset(w1_s[:].bitcast(I32), 0)
+        nc.vector.memset(w1_s_in[:].bitcast(I32), 0)
         nc.gpsimd.memset(w3_s[:].bitcast(I32), 0)
         nc.gpsimd.memset(one[:], 1.0)
         make_identity(nc, ident[:])
 
         def load_w2(b):
-            raw = work.tile([P, PACK, PASS], F32, name="raw", tag="wide", bufs=4)
+            raw = work.tile([P, PACK, PASS], F32, name="raw", tag="wide%d" % b, align_bytes=64)
             nc.sync.dma_start(
                 out=raw[:],
                 in_=w2.rearrange("(p j) c -> p j c", j=PACK)[:, :, b * PASS : (b + 1) * PASS],
             )
             return raw
 
-        def quantize_w2(raw, b, copy, width):
-            rounded = work.tile([P, PACK * PASS], BF16, name="rounded", tag="rounded", bufs=3, align_bytes=64)
-            for lo in range(0, PASS, width):
-                copy(*interleaved(rounded[:, PACK * lo : PACK * (lo + width)], raw[:, :, lo : lo + width]))
+        def quantize_w2(raw, b, copies):
+            rounded = work.tile([P, 2, PACK * CHUNK], BF16, name="rounded", tag="damp%d" % (1 - b), align_bytes=64)
             codes = keep.tile([P, PASS], U32, name="w2_w%d" % b, align_bytes=64)
             scales = keep.tile([P, PASS], U8, name="w2_s%d" % b, align_bytes=64)
-            nc.vector.quantize_mx(out=codes[:].bitcast(FP8X4), scales=scales[:], in_=rounded[:])
+            for g, copy in enumerate(copies):
+                copy(
+                    rounded[:, g].rearrange("p (m e j) -> p m j e", e=2, j=PACK),
+                    raw[:].rearrange("p j (m g e) -> p g m j e", g=2, e=2)[:, g],
+                )
+                pair = slice(g * CHUNK, (g + 1) * CHUNK)
+                nc.vector.quantize_mx(out=codes[:, pair].bitcast(FP8X4), scales=scales[:, pair], in_=rounded[:, g])
             return codes, scales
 
-        def load_wg(t0, t1, lo, hi):
+        def load_wg(g, lo, hi):
             rows = wgs.rearrange("(i t) c -> i t c", t=PACK)
             for quadrant in (0, 2, 1, 3):
                 nc.sync.dma_start(
-                    out=wg[32 * quadrant : 32 * quadrant + 32, t0:t1, lo:hi], in_=rows[:, t0:t1, lo:hi]
+                    out=wg[32 * quadrant : 32 * quadrant + 32, 2 * g : 2 * g + 2, lo:hi],
+                    in_=rows[:, 2 * g : 2 * g + 2, lo:hi],
                 )
 
         def load_page(b, t):
-            page = work.tile([P, T2], F32, name="page", tag="page", bufs=PAGE_BUFS)
+            page = work.tile([P, T2], F32, name="page%d%d" % (b, t), align_bytes=64)
             nc.sync.dma_start(
                 out=page[:],
                 in_=page0.rearrange("(b p t) c -> b t p c", b=BLOCKS, t=PACK)[b, t],
             )
             return page
 
-        for r in range(4):
-            nc.sync.dma_start(
-                out=tab_s[r:P:32, :].bitcast(I32), in_=tab_scales[0, r:16:4, :].bitcast(I32)
-            )
-        nc.sync.dma_start(idx[:], offs)
+        def load_scales(plane, rows):
+            for r in range(4):
+                nc.sync.dma_start(out=plane[r:P:32, :].bitcast(I32), in_=rows[0, r:16:4, :].bitcast(I32))
+
+        def load_w1(b):
+            words = keep.tile([P, CHUNK], I32, name="w1_in", tag="words%d" % (1 - b), align_bytes=64)
+            nc.sync.dma_start(out=words[:], in_=w1_words[0].bitcast(I32)[:, b * CHUNK : (b + 1) * CHUNK])
+            return words
+
         w2_raw0 = load_w2(0)
+        load_scales(tab_s, tab_scales)
+        nc.sync.dma_start(idx[:], offs)
         nc.sync.dma_start(
             out=tab_w[:], in_=tab_words[0].rearrange("p n t -> p (n t)").bitcast(I32)
         )
-        nc.sync.dma_start(out=w1_w[:].bitcast(I32), in_=w1_words[0].bitcast(I32))
-        for r in range(4):
-            nc.sync.dma_start(
-                out=w1_s[r:P:32, :].bitcast(I32), in_=w1_scales[0, r:16:4, :].bitcast(I32)
-            )
-        w2_raw1 = load_w2(1)
+        load_scales(w1_s_in, w1_scales)
+        w1_w_in = [load_w1(0)]
         pages = {(0, 0): load_page(0, 0)}
         nc.sync.dma_start(idx2[:], offs2)
-        load_wg(0, 4, 0, CHUNK)
+        load_wg(0, 0, CHUNK)
+        w1_w_in.append(load_w1(1))
         pages[0, 1] = load_page(0, 1)
-        pages[0, 2] = load_page(0, 2)
-        load_wg(0, 4, CHUNK, 2 * CHUNK)
-        pages[0, 3] = load_page(0, 3)
-        load_wg(0, 4, S // 2, S)
+        load_wg(0, CHUNK, S)
+        w2_raw1 = load_w2(1)
         nc.sync.dma_start(idx4[:], offs4)
+        pages[0, 2] = load_page(0, 2)
+        load_wg(1, 0, S)
+        pages[0, 3] = load_page(0, 3)
+        for t in range(PACK - 1):
+            pages[1, t] = load_page(1, t)
         nc.sync.dma_start(idx3[:], offs3)
         nc.sync.dma_start(
             out=gain_sb[:], in_=gain.rearrange("(b p t) -> p b t", b=BLOCKS, t=PACK)
         )
-        pages[1, 0] = load_page(1, 0)
         for b in range(BLOCKS):
             nc.sync.dma_start(
                 out=w3_w[:, b * N : (b + 1) * N],
@@ -145,50 +155,65 @@ def tile_list_trie_leak_audit_kernel(
             )
 
         nc.vector.tensor_copy(v_s[:], tab_s[:].indirect(idx[:]))
-        w2_mx = [quantize_w2(w2_raw0, 0, nc.scalar.copy, PASS)]
-        for lo in range(0, S, S // 2):
-            hi = lo + S // 2
+        w2_mx = [quantize_w2(w2_raw0, 0, (nc.scalar.copy, nc.scalar.copy))]
+
+        def gather_words(lo, tag):
+            words = keep.tile([P, HALF], U32, name="v_w", tag=tag, align_bytes=64)
+            nc.vector.tensor_copy(words[:], tab_w[:].bitcast(U32).indirect(entries(idx, lo, lo + HALF)))
+            return words
+
+        def deal_w1(b):
             nc.vector.tensor_copy(
-                v_w[:, lo:hi], tab_w[:].bitcast(U32).indirect(entries(idx, lo, hi))
+                w1_s[:].rearrange("p (b g m e) -> p b g m e", b=BLOCKS, g=2, e=2)[:, b],
+                w1_s_in[:].rearrange("p (b m g e) -> p b g m e", b=BLOCKS, g=2, e=2)[:, b],
+            )
+            nc.vector.tensor_copy(
+                w1_w[:].rearrange("p (b g m) -> p b g m", b=BLOCKS, g=2)[:, b],
+                w1_w_in[b][:].rearrange("p (m g) -> p g m", g=2),
             )
 
-        def features(b, q, h, rows, span):
-            first = work.tile([P, 2, PACK, P], F32, name="first", tag="first", bufs=2)
-            second = work.tile([P, 2, PACK, P], F32, name="second", tag="second%d" % (q % 2), align_bytes=64)
-            sums = []
-            for u in range(2):
-                cols = slice(q * CHUNK + u * P, q * CHUNK + (u + 1) * P)
-                w2_w, w2_s = w2_mx[b]
-                acc2 = psum.tile([P, PASS], F32, name="acc2", tag="sums")
-                nc.tensor.matmul_mx(
-                    out=acc2[:],
-                    lhsT=v_w[:, cols].bitcast(FP8X4), lhsT_scale=v_s[:, cols],
-                    rhs=w2_w[:].bitcast(FP8X4), rhs_scale=w2_s[:],
-                    start=True, stop=True,
-                )
-                acc1 = psum.tile([P, PASS], F32, name="acc1", tag="sums")
-                nc.tensor.matmul_mx(
-                    out=acc1[:],
-                    lhsT=v_w[:, cols].bitcast(FP8X4), lhsT_scale=v_s[:, cols],
-                    rhs=w1_w[:, 2 * b * PASS : 2 * (b + 1) * PASS].bitcast(FP4X4),
-                    rhs_scale=w1_s[:, b * PASS : (b + 1) * PASS],
-                    start=True, stop=True,
-                )
-                sums.append([acc[:].rearrange("p (m t) -> p t m", t=PACK) for acc in (acc1, acc2)])
-            for s0 in range(0, PACK, span):
-                slots = slice(s0, s0 + span)
+        v_w = [gather_words(0, "v_w0")]
+        deal_w1(0)
+        v_w.append(gather_words(HALF, "words1"))
+        deal_w1(1)
+
+        def products(b, g, q, banks):
+            w2_w, w2_s = w2_mx[b]
+            pair = slice(g * CHUNK, (g + 1) * CHUNK)
+            lo = b * PASS + g * CHUNK
+            acc2 = psum.tile([P, 2, CHUNK], F32, name="acc2", tag="bank%d" % banks[0])
+            acc1 = psum.tile([P, 2, CHUNK], F32, name="acc1", tag="bank%d" % banks[1])
+            for acc, codes, scales in (
+                (acc2, w2_w[:, pair].bitcast(FP8X4), w2_s[:, pair]),
+                (acc1, w1_w[:].bitcast(U8)[:, 2 * lo : 2 * (lo + CHUNK)].bitcast(FP4X4), w1_s[:, lo : lo + CHUNK]),
+            ):
                 for u in range(2):
-                    nc.scalar.activation(second[:, u, slots], sums[u][1][:, slots], ACT.Tanh, scale=-1.0)
-                    nc.scalar.copy(first[:, u, slots], sums[u][0][:, slots])
-                for t0 in range(s0, s0 + span, rows):
-                    turned = psum.tile([P, rows, CHUNK], F32, name="turned", tag="turned")
-                    for e in range(rows):
-                        for u in range(2):
-                            dst = turned[:, e, u * P : (u + 1) * P]
-                            t = t0 + e
-                            nc.tensor.matmul(dst, first[:, u, t, :], ident[:], start=True, stop=False, is_transpose=True)
-                            nc.tensor.matmul(dst, second[:, u, t, :], ident[:], start=False, stop=True, is_transpose=True)
-                    nc.scalar.copy(h[:, t0 : t0 + rows, q * CHUNK : (q + 1) * CHUNK], turned[:])
+                    cols = slice(q * CHUNK + u * P, q * CHUNK + (u + 1) * P)
+                    nc.tensor.matmul_mx(
+                        out=acc[:, u, :],
+                        lhsT=v_w[q // 2][:, cols.start % HALF : cols.start % HALF + P].bitcast(FP8X4),
+                        lhsT_scale=v_s[:, cols],
+                        rhs=codes, rhs_scale=scales,
+                        start=True, stop=True,
+                    )
+            return [acc[:].rearrange("p u (m e) -> p e u m", e=2) for acc in (acc1, acc2)]
+
+        def features(b, g, q, h, span):
+            banks = (2 * (q % 2), 2 * (q % 2) + 1)
+            acc1, acc2 = products(b, g, q, banks)
+            first = work.tile([P, 2, 2, P], F32, name="first", tag="first", bufs=2)
+            second = work.tile([P, 2, 2, P], F32, name="second", tag="second%d" % (q % 2), align_bytes=64)
+            for e0 in range(0, 2, span):
+                slots = slice(e0, e0 + span)
+                nc.scalar.activation(second[:, slots], acc2[:, slots], ACT.Tanh, scale=-1.0)
+                nc.scalar.copy(first[:, slots], acc1[:, slots])
+                turned = psum.tile([P, span, CHUNK], F32, name="turned", tag="bank%d" % (4 + (q + 3 * e0) % 4))
+                for e in range(span):
+                    for u in range(2):
+                        dst = turned[:, e, u * P : (u + 1) * P]
+                        nc.tensor.matmul(dst, first[:, e0 + e, u, :], ident[:], start=True, stop=False, is_transpose=True)
+                        nc.tensor.matmul(dst, second[:, e0 + e, u, :], ident[:], start=False, stop=True, is_transpose=True)
+                nc.scalar.copy(h[:, 2 * g + e0 : 2 * g + e0 + span, q * CHUNK : (q + 1) * CHUNK], turned[:])
 
         def scatter(b, t, h, lo, hi):
             nc.vector.tensor_tensor(
@@ -196,26 +221,28 @@ def tile_list_trie_leak_audit_kernel(
                 h[:, t, lo:hi], wg[:, t, lo:hi], MULT,
             )
 
-        def scatter_all(b, t, h):
-            scatter(b, t, h, 0, S)
 
         def fetch_link(b, t):
-            damp = work.tile([P, M], F32, name="damp", tag="damp", bufs=PACK)
-            nc.vector.tensor_copy(damp[:], pages[b, t][:].indirect(idx4[:]))
-            return damp
+            nc.vector.tensor_copy(damps[b][:, t, :], pages[b, t][:].indirect(idx4[:]))
 
-        def damping(b, t, tag):
-            damp = damps[b, t]
-            root = work.tile([P, M], F32, name="root", tag=tag, align_bytes=64)
-            nc.scalar.activation(root[:], damp[:], ACT.Abs)
-            nc.scalar.activation(root[:], root[:], ACT.Abs_reciprocal_sqrt, bias=one[:])
-            nc.scalar.activation(root[:], root[:], ACT.Square)
-            nc.scalar.activation(damp[:], root[:], ACT.Copy, scale=gain_sb[:, b, t : t + 1])
+        def damping(b, parts, tag, tag2=None):
+            shape = [P, len(parts), parts[0][2] - parts[0][1]]
+            size = work.tile(shape, F32, name="size", tag=tag, align_bytes=64)
+            root = size if tag2 is None else work.tile(shape, F32, name="root", tag=tag2, align_bytes=64)
+            for e, (t, lo, hi) in enumerate(parts):
+                nc.scalar.activation(size[:, e], damps[b][:, t, lo:hi], ACT.Abs)
+            for e in range(len(parts)):
+                nc.scalar.activation(root[:, e], size[:, e], ACT.Abs_reciprocal_sqrt, bias=one[:])
+            for e in range(len(parts)):
+                nc.scalar.activation(root[:, e], root[:, e], ACT.Square)
+            for e, (t, lo, hi) in enumerate(parts):
+                nc.scalar.activation(damps[b][:, t, lo:hi], root[:, e], ACT.Copy, scale=gain_sb[:, b, t : t + 1])
 
-        def fetch_node(b, t, z, lo, hi):
-            nc.vector.tensor_tensor(
-                z[:, t, :], pages[b, t][:].indirect(entries(idx3, lo, hi)), damps[b, t][:, lo:hi], MULT
-            )
+        def fetch_nodes(b, lo, hi, z):
+            for t in range(PACK):
+                nc.vector.tensor_tensor(
+                    z[:, t, :], pages[b, t][:].indirect(entries(idx3, lo, hi)), damps[b][:, t, lo:hi], MULT
+                )
 
         z_w = [keep.tile([P, M], U32, name="z_w%d" % b, align_bytes=64) for b in range(BLOCKS)]
         z_s = [keep.tile([P, M], U8, name="z_s%d" % b, align_bytes=64) for b in range(BLOCKS)]
@@ -224,95 +251,91 @@ def tile_list_trie_leak_audit_kernel(
             copy(*interleaved(part, z))
             nc.vector.quantize_mx(out=z_w[b][:, lo:hi].bitcast(FP8X4), scales=z_s[b][:, lo:hi], in_=part)
 
-        def rounding_tile(lo, hi):
-            rounded = work.tile([P, PACK * PASS], BF16, name="rounded", tag="rounded", bufs=3, align_bytes=64)
-            return rounded[:, : PACK * (hi - lo)]
-
         def scores_pass(b, banks, lo, hi):
+            share = N // P // len(banks)
             for n in range(N // P):
                 cols = slice(b * N + n * P, b * N + (n + 1) * P)
                 nc.tensor.matmul_mx(
-                    out=banks[n][:, : hi - lo],
+                    out=banks[n // share][:, n % share, :],
                     lhsT=w3_w[:, cols].bitcast(FP8X4), lhsT_scale=w3_s[:, cols],
                     rhs=z_w[b][:, lo:hi].bitcast(FP8X4), rhs_scale=z_s[b][:, lo:hi],
-                    start=(b == 0), stop=(b == BLOCKS - 1),
+                    start=(b == 0 and n % share == 0), stop=(b == BLOCKS - 1 and n % share == share - 1),
                 )
-
-        def score_banks(tag):
-            return [psum.tile([P, PASS], F32, name="scores", tag=tag) for n in range(N // P)]
 
         out_rows = out.rearrange("(n p) m -> p n m", p=P)
 
-        def store(banks, first_n, last_n, lo, hi, copy, staged):
-            for n in range(first_n, last_n):
-                copy(staged[:, n - first_n, : hi - lo], banks[n][:, : hi - lo])
-            nc.sync.dma_start(
-                out=out_rows[:, first_n:last_n, lo:hi], in_=staged[:, : last_n - first_n, : hi - lo]
-            )
-
         h0 = work.tile([P, PACK, S], F32, name="h0", tag="rows0", align_bytes=64)
         for q in range(S // CHUNK):
-            if q == 0:
-                features(0, q, h0, 1, 2)
-                w2_mx.append(quantize_w2(w2_raw1, 1, nc.vector.tensor_copy, PASS))
-            else:
-                features(0, q, h0, 2, PACK)
-            if q < 2:
-                for t in range(PACK):
-                    scatter(0, t, h0, q * CHUNK, (q + 1) * CHUNK)
-        for t in range(PACK):
-            scatter(0, t, h0, S // 2, S)
-        h1 = work.tile([P, PACK, S], F32, name="h1", tag="rows1", align_bytes=64)
+            features(0, 0, q, h0, 1 if q == 0 else 2)
+            for t in range(2):
+                scatter(0, t, h0, q * CHUNK, (q + 1) * CHUNK)
+        w2_mx.append(quantize_w2(w2_raw1, 1, (nc.scalar.copy, nc.scalar.copy)))
+        damps = [work.tile([P, PACK, M], F32, name="damp%d" % b, align_bytes=64) for b in range(BLOCKS)]
+        for t in range(2):
+            fetch_link(0, t)
         for q in range(S // CHUNK):
-            features(1, q, h1, 2, PACK)
-        damps = {(0, t): fetch_link(0, t) for t in range(PACK)}
-        scatter_all(1, 0, h1)
-
-        z0 = work.tile([P, PACK, M], F32, name="z0", tag="rows0", align_bytes=64)
-        for t in range(PACK):
-            damping(0, t, "second1")
-            fetch_node(0, t, z0[:], 0, M)
-            damps[1, t] = fetch_link(1, t)
-            if t + 1 < PACK:
-                pages[1, t + 1] = load_page(1, t + 1)
-                scatter_all(1, t + 1, h1)
-
-
+            features(0, 1, q, h0, 2)
+        for lo in range(0, S, HALF):
+            for t in range(2, PACK):
+                scatter(0, t, h0, lo, lo + HALF)
+        for t in range(2, PACK):
+            fetch_link(0, t)
+        h1 = work.tile([P, PACK, S], F32, name="h1", tag="rows1", align_bytes=64)
+        for g in range(2):
+            for q in range(S // CHUNK):
+                features(1, g, q, h1, 2)
         last = PACK - 1
-        lead = PIECES[1][1]
-        z = work.tile([P, PACK, lead], F32, name="z", tag="rows1", align_bytes=64)
         for t in range(last):
-            damping(1, t, "second1")
-            fetch_node(1, t, z[:], 0, lead)
-        rounded0 = work.tile([P, PACK * M], BF16, name="rounded0", tag="second1", align_bytes=64)
-        quantize_z(0, z0[:], 0, M, nc.scalar.copy, rounded0[:])
-        damping(1, last, "rows0")
-        ready = [z[:, :, lo:hi] for lo, hi in PIECES[:2]]
-        for part, (lo, hi) in zip(ready, PIECES):
-            fetch_node(1, last, part, lo, hi)
+            scatter(1, t, h1, 0, S)
+            fetch_link(1, t)
 
-        def finish(banks, lo, hi, engines):
-            share = N // P // len(engines)
-            for e, copy in enumerate(engines):
-                staged = work.tile([P, share, hi - lo], F32, name="staged", tag="wide", bufs=4)
-                store(banks, e * share, (e + 1) * share, lo, hi, copy, staged)
+        damping(0, [(0, 0, M), (1, 0, M)], "second1")
+        damping(0, [(2, 0, M), (3, 0, M)], "second1", "page13")
+        pages[1, last] = load_page(1, last)
+        damping(1, [(0, 0, M), (1, 0, M)], "second1")
+        damping(1, [(2, 0, HALF), (2, HALF, M)], "second1")
 
-        waiting = None
+        def quantize_z0(k, z, tag):
+            rounded = work.tile([P, PACK * HALF], BF16, name="rounded0", tag=tag, align_bytes=64)
+            quantize_z(0, z[:], k * HALF, (k + 1) * HALF, nc.scalar.copy, rounded[:])
+
+        z00 = work.tile([P, PACK, HALF], F32, name="z0", tag="rows0", align_bytes=64)
+        fetch_nodes(0, 0, HALF, z00[:])
+        quantize_z0(0, z00, "second1")
+        scatter(1, last, h1, 0, S)
+        fetch_link(1, last)
+        damping(1, [(last, 0, HALF), (last, HALF, M)], "rows0", "wide1")
+        z01 = work.tile([P, PACK, HALF], F32, name="z0", tag="rows1", align_bytes=64)
+        fetch_nodes(0, HALF, M, z01[:])
+        quantize_z0(1, z01, "rows0")
+        staged = work.tile([P, N // P, M], F32, name="staged", tag="damp0", align_bytes=64)
+
+        banks = []
         for i, (lo, hi) in enumerate(PIECES):
+            count = 1 if i == len(PIECES) - 2 else 2
+            banks.append([
+                psum.tile([P, N // P // count, hi - lo], F32, name="scores", tag="bank%d" % ((sum(map(len, banks)) + e) % 8))
+                for e in range(count)
+            ])
+
+        def finish(i):
+            lo, hi = PIECES[i]
             final = i == len(PIECES) - 1
-            if len(ready) == i + 1 < len(PIECES):
-                ahead_lo, ahead_hi = PIECES[i + 1]
-                ahead = work.tile(
-                    [P, PACK, ahead_hi - ahead_lo], F32, name="z", tag="rows%d" % (len(ready) % 2), align_bytes=64
-                )
-                for t in range(PACK):
-                    fetch_node(1, t, ahead[:], ahead_lo, ahead_hi)
-                ready.append(ahead[:])
-            banks = score_banks(("sums", "turned")[i % 2])
-            scores_pass(0, banks, lo, hi)
-            quantize_z(1, ready[i], lo, hi, nc.vector.tensor_copy if i >= 3 else nc.scalar.copy, rounding_tile(lo, hi))
-            scores_pass(1, banks, lo, hi)
-            if waiting:
-                finish(*waiting)
-            waiting = (banks, lo, hi, [nc.vector.tensor_copy, nc.scalar.copy] if final else [nc.scalar.copy])
-        finish(*waiting)
+            share = N // P // len(banks[i])
+            for e, bank in enumerate(banks[i]):
+                part = staged[:, e * share : (e + 1) * share, lo:hi]
+                copy = nc.vector.tensor_copy if final and e == 0 else nc.scalar.copy
+                copy(part, bank[:])
+                nc.sync.dma_start(out=out_rows[:, e * share : (e + 1) * share, lo:hi], in_=part)
+
+        for i, (lo, hi) in enumerate(PIECES):
+            z = work.tile([P, PACK, hi - lo], F32, name="z", tag=("wide0", "rows1")[i % 2], align_bytes=64)
+            fetch_nodes(1, lo, hi, z[:])
+            scores_pass(0, banks[i], lo, hi)
+            rounded = work.tile([P, PACK * CHUNK], BF16, name="rounded", tag="rounded", bufs=2, align_bytes=64)
+            final = i == len(PIECES) - 1
+            quantize_z(1, z[:], lo, hi, nc.vector.tensor_copy if final else nc.scalar.copy, rounded[:, : PACK * (hi - lo)])
+            scores_pass(1, banks[i], lo, hi)
+            if i > 0:
+                finish(i - 1)
+        finish(len(PIECES) - 1)

@@ -72,26 +72,28 @@ def tile_list_trie_leak_audit_kernel(
         nc.gpsimd.memset(one[:], 1.0)
         make_identity(nc, ident[:])
 
-        def load_w2(b):
-            raw = work.tile([P, PACK, PASS], F32, name="raw", tag="wide%d" % b, align_bytes=64)
-            nc.sync.dma_start(
-                out=raw[:],
-                in_=w2.rearrange("(p j) c -> p j c", j=PACK)[:, :, b * PASS : (b + 1) * PASS],
-            )
+        w2_rows = w2.rearrange("(p j) c -> p j c", j=PACK)
+
+        def load_w2(lo, hi, tag):
+            raw = work.tile([P, PACK, hi - lo], F32, name="raw", tag=tag, align_bytes=64)
+            nc.sync.dma_start(out=raw[:], in_=w2_rows[:, :, lo:hi])
             return raw
 
-        def quantize_w2(raw, b, copies):
-            rounded = work.tile([P, 2, PACK * CHUNK], BF16, name="rounded", tag="damp%d" % (1 - b), align_bytes=64)
-            codes = keep.tile([P, PASS], U32, name="w2_w%d" % b, align_bytes=64)
-            scales = keep.tile([P, PASS], U8, name="w2_s%d" % b, align_bytes=64)
+        w2_w = keep.tile([P, BLOCKS, 2, CHUNK], U32, align_bytes=64)
+        w2_s = keep.tile([P, BLOCKS, 2, CHUNK], U8, align_bytes=64)
+
+        def quantize_w2(raw, lo, copies, tag):
+            width = raw.shape[2] // 2
+            rounded = work.tile([P, 2, PACK * width], BF16, name="rounded", tag=tag, align_bytes=64)
+            cols = slice(lo % PASS // 2, lo % PASS // 2 + width)
             for g, copy in enumerate(copies):
                 copy(
                     rounded[:, g].rearrange("p (m e j) -> p m j e", e=2, j=PACK),
                     raw[:].rearrange("p j (m g e) -> p g m j e", g=2, e=2)[:, g],
                 )
-                pair = slice(g * CHUNK, (g + 1) * CHUNK)
-                nc.vector.quantize_mx(out=codes[:, pair].bitcast(FP8X4), scales=scales[:, pair], in_=rounded[:, g])
-            return codes, scales
+                nc.vector.quantize_mx(
+                    out=w2_w[:, lo // PASS, g, cols].bitcast(FP8X4), scales=w2_s[:, lo // PASS, g, cols], in_=rounded[:, g]
+                )
 
         def load_wg(g, lo, hi):
             rows = wgs.rearrange("(i t) c -> i t c", t=PACK)
@@ -114,11 +116,11 @@ def tile_list_trie_leak_audit_kernel(
                 nc.sync.dma_start(out=plane[r:P:32, :].bitcast(I32), in_=rows[0, r:16:4, :].bitcast(I32))
 
         def load_w1(b):
-            words = keep.tile([P, CHUNK], I32, name="w1_in", tag="words%d" % (1 - b), align_bytes=64)
+            words = keep.tile([P, CHUNK], I32, name="w1_in", tag="w1_in%d" % b)
             nc.sync.dma_start(out=words[:], in_=w1_words[0].bitcast(I32)[:, b * CHUNK : (b + 1) * CHUNK])
             return words
 
-        w2_raw0 = load_w2(0)
+        w2_raw = [load_w2(0, CHUNK, "wide0")]
         load_scales(tab_s, tab_scales)
         nc.sync.dma_start(idx[:], offs)
         nc.sync.dma_start(
@@ -126,17 +128,19 @@ def tile_list_trie_leak_audit_kernel(
         )
         load_scales(w1_s_in, w1_scales)
         w1_w_in = [load_w1(0)]
+        w2_raw.append(load_w2(CHUNK, PASS, "rows1"))
         pages = {(0, 0): load_page(0, 0)}
         nc.sync.dma_start(idx2[:], offs2)
         load_wg(0, 0, CHUNK)
-        w1_w_in.append(load_w1(1))
         pages[0, 1] = load_page(0, 1)
-        load_wg(0, CHUNK, S)
-        w2_raw1 = load_w2(1)
+        w1_w_in.append(load_w1(1))
+        load_wg(0, CHUNK, HALF)
+        load_wg(0, HALF, S)
+        w2_raw.append(load_w2(PASS, H, "wide1"))
         nc.sync.dma_start(idx4[:], offs4)
         pages[0, 2] = load_page(0, 2)
-        load_wg(1, 0, S)
         pages[0, 3] = load_page(0, 3)
+        load_wg(1, 0, S)
         for t in range(PACK - 1):
             pages[1, t] = load_page(1, t)
         nc.sync.dma_start(idx3[:], offs3)
@@ -155,10 +159,10 @@ def tile_list_trie_leak_audit_kernel(
             )
 
         nc.vector.tensor_copy(v_s[:], tab_s[:].indirect(idx[:]))
-        w2_mx = [quantize_w2(w2_raw0, 0, (nc.scalar.copy, nc.scalar.copy))]
+        quantize_w2(w2_raw[0], 0, (nc.scalar.copy, nc.scalar.copy), "damp1")
 
         def gather_words(lo, tag):
-            words = keep.tile([P, HALF], U32, name="v_w", tag=tag, align_bytes=64)
+            words = work.tile([P, HALF], U32, name="v_w", tag=tag, align_bytes=64)
             nc.vector.tensor_copy(words[:], tab_w[:].bitcast(U32).indirect(entries(idx, lo, lo + HALF)))
             return words
 
@@ -174,18 +178,16 @@ def tile_list_trie_leak_audit_kernel(
 
         v_w = [gather_words(0, "v_w0")]
         deal_w1(0)
-        v_w.append(gather_words(HALF, "words1"))
-        deal_w1(1)
+        quantize_w2(w2_raw[1], CHUNK, (nc.vector.tensor_copy, nc.vector.tensor_copy), "late")
+        v_w.append(gather_words(HALF, "late"))
 
         def products(b, g, q, banks):
-            w2_w, w2_s = w2_mx[b]
-            pair = slice(g * CHUNK, (g + 1) * CHUNK)
             lo = b * PASS + g * CHUNK
             acc2 = psum.tile([P, 2, CHUNK], F32, name="acc2", tag="bank%d" % banks[0])
             acc1 = psum.tile([P, 2, CHUNK], F32, name="acc1", tag="bank%d" % banks[1])
             for acc, codes, scales in (
-                (acc2, w2_w[:, pair].bitcast(FP8X4), w2_s[:, pair]),
                 (acc1, w1_w[:].bitcast(U8)[:, 2 * lo : 2 * (lo + CHUNK)].bitcast(FP4X4), w1_s[:, lo : lo + CHUNK]),
+                (acc2, w2_w[:, b, g].bitcast(FP8X4), w2_s[:, b, g]),
             ):
                 for u in range(2):
                     cols = slice(q * CHUNK + u * P, q * CHUNK + (u + 1) * P)
@@ -198,21 +200,26 @@ def tile_list_trie_leak_audit_kernel(
                     )
             return [acc[:].rearrange("p u (m e) -> p e u m", e=2) for acc in (acc1, acc2)]
 
-        def features(b, g, q, h, span):
-            banks = (2 * (q % 2), 2 * (q % 2) + 1)
+        def features(b, g, q, h, span, second=None):
+            unit = q
+            banks = (2 * (unit % 2), 2 * (unit % 2) + 1)
             acc1, acc2 = products(b, g, q, banks)
-            first = work.tile([P, 2, 2, P], F32, name="first", tag="first", bufs=2)
-            second = work.tile([P, 2, 2, P], F32, name="second", tag="second%d" % (q % 2), align_bytes=64)
+            if (b, g, q) == (1, 1, 3):
+                first = work.tile([P, 2, 2, P], F32, name="first", tag="damp1", align_bytes=64)
+            else:
+                first = work.tile([P, 2, 2, P], F32, name="first", tag="first", bufs=2)
+            if second is None:
+                second = work.tile([P, 2, 2, P], F32, name="second", tag="second%d" % (unit % 2), align_bytes=64)
             for e0 in range(0, 2, span):
                 slots = slice(e0, e0 + span)
-                nc.scalar.activation(second[:, slots], acc2[:, slots], ACT.Tanh, scale=-1.0)
                 nc.scalar.copy(first[:, slots], acc1[:, slots])
-                turned = psum.tile([P, span, CHUNK], F32, name="turned", tag="bank%d" % (4 + (q + 3 * e0) % 4))
+                nc.scalar.activation(second[:, slots], acc2[:, slots], ACT.Tanh, scale=-1.0)
+                turned = psum.tile([P, span, CHUNK], F32, name="turned", tag="bank%d" % (banks[1 - e0] if (b, g) == (0, 0) and q < 2 else 4 + unit % 4))
                 for e in range(span):
                     for u in range(2):
                         dst = turned[:, e, u * P : (u + 1) * P]
-                        nc.tensor.matmul(dst, first[:, e0 + e, u, :], ident[:], start=True, stop=False, is_transpose=True)
-                        nc.tensor.matmul(dst, second[:, e0 + e, u, :], ident[:], start=False, stop=True, is_transpose=True)
+                        nc.tensor.matmul(dst, second[:, e0 + e, u, :], ident[:], start=True, stop=False, is_transpose=True)
+                        nc.tensor.matmul(dst, first[:, e0 + e, u, :], ident[:], start=False, stop=True, is_transpose=True)
                 nc.scalar.copy(h[:, 2 * g + e0 : 2 * g + e0 + span, q * CHUNK : (q + 1) * CHUNK], turned[:])
 
         def scatter(b, t, h, lo, hi):
@@ -269,12 +276,14 @@ def tile_list_trie_leak_audit_kernel(
             features(0, 0, q, h0, 1 if q == 0 else 2)
             for t in range(2):
                 scatter(0, t, h0, q * CHUNK, (q + 1) * CHUNK)
-        w2_mx.append(quantize_w2(w2_raw1, 1, (nc.scalar.copy, nc.scalar.copy)))
-        damps = [work.tile([P, PACK, M], F32, name="damp%d" % b, align_bytes=64) for b in range(BLOCKS)]
+        deal_w1(1)
+        quantize_w2(w2_raw[2], PASS, (nc.scalar.copy, nc.scalar.copy), "damp0")
+        damps = [work.tile([P, PACK, M], F32, name="damp0", align_bytes=64)]
         for t in range(2):
             fetch_link(0, t)
+        held = work.tile([P, 2, 2, 2, P], F32, name="held", tag="wide1", align_bytes=64)
         for q in range(S // CHUNK):
-            features(0, 1, q, h0, 2)
+            features(0, 1, q, h0, 2, held[:, q - 1] if q in (1, 2) else None)
         for lo in range(0, S, HALF):
             for t in range(2, PACK):
                 scatter(0, t, h0, lo, lo + HALF)
@@ -284,10 +293,13 @@ def tile_list_trie_leak_audit_kernel(
         for g in range(2):
             for q in range(S // CHUNK):
                 features(1, g, q, h1, 2)
+        damps.append(work.tile([P, PACK, M], F32, name="damp1", align_bytes=64))
         last = PACK - 1
         for t in range(last):
             scatter(1, t, h1, 0, S)
-            fetch_link(1, t)
+            if t > 0:
+                fetch_link(1, t - 1)
+        fetch_link(1, last - 1)
 
         damping(0, [(0, 0, M), (1, 0, M)], "second1")
         damping(0, [(2, 0, M), (3, 0, M)], "second1", "page13")

@@ -55,6 +55,7 @@ def tile_list_trie_leak_audit_kernel(
 
         tab_w = keep.tile([P, T], I32, align_bytes=64)
         tab_s = keep.tile([P, T], U8, align_bytes=64)
+        v_s_spread = keep.tile([P, S], U8, align_bytes=64)
         w1_s_in = keep.tile([P, H], U8)
         w1_w = keep.tile([P, H // 2], I32, align_bytes=64)
         w1_s = keep.tile([P, H], U8, align_bytes=64)
@@ -67,7 +68,8 @@ def tile_list_trie_leak_audit_kernel(
         one = keep.tile([P, 1], F32)
 
         nc.vector.memset(tab_s[:].bitcast(I32), 0)
-        nc.vector.memset(w1_s_in[:].bitcast(I32), 0)
+        nc.gpsimd.memset(w1_s_in[:].bitcast(I32), 0)
+        nc.vector.memset(v_s[:].bitcast(I32), 0)
         nc.gpsimd.memset(w3_s[:].bitcast(I32), 0)
         nc.gpsimd.memset(one[:], 1.0)
         make_identity(nc, ident[:])
@@ -121,14 +123,17 @@ def tile_list_trie_leak_audit_kernel(
             return words
 
         w2_raw = [load_w2(0, CHUNK, "wide0")]
-        load_scales(tab_s, tab_scales)
+        nc.sync.dma_start(out=tab_s[0:P:8, :].bitcast(I32), in_=tab_scales[0].bitcast(I32))
+        load_scales(w1_s_in, w1_scales)
         nc.sync.dma_start(idx[:], offs)
         nc.sync.dma_start(
             out=tab_w[:], in_=tab_words[0].rearrange("p n t -> p (n t)").bitcast(I32)
         )
-        load_scales(w1_s_in, w1_scales)
         w1_w_in = [load_w1(0)]
         w2_raw.append(load_w2(CHUNK, PASS, "rows1"))
+        nc.vector.tensor_copy(v_s_spread[:], tab_s[:].indirect(idx[:]))
+        for r in range(4):
+            nc.sync.dma_start(out=v_s[r:P:32, :].bitcast(I32), in_=v_s_spread[8 * r : P : 32, :].bitcast(I32))
         pages = {(0, 0): load_page(0, 0)}
         nc.sync.dma_start(idx2[:], offs2)
         load_wg(0, 0, CHUNK)
@@ -158,7 +163,6 @@ def tile_list_trie_leak_audit_kernel(
                 in_=w3_scales[:, 4 * quadrant : 4 * quadrant + 4, :].bitcast(I32).rearrange("b r n -> r b n"),
             )
 
-        nc.vector.tensor_copy(v_s[:], tab_s[:].indirect(idx[:]))
         quantize_w2(w2_raw[0], 0, (nc.scalar.copy, nc.scalar.copy), "damp1")
 
         def gather_words(lo, tag):

@@ -16,6 +16,7 @@ FP8X4 = mybir.dt.float8_e4m3fn_x4
 FP4X4 = mybir.dt.float4_e2m1fn_x4
 ACT = mybir.ActivationFunctionType
 MULT = mybir.AluOpType.mult
+SUBTRACT = mybir.AluOpType.subtract
 
 P = 128
 PACK = 4
@@ -28,13 +29,6 @@ PIECES = ((0, 256), (256, 512), (512, 768), (768, 896), (896, 1024))
 
 def entries(offsets, lo, hi):
     return offsets[:, lo // 16 : hi // 16]
-
-
-def interleaved(dst, src):
-    return (
-        dst.rearrange("p (c i t) -> p c t i", i=4, t=PACK),
-        src.rearrange("p t (c i) -> p c t i", i=4),
-    )
 
 
 def tile_list_trie_leak_audit_kernel(
@@ -54,14 +48,20 @@ def tile_list_trie_leak_audit_kernel(
         idx4 = lists.tile([P, M // 16], U16)
 
         tab_w = keep.tile([P, T], I32, align_bytes=64)
-        tab_s = keep.tile([P, T], U8, align_bytes=64)
+        tab_s = work.tile([P, T], U8, tag="page00", align_bytes=64)
+        v_w = keep.tile([P, S], U32, align_bytes=64)
         v_s_spread = keep.tile([P, S], U8, align_bytes=64)
+        v_s = keep.tile([P, S], U8, align_bytes=64)
+        w1_w_in = keep.tile([P, 2 * H], U8)
         w1_s_in = keep.tile([P, H], U8)
-        w1_w = keep.tile([P, H // 2], I32, align_bytes=64)
-        w1_s = keep.tile([P, H], U8, align_bytes=64)
+        w1_w = keep.tile([P, BLOCKS, PACK, 2 * P], U8, align_bytes=64)
+        w1_s = keep.tile([P, BLOCKS, PACK, P], U8, align_bytes=64)
+        w2_w = keep.tile([P, BLOCKS, PACK, P], U32, align_bytes=64)
+        w2_s = keep.tile([P, BLOCKS, PACK, P], U8, align_bytes=64)
         w3_w = keep.tile([P, BLOCKS * N], I32, align_bytes=64)
         w3_s = keep.tile([P, BLOCKS * N], U8, align_bytes=64)
-        v_s = keep.tile([P, S], U8, align_bytes=64)
+        z_w = keep.tile([P, BLOCKS, M], U32, align_bytes=64)
+        z_s = keep.tile([P, BLOCKS, M], U8, align_bytes=64)
         wg = keep.tile([P, PACK, S], F32)
         gain_sb = keep.tile([P, BLOCKS, PACK], F32)
         ident = keep.tile([P, P], F32)
@@ -74,84 +74,56 @@ def tile_list_trie_leak_audit_kernel(
         nc.gpsimd.memset(one[:], 1.0)
         make_identity(nc, ident[:])
 
-        w2_rows = w2.rearrange("(p j) c -> p j c", j=PACK)
-
-        def load_w2(lo, hi, tag):
-            raw = work.tile([P, PACK, hi - lo], F32, name="raw", tag=tag, align_bytes=64)
-            nc.sync.dma_start(out=raw[:], in_=w2_rows[:, :, lo:hi])
+        def load_w2(b):
+            raw = work.tile([P, PACK, PASS], F32, name="raw", tag="wide%d" % b, align_bytes=64)
+            nc.sync.dma_start(
+                out=raw[:], in_=w2.rearrange("(p j) c -> p j c", j=PACK)[:, :, b * PASS : (b + 1) * PASS]
+            )
             return raw
 
-        w2_w = keep.tile([P, BLOCKS, 2, CHUNK], U32, align_bytes=64)
-        w2_s = keep.tile([P, BLOCKS, 2, CHUNK], U8, align_bytes=64)
-
-        def quantize_w2(raw, lo, copies, tag):
-            width = raw.shape[2] // 2
-            rounded = work.tile([P, 2, PACK * width], BF16, name="rounded", tag=tag, align_bytes=64)
-            cols = slice(lo % PASS // 2, lo % PASS // 2 + width)
-            for g, copy in enumerate(copies):
-                copy(
-                    rounded[:, g].rearrange("p (m e j) -> p m j e", e=2, j=PACK),
-                    raw[:].rearrange("p j (m g e) -> p g m j e", g=2, e=2)[:, g],
-                )
-                nc.vector.quantize_mx(
-                    out=w2_w[:, lo // PASS, g, cols].bitcast(FP8X4), scales=w2_s[:, lo // PASS, g, cols], in_=rounded[:, g]
-                )
-
-        def load_wg(g, lo, hi):
+        def load_wg(t0, t1, lo, hi):
             rows = wgs.rearrange("(i t) c -> i t c", t=PACK)
             for quadrant in (0, 2, 1, 3):
                 nc.sync.dma_start(
-                    out=wg[32 * quadrant : 32 * quadrant + 32, 2 * g : 2 * g + 2, lo:hi],
-                    in_=rows[:, 2 * g : 2 * g + 2, lo:hi],
+                    out=wg[32 * quadrant : 32 * quadrant + 32, t0:t1, lo:hi], in_=rows[:, t0:t1, lo:hi]
                 )
 
+        pages = {}
+
         def load_page(b, t):
-            page = work.tile([P, T2], F32, name="page%d%d" % (b, t), align_bytes=64)
+            pages[b, t] = work.tile([P, T2], F32, name="page%d%d" % (b, t), align_bytes=64)
             nc.sync.dma_start(
-                out=page[:],
-                in_=page0.rearrange("(b p t) c -> b t p c", b=BLOCKS, t=PACK)[b, t],
+                out=pages[b, t][:], in_=page0.rearrange("(b p t) c -> b t p c", b=BLOCKS, t=PACK)[b, t]
             )
-            return page
 
-        def load_scales(plane, rows):
-            for r in range(4):
-                nc.sync.dma_start(out=plane[r:P:32, :].bitcast(I32), in_=rows[0, r:16:4, :].bitcast(I32))
-
-        def load_w1(b):
-            words = keep.tile([P, CHUNK], I32, name="w1_in", tag="w1_in%d" % b)
-            nc.sync.dma_start(out=words[:], in_=w1_words[0].bitcast(I32)[:, b * CHUNK : (b + 1) * CHUNK])
-            return words
-
-        w2_raw = [load_w2(0, CHUNK, "wide0")]
-        nc.sync.dma_start(out=tab_s[0:P:8, :].bitcast(I32), in_=tab_scales[0].bitcast(I32))
-        load_scales(w1_s_in, w1_scales)
         nc.sync.dma_start(idx[:], offs)
-        nc.sync.dma_start(
-            out=tab_w[:], in_=tab_words[0].rearrange("p n t -> p (n t)").bitcast(I32)
-        )
-        w1_w_in = [load_w1(0)]
-        w2_raw.append(load_w2(CHUNK, PASS, "rows1"))
+        w2_raw = [load_w2(0)]
+        nc.sync.dma_start(out=tab_s[0:P:8, :].bitcast(I32), in_=tab_scales[0].bitcast(I32))
+        for r in range(4):
+            nc.sync.dma_start(out=w1_s_in[r:P:32, :].bitcast(I32), in_=w1_scales[0, r:16:4, :].bitcast(I32))
+        nc.sync.dma_start(out=w1_w_in[:].bitcast(I32), in_=w1_words[0].bitcast(I32))
+        nc.sync.dma_start(out=tab_w[:], in_=tab_words[0].rearrange("p n t -> p (n t)").bitcast(I32))
         nc.vector.tensor_copy(v_s_spread[:], tab_s[:].indirect(idx[:]))
         for r in range(4):
             nc.sync.dma_start(out=v_s[r:P:32, :].bitcast(I32), in_=v_s_spread[8 * r : P : 32, :].bitcast(I32))
-        pages = {(0, 0): load_page(0, 0)}
+        load_page(0, 0)
         nc.sync.dma_start(idx2[:], offs2)
-        load_wg(0, 0, CHUNK)
-        pages[0, 1] = load_page(0, 1)
-        w1_w_in.append(load_w1(1))
-        load_wg(0, CHUNK, HALF)
-        load_wg(0, HALF, S)
-        w2_raw.append(load_w2(PASS, H, "wide1"))
+        load_wg(0, 1, 0, CHUNK)
+        load_wg(0, 1, CHUNK, HALF)
+        load_wg(0, 1, HALF, S)
+        load_page(0, 1)
+        load_wg(1, 2, 0, HALF)
         nc.sync.dma_start(idx4[:], offs4)
-        pages[0, 2] = load_page(0, 2)
-        pages[0, 3] = load_page(0, 3)
-        load_wg(1, 0, S)
+        w2_raw.append(load_w2(1))
+        load_page(0, 2)
+        load_wg(1, 2, HALF, S)
+        load_page(0, 3)
+        load_wg(2, 4, 0, HALF)
+        load_wg(2, 4, HALF, S)
         for t in range(PACK - 1):
-            pages[1, t] = load_page(1, t)
+            load_page(1, t)
         nc.sync.dma_start(idx3[:], offs3)
-        nc.sync.dma_start(
-            out=gain_sb[:], in_=gain.rearrange("(b p t) -> p b t", b=BLOCKS, t=PACK)
-        )
+        nc.sync.dma_start(out=gain_sb[:], in_=gain.rearrange("(b p t) -> p b t", b=BLOCKS, t=PACK))
         for b in range(BLOCKS):
             nc.sync.dma_start(
                 out=w3_w[:, b * N : (b + 1) * N],
@@ -163,75 +135,79 @@ def tile_list_trie_leak_audit_kernel(
                 in_=w3_scales[:, 4 * quadrant : 4 * quadrant + 4, :].bitcast(I32).rearrange("b r n -> r b n"),
             )
 
-        quantize_w2(w2_raw[0], 0, (nc.scalar.copy, nc.scalar.copy), "damp1")
-
-        def gather_words(lo, tag):
-            words = work.tile([P, HALF], U32, name="v_w", tag=tag, align_bytes=64)
-            nc.vector.tensor_copy(words[:], tab_w[:].bitcast(U32).indirect(entries(idx, lo, lo + HALF)))
-            return words
-
-        def deal_w1(b):
-            nc.vector.tensor_copy(
-                w1_s[:].rearrange("p (b g m e) -> p b g m e", b=BLOCKS, g=2, e=2)[:, b],
-                w1_s_in[:].rearrange("p (b m g e) -> p b g m e", b=BLOCKS, g=2, e=2)[:, b],
+        def quantize_w2(b, tag):
+            rounded = work.tile([P, PACK, P, PACK], BF16, name="rounded", tag=tag, align_bytes=64)
+            nc.scalar.copy(
+                rounded[:].rearrange("p t m j -> p m j t"),
+                w2_raw[b][:].rearrange("p j (m t) -> p m j t", t=PACK),
             )
-            nc.vector.tensor_copy(
-                w1_w[:].rearrange("p (b g m) -> p b g m", b=BLOCKS, g=2)[:, b],
-                w1_w_in[b][:].rearrange("p (m g) -> p g m", g=2),
+            nc.vector.quantize_mx(
+                out=w2_w[:, b].rearrange("p t m -> p (t m)").bitcast(FP8X4),
+                scales=w2_s[:, b].rearrange("p t m -> p (t m)"),
+                in_=rounded[:].rearrange("p t m j -> p (t m j)"),
             )
 
-        v_w = [gather_words(0, "v_w0")]
-        deal_w1(0)
-        quantize_w2(w2_raw[1], CHUNK, (nc.vector.tensor_copy, nc.vector.tensor_copy), "late")
-        v_w.append(gather_words(HALF, "late"))
+        nc.vector.tensor_copy(w1_s[:], w1_s_in[:].rearrange("p (b m t) -> p b t m", b=BLOCKS, t=PACK))
+        quantize_w2(0, "damp1")
+        for b in range(BLOCKS):
+            nc.vector.tensor_copy(
+                w1_w[:, b].rearrange("p t (m e) -> p t m e", e=2),
+                w1_w_in[:].rearrange("p (b m t e) -> p b t m e", b=BLOCKS, t=PACK, e=2)[:, b],
+            )
+        for lo in range(0, S, HALF):
+            nc.vector.tensor_copy(
+                v_w[:, lo : lo + HALF], tab_w[:].bitcast(U32).indirect(entries(idx, lo, lo + HALF))
+            )
 
-        def products(b, g, q, banks):
-            lo = b * PASS + g * CHUNK
-            acc2 = psum.tile([P, 2, CHUNK], F32, name="acc2", tag="bank%d" % banks[0])
-            acc1 = psum.tile([P, 2, CHUNK], F32, name="acc1", tag="bank%d" % banks[1])
-            for acc, codes, scales in (
-                (acc1, w1_w[:].bitcast(U8)[:, 2 * lo : 2 * (lo + CHUNK)].bitcast(FP4X4), w1_s[:, lo : lo + CHUNK]),
-                (acc2, w2_w[:, b, g].bitcast(FP8X4), w2_s[:, b, g]),
-            ):
-                for u in range(2):
-                    cols = slice(q * CHUNK + u * P, q * CHUNK + (u + 1) * P)
+        def weights(b, t):
+            return (
+                (w1_w[:, b, t].bitcast(FP4X4), w1_s[:, b, t]),
+                (w2_w[:, b, t].bitcast(FP8X4), w2_s[:, b, t]),
+            )
+
+        def bank(shape, number, name):
+            return psum.tile(shape, F32, name=name, tag="bank%d" % number)
+
+        def first_features(h, q):
+            cols = slice(q * CHUNK, (q + 1) * CHUNK)
+            sums = [bank([P, CHUNK], 2 * q + e, "sums") for e in range(2)]
+            for acc, (codes, scales) in reversed(list(zip(sums, weights(0, 0)))):
+                nc.tensor.matmul_mx(
+                    out=acc[:], lhsT=codes, lhsT_scale=scales,
+                    rhs=v_w[:, cols].bitcast(FP8X4), rhs_scale=v_s[:, cols],
+                    start=True, stop=True,
+                )
+            second = work.tile([P, CHUNK], F32, name="second", tag="second%d" % q, align_bytes=64)
+            nc.scalar.activation(second[:], sums[1][:], ACT.Tanh)
+            nc.vector.tensor_tensor(h[:, 0, cols], sums[0][:], second[:], SUBTRACT)
+
+        def features(unit, b, t, lo, h, first=None, second=None, spare=0):
+            sums = [bank([P, PACK, P], spare + 2 * (unit % 2) + e, "sums") for e in range(2)]
+            for acc, (codes, scales) in zip(sums, weights(b, t)):
+                for u in range(PACK):
+                    cols = slice(lo + u * P, lo + (u + 1) * P)
                     nc.tensor.matmul_mx(
-                        out=acc[:, u, :],
-                        lhsT=v_w[q // 2][:, cols.start % HALF : cols.start % HALF + P].bitcast(FP8X4),
-                        lhsT_scale=v_s[:, cols],
-                        rhs=codes, rhs_scale=scales,
-                        start=True, stop=True,
+                        out=acc[:, u], lhsT=v_w[:, cols].bitcast(FP8X4), lhsT_scale=v_s[:, cols],
+                        rhs=codes, rhs_scale=scales, start=True, stop=True,
                     )
-            return [acc[:].rearrange("p u (m e) -> p e u m", e=2) for acc in (acc1, acc2)]
-
-        def features(b, g, q, h, span, second=None):
-            unit = q
-            banks = (2 * (unit % 2), 2 * (unit % 2) + 1)
-            acc1, acc2 = products(b, g, q, banks)
-            if (b, g, q) == (1, 1, 3):
-                first = work.tile([P, 2, 2, P], F32, name="first", tag="damp1", align_bytes=64)
-            else:
-                first = work.tile([P, 2, 2, P], F32, name="first", tag="first", bufs=2)
+            if first is None:
+                first = work.tile([P, PACK, P], F32, name="first", tag="first", bufs=2)
             if second is None:
-                second = work.tile([P, 2, 2, P], F32, name="second", tag="second%d" % (unit % 2), align_bytes=64)
-            for e0 in range(0, 2, span):
-                slots = slice(e0, e0 + span)
-                nc.scalar.copy(first[:, slots], acc1[:, slots])
-                nc.scalar.activation(second[:, slots], acc2[:, slots], ACT.Tanh, scale=-1.0)
-                turned = psum.tile([P, span, CHUNK], F32, name="turned", tag="bank%d" % (banks[1 - e0] if (b, g) == (0, 0) and q < 2 else 4 + unit % 4))
-                for e in range(span):
-                    for u in range(2):
-                        dst = turned[:, e, u * P : (u + 1) * P]
-                        nc.tensor.matmul(dst, second[:, e0 + e, u, :], ident[:], start=True, stop=False, is_transpose=True)
-                        nc.tensor.matmul(dst, first[:, e0 + e, u, :], ident[:], start=False, stop=True, is_transpose=True)
-                nc.scalar.copy(h[:, 2 * g + e0 : 2 * g + e0 + span, q * CHUNK : (q + 1) * CHUNK], turned[:])
+                second = work.tile([P, PACK, P], F32, name="second", tag="second%d" % (unit % 2), align_bytes=64)
+            nc.scalar.copy(first[:], sums[0][:])
+            nc.scalar.activation(second[:], sums[1][:], ACT.Tanh, scale=-1.0)
+            turned = bank([P, PACK, P], (4 + spare + unit % 4) % 8, "turned")
+            for u in range(PACK):
+                nc.tensor.matmul(turned[:, u], second[:, u], ident[:], start=True, stop=False, is_transpose=True)
+                nc.tensor.matmul(turned[:, u], first[:, u], ident[:], start=False, stop=True, is_transpose=True)
+            nc.scalar.copy(h[:, t, lo : lo + HALF], turned[:].rearrange("p u j -> p (u j)"))
 
         def scatter(b, t, h, lo, hi):
             nc.vector.tensor_tensor(
-                pages[b, t][:].indirect(entries(idx2, lo, hi)),
-                h[:, t, lo:hi], wg[:, t, lo:hi], MULT,
+                pages[b, t][:].indirect(entries(idx2, lo, hi)), h[:, t, lo:hi], wg[:, t, lo:hi], MULT
             )
 
+        damps = []
 
         def fetch_link(b, t):
             nc.vector.tensor_copy(damps[b][:, t, :], pages[b, t][:].indirect(idx4[:]))
@@ -249,108 +225,106 @@ def tile_list_trie_leak_audit_kernel(
             for e, (t, lo, hi) in enumerate(parts):
                 nc.scalar.activation(damps[b][:, t, lo:hi], root[:, e], ACT.Copy, scale=gain_sb[:, b, t : t + 1])
 
-        def fetch_nodes(b, lo, hi, z):
+        def fetch_nodes(b, lo, hi, tag):
+            z = work.tile([P, PACK, hi - lo], F32, name="z", tag=tag, align_bytes=64)
             for t in range(PACK):
                 nc.vector.tensor_tensor(
-                    z[:, t, :], pages[b, t][:].indirect(entries(idx3, lo, hi)), damps[b][:, t, lo:hi], MULT
+                    z[:, t], pages[b, t][:].indirect(entries(idx3, lo, hi)), damps[b][:, t, lo:hi], MULT
                 )
+            return z
 
-        z_w = [keep.tile([P, M], U32, name="z_w%d" % b, align_bytes=64) for b in range(BLOCKS)]
-        z_s = [keep.tile([P, M], U8, name="z_s%d" % b, align_bytes=64) for b in range(BLOCKS)]
-
-        def quantize_z(b, z, lo, hi, copy, part):
-            copy(*interleaved(part, z))
-            nc.vector.quantize_mx(out=z_w[b][:, lo:hi].bitcast(FP8X4), scales=z_s[b][:, lo:hi], in_=part)
+        def quantize_z(b, z, lo, hi, copy, tag, bufs=1):
+            rounded = work.tile([P, PACK * (hi - lo)], BF16, name="rounded", tag=tag, bufs=bufs, align_bytes=64)
+            copy(
+                rounded[:].rearrange("p (c i t) -> p c t i", i=4, t=PACK),
+                z[:].rearrange("p t (c i) -> p c t i", i=4),
+            )
+            nc.vector.quantize_mx(out=z_w[:, b, lo:hi].bitcast(FP8X4), scales=z_s[:, b, lo:hi], in_=rounded[:])
 
         def scores_pass(b, banks, lo, hi):
             share = N // P // len(banks)
             for n in range(N // P):
                 cols = slice(b * N + n * P, b * N + (n + 1) * P)
                 nc.tensor.matmul_mx(
-                    out=banks[n // share][:, n % share, :],
+                    out=banks[n // share][:, n % share],
                     lhsT=w3_w[:, cols].bitcast(FP8X4), lhsT_scale=w3_s[:, cols],
-                    rhs=z_w[b][:, lo:hi].bitcast(FP8X4), rhs_scale=z_s[b][:, lo:hi],
+                    rhs=z_w[:, b, lo:hi].bitcast(FP8X4), rhs_scale=z_s[:, b, lo:hi],
                     start=(b == 0 and n % share == 0), stop=(b == BLOCKS - 1 and n % share == share - 1),
                 )
 
-        out_rows = out.rearrange("(n p) m -> p n m", p=P)
-
         h0 = work.tile([P, PACK, S], F32, name="h0", tag="rows0", align_bytes=64)
-        for q in range(S // CHUNK):
-            features(0, 0, q, h0, 1 if q == 0 else 2)
-            for t in range(2):
-                scatter(0, t, h0, q * CHUNK, (q + 1) * CHUNK)
-        deal_w1(1)
-        quantize_w2(w2_raw[2], PASS, (nc.scalar.copy, nc.scalar.copy), "damp0")
-        damps = [work.tile([P, PACK, M], F32, name="damp0", align_bytes=64)]
-        for t in range(2):
-            fetch_link(0, t)
-        held = work.tile([P, 2, 2, 2, P], F32, name="held", tag="wide1", align_bytes=64)
-        for q in range(S // CHUNK):
-            features(0, 1, q, h0, 2, held[:, q - 1] if q in (1, 2) else None)
+        for q in range(2):
+            first_features(h0, q)
+        for q in range(2):
+            scatter(0, 0, h0, q * CHUNK, (q + 1) * CHUNK)
+        features(0, 0, 0, HALF, h0, spare=4)
+        scatter(0, 0, h0, HALF, S)
+        damps.append(work.tile([P, PACK, M], F32, name="damp0", align_bytes=64))
+        features(1, 0, 1, 0, h0)
+        scatter(0, 1, h0, 0, HALF)
+        fetch_link(0, 0)
+        features(2, 0, 1, HALF, h0)
+        scatter(0, 1, h0, HALF, S)
+        features(3, 0, 2, 0, h0)
+        quantize_w2(1, "rounded_w2")
+        fetch_link(0, 1)
+        held = work.tile([P, 2, PACK, P], F32, name="held", tag="wide1", align_bytes=64)
+        features(4, 0, 3, 0, h0, second=held[:, 0])
+        features(5, 0, 2, HALF, h0, second=held[:, 1])
+        features(6, 0, 3, HALF, h0)
         for lo in range(0, S, HALF):
             for t in range(2, PACK):
                 scatter(0, t, h0, lo, lo + HALF)
         for t in range(2, PACK):
             fetch_link(0, t)
         h1 = work.tile([P, PACK, S], F32, name="h1", tag="rows1", align_bytes=64)
-        for g in range(2):
-            for q in range(S // CHUNK):
-                features(1, g, q, h1, 2)
-        damps.append(work.tile([P, PACK, M], F32, name="damp1", align_bytes=64))
         last = PACK - 1
+        for t in range(PACK):
+            for k in range(2):
+                first = None
+                if (t, k) == (last, 1):
+                    first = work.tile([P, PACK, P], F32, name="first", tag="damp1", align_bytes=64)
+                features(2 * t + k + 1, 1, t, k * HALF, h1, first=first)
+        damps.append(work.tile([P, PACK, M], F32, name="damp1", align_bytes=64))
         for t in range(last):
             scatter(1, t, h1, 0, S)
             if t > 0:
                 fetch_link(1, t - 1)
         fetch_link(1, last - 1)
 
-        damping(0, [(0, 0, M), (1, 0, M)], "second1")
-        damping(0, [(2, 0, M), (3, 0, M)], "second1", "page13")
-        pages[1, last] = load_page(1, last)
-        damping(1, [(0, 0, M), (1, 0, M)], "second1")
-        damping(1, [(2, 0, HALF), (2, HALF, M)], "second1")
-
-        def quantize_z0(k, z, tag):
-            rounded = work.tile([P, PACK * HALF], BF16, name="rounded0", tag=tag, align_bytes=64)
-            quantize_z(0, z[:], k * HALF, (k + 1) * HALF, nc.scalar.copy, rounded[:])
-
-        z00 = work.tile([P, PACK, HALF], F32, name="z0", tag="rows0", align_bytes=64)
-        fetch_nodes(0, 0, HALF, z00[:])
-        quantize_z0(0, z00, "second1")
+        damping(0, [(0, 0, M), (1, 0, M)], "second0")
+        damping(0, [(2, 0, M), (3, 0, M)], "second0", "page13")
+        load_page(1, last)
+        damping(1, [(0, 0, M), (1, 0, M)], "second0")
+        damping(1, [(2, 0, HALF), (2, HALF, M)], "second0")
+        quantize_z(0, fetch_nodes(0, 0, HALF, "rows0"), 0, HALF, nc.scalar.copy, "second0")
         scatter(1, last, h1, 0, S)
         fetch_link(1, last)
         damping(1, [(last, 0, HALF), (last, HALF, M)], "rows0", "wide1")
-        z01 = work.tile([P, PACK, HALF], F32, name="z0", tag="rows1", align_bytes=64)
-        fetch_nodes(0, HALF, M, z01[:])
-        quantize_z0(1, z01, "rows0")
-        staged = work.tile([P, N // P, M], F32, name="staged", tag="damp0", align_bytes=64)
+        quantize_z(0, fetch_nodes(0, HALF, M, "rows1"), HALF, M, nc.scalar.copy, "rows0")
 
+        staged = work.tile([P, N // P, M], F32, name="staged", tag="damp0", align_bytes=64)
+        out_rows = out.rearrange("(n p) m -> p n m", p=P)
         banks = []
         for i, (lo, hi) in enumerate(PIECES):
             count = 1 if i == len(PIECES) - 2 else 2
-            banks.append([
-                psum.tile([P, N // P // count, hi - lo], F32, name="scores", tag="bank%d" % ((sum(map(len, banks)) + e) % 8))
-                for e in range(count)
-            ])
+            used = sum(map(len, banks))
+            banks.append([bank([P, N // P // count, hi - lo], (used + e) % 8, "scores") for e in range(count)])
 
         def finish(i):
             lo, hi = PIECES[i]
             final = i == len(PIECES) - 1
             share = N // P // len(banks[i])
-            for e, bank in enumerate(banks[i]):
-                part = staged[:, e * share : (e + 1) * share, lo:hi]
+            for e, sums in enumerate(banks[i]):
+                rows = slice(e * share, (e + 1) * share)
                 copy = nc.vector.tensor_copy if final and e == 0 else nc.scalar.copy
-                copy(part, bank[:])
-                nc.sync.dma_start(out=out_rows[:, e * share : (e + 1) * share, lo:hi], in_=part)
+                copy(staged[:, rows, lo:hi], sums[:])
+                nc.sync.dma_start(out=out_rows[:, rows, lo:hi], in_=staged[:, rows, lo:hi])
 
         for i, (lo, hi) in enumerate(PIECES):
-            z = work.tile([P, PACK, hi - lo], F32, name="z", tag=("wide0", "rows1")[i % 2], align_bytes=64)
-            fetch_nodes(1, lo, hi, z[:])
+            z = fetch_nodes(1, lo, hi, ("wide0", "rows1")[i % 2])
             scores_pass(0, banks[i], lo, hi)
-            rounded = work.tile([P, PACK * CHUNK], BF16, name="rounded", tag="rounded", bufs=2, align_bytes=64)
-            final = i == len(PIECES) - 1
-            quantize_z(1, z[:], lo, hi, nc.vector.tensor_copy if final else nc.scalar.copy, rounded[:, : PACK * (hi - lo)])
+            quantize_z(1, z, lo, hi, nc.vector.tensor_copy if hi - lo == P else nc.scalar.copy, "rounded", 2)
             scores_pass(1, banks[i], lo, hi)
             if i > 0:
                 finish(i - 1)

@@ -88,6 +88,10 @@ def tile_list_trie_leak_audit_kernel(
                     out=wg[32 * quadrant : 32 * quadrant + 32, t0:t1, lo:hi], in_=rows[:, t0:t1, lo:hi]
                 )
 
+        def load_w1(lo, hi):
+            cols = slice(2 * lo, 2 * hi)
+            nc.sync.dma_start(out=w1_w_in[:, cols].bitcast(I32), in_=w1_words[0][:, cols].bitcast(I32))
+
         pages = {}
 
         def load_page(b, t):
@@ -101,7 +105,7 @@ def tile_list_trie_leak_audit_kernel(
         nc.sync.dma_start(out=tab_s[0:P:8, :].bitcast(I32), in_=tab_scales[0].bitcast(I32))
         for r in range(4):
             nc.sync.dma_start(out=w1_s_in[r:P:32, :].bitcast(I32), in_=w1_scales[0, r:16:4, :].bitcast(I32))
-        nc.sync.dma_start(out=w1_w_in[:].bitcast(I32), in_=w1_words[0].bitcast(I32))
+        load_w1(0, PASS)
         nc.sync.dma_start(out=tab_w[:], in_=tab_words[0].rearrange("p n t -> p (n t)").bitcast(I32))
         nc.vector.tensor_copy(v_s_spread[:], tab_s[:].indirect(idx[:]))
         for r in range(4):
@@ -109,16 +113,19 @@ def tile_list_trie_leak_audit_kernel(
         load_page(0, 0)
         nc.sync.dma_start(idx2[:], offs2)
         load_wg(0, 1, 0, CHUNK)
+        load_w1(PASS, PASS + CHUNK)
         load_wg(0, 1, CHUNK, HALF)
+        load_w1(PASS + CHUNK, H)
         load_wg(0, 1, HALF, S)
         load_page(0, 1)
         load_wg(1, 2, 0, HALF)
         nc.sync.dma_start(idx4[:], offs4)
         w2_raw.append(load_w2(1))
-        load_page(0, 2)
         load_wg(1, 2, HALF, S)
+        load_page(0, 2)
+        load_wg(2, 3, 0, HALF)
         load_page(0, 3)
-        load_wg(2, 4, 0, HALF)
+        load_wg(3, 4, 0, HALF)
         load_wg(2, 4, HALF, S)
         for t in range(PACK - 1):
             load_page(1, t)
@@ -135,25 +142,31 @@ def tile_list_trie_leak_audit_kernel(
                 in_=w3_scales[:, 4 * quadrant : 4 * quadrant + 4, :].bitcast(I32).rearrange("b r n -> r b n"),
             )
 
-        def quantize_w2(b, tag):
-            rounded = work.tile([P, PACK, P, PACK], BF16, name="rounded", tag=tag, align_bytes=64)
-            nc.scalar.copy(
-                rounded[:].rearrange("p t m j -> p m j t"),
-                w2_raw[b][:].rearrange("p j (m t) -> p m j t", t=PACK),
-            )
-            nc.vector.quantize_mx(
-                out=w2_w[:, b].rearrange("p t m -> p (t m)").bitcast(FP8X4),
-                scales=w2_s[:, b].rearrange("p t m -> p (t m)"),
-                in_=rounded[:].rearrange("p t m j -> p (t m j)"),
-            )
+        def quantize_w2(b, span):
+            rounded = work.tile([P, PACK, P, PACK], BF16, name="rounded_w2", align_bytes=64)
+            for t in range(0, PACK, span):
+                slots = slice(t, t + span)
+                nc.scalar.copy(
+                    rounded[:, slots].rearrange("p t m j -> p m j t"),
+                    w2_raw[b][:].rearrange("p j (m t) -> p m j t", t=PACK)[:, :, :, slots],
+                )
+                nc.vector.quantize_mx(
+                    out=w2_w[:, b, slots].rearrange("p t m -> p (t m)").bitcast(FP8X4),
+                    scales=w2_s[:, b, slots].rearrange("p t m -> p (t m)"),
+                    in_=rounded[:, slots].rearrange("p t m j -> p (t m j)"),
+                )
 
         nc.vector.tensor_copy(w1_s[:], w1_s_in[:].rearrange("p (b m t) -> p b t m", b=BLOCKS, t=PACK))
-        quantize_w2(0, "damp1")
-        for b in range(BLOCKS):
+        quantize_w2(0, PACK)
+
+        def deal_w1(lo, hi):
+            rows = slice(lo % PASS // PACK, (hi - 1) % PASS // PACK + 1)
             nc.vector.tensor_copy(
-                w1_w[:, b].rearrange("p t (m e) -> p t m e", e=2),
-                w1_w_in[:].rearrange("p (b m t e) -> p b t m e", b=BLOCKS, t=PACK, e=2)[:, b],
+                w1_w[:, lo // PASS].rearrange("p t (m e) -> p t m e", e=2)[:, :, rows],
+                w1_w_in[:, 2 * lo : 2 * hi].rearrange("p (m t e) -> p t m e", t=PACK, e=2),
             )
+
+        deal_w1(0, PASS)
         for lo in range(0, S, HALF):
             nc.vector.tensor_copy(
                 v_w[:, lo : lo + HALF], tab_w[:].bitcast(U32).indirect(entries(idx, lo, lo + HALF))
@@ -207,29 +220,34 @@ def tile_list_trie_leak_audit_kernel(
                 pages[b, t][:].indirect(entries(idx2, lo, hi)), h[:, t, lo:hi], wg[:, t, lo:hi], MULT
             )
 
-        damps = []
+        damps = {}
+
+        def damp_tile(b, t0, t1):
+            tile = work.tile([P, t1 - t0, M], F32, name="damp%d%d" % (b, t0), align_bytes=64)
+            for t in range(t0, t1):
+                damps[b, t] = tile[:, t - t0]
 
         def fetch_link(b, t):
-            nc.vector.tensor_copy(damps[b][:, t, :], pages[b, t][:].indirect(idx4[:]))
+            nc.vector.tensor_copy(damps[b, t], pages[b, t][:].indirect(idx4[:]))
 
         def damping(b, parts, tag, tag2=None):
             shape = [P, len(parts), parts[0][2] - parts[0][1]]
             size = work.tile(shape, F32, name="size", tag=tag, align_bytes=64)
             root = size if tag2 is None else work.tile(shape, F32, name="root", tag=tag2, align_bytes=64)
             for e, (t, lo, hi) in enumerate(parts):
-                nc.scalar.activation(size[:, e], damps[b][:, t, lo:hi], ACT.Abs)
+                nc.scalar.activation(size[:, e], damps[b, t][:, lo:hi], ACT.Abs)
             for e in range(len(parts)):
                 nc.scalar.activation(root[:, e], size[:, e], ACT.Abs_reciprocal_sqrt, bias=one[:])
             for e in range(len(parts)):
                 nc.scalar.activation(root[:, e], root[:, e], ACT.Square)
             for e, (t, lo, hi) in enumerate(parts):
-                nc.scalar.activation(damps[b][:, t, lo:hi], root[:, e], ACT.Copy, scale=gain_sb[:, b, t : t + 1])
+                nc.scalar.activation(damps[b, t][:, lo:hi], root[:, e], ACT.Copy, scale=gain_sb[:, b, t : t + 1])
 
         def fetch_nodes(b, lo, hi, tag):
             z = work.tile([P, PACK, hi - lo], F32, name="z", tag=tag, align_bytes=64)
             for t in range(PACK):
                 nc.vector.tensor_tensor(
-                    z[:, t], pages[b, t][:].indirect(entries(idx3, lo, hi)), damps[b][:, t, lo:hi], MULT
+                    z[:, t], pages[b, t][:].indirect(entries(idx3, lo, hi)), damps[b, t][:, lo:hi], MULT
                 )
             return z
 
@@ -257,16 +275,17 @@ def tile_list_trie_leak_audit_kernel(
             first_features(h0, q)
         for q in range(2):
             scatter(0, 0, h0, q * CHUNK, (q + 1) * CHUNK)
+            deal_w1(PASS + q * CHUNK, PASS + (q + 1) * CHUNK)
         features(0, 0, 0, HALF, h0, spare=4)
         scatter(0, 0, h0, HALF, S)
-        damps.append(work.tile([P, PACK, M], F32, name="damp0", align_bytes=64))
+        damp_tile(0, 0, PACK)
         features(1, 0, 1, 0, h0)
         scatter(0, 1, h0, 0, HALF)
         fetch_link(0, 0)
         features(2, 0, 1, HALF, h0)
         scatter(0, 1, h0, HALF, S)
         features(3, 0, 2, 0, h0)
-        quantize_w2(1, "rounded_w2")
+        quantize_w2(1, 2)
         fetch_link(0, 1)
         held = work.tile([P, 2, PACK, P], F32, name="held", tag="wide1", align_bytes=64)
         features(4, 0, 3, 0, h0, second=held[:, 0])
@@ -283,16 +302,17 @@ def tile_list_trie_leak_audit_kernel(
             for k in range(2):
                 first = None
                 if (t, k) == (last, 1):
-                    first = work.tile([P, PACK, P], F32, name="first", tag="damp1", align_bytes=64)
+                    first = work.tile([P, PACK, P], F32, name="first", tag="damp10", align_bytes=64)
                 features(2 * t + k + 1, 1, t, k * HALF, h1, first=first)
-        damps.append(work.tile([P, PACK, M], F32, name="damp1", align_bytes=64))
+        damp_tile(1, 0, 2)
         for t in range(last):
             scatter(1, t, h1, 0, S)
             if t > 0:
                 fetch_link(1, t - 1)
-        fetch_link(1, last - 1)
 
-        damping(0, [(0, 0, M), (1, 0, M)], "second0")
+        damping(0, [(0, 0, M), (1, 0, M)], "second0", "damp12")
+        damp_tile(1, 2, PACK)
+        fetch_link(1, last - 1)
         damping(0, [(2, 0, M), (3, 0, M)], "second0", "page13")
         load_page(1, last)
         damping(1, [(0, 0, M), (1, 0, M)], "second0")
@@ -303,7 +323,7 @@ def tile_list_trie_leak_audit_kernel(
         damping(1, [(last, 0, HALF), (last, HALF, M)], "rows0", "wide1")
         quantize_z(0, fetch_nodes(0, HALF, M, "rows1"), HALF, M, nc.scalar.copy, "rows0")
 
-        staged = work.tile([P, N // P, M], F32, name="staged", tag="damp0", align_bytes=64)
+        staged = work.tile([P, N // P, M], F32, name="staged", tag="damp00", align_bytes=64)
         out_rows = out.rearrange("(n p) m -> p n m", p=P)
         banks = []
         for i, (lo, hi) in enumerate(PIECES):

@@ -231,33 +231,32 @@ def tile_list_trie_leak_audit_kernel(
             nc.vector.tensor_copy(damps[b, t], pages[b, t][:].indirect(idx4[:]))
 
         def damping(b, parts, tag, tag2=None):
-            shape = [P, len(parts), parts[0][2] - parts[0][1]]
-            size = work.tile(shape, F32, name="size", tag=tag, align_bytes=64)
-            root = size if tag2 is None else work.tile(shape, F32, name="root", tag=tag2, align_bytes=64)
-            for e, (t, lo, hi) in enumerate(parts):
-                nc.scalar.activation(size[:, e], damps[b, t][:, lo:hi], ACT.Abs)
-            for e in range(len(parts)):
-                nc.scalar.activation(root[:, e], size[:, e], ACT.Abs_reciprocal_sqrt, bias=one[:])
-            for e in range(len(parts)):
-                nc.scalar.activation(root[:, e], root[:, e], ACT.Square)
-            for e, (t, lo, hi) in enumerate(parts):
-                nc.scalar.activation(damps[b, t][:, lo:hi], root[:, e], ACT.Copy, scale=gain_sb[:, b, t : t + 1])
+            total = sum(hi - lo for _, lo, hi in parts)
+            size = work.tile([P, total], F32, name="size", tag=tag, align_bytes=64)
+            root = size if tag2 is None else work.tile([P, total], F32, name="root", tag=tag2, align_bytes=64)
+            first = parts[0][2] - parts[0][1]
+            spans = (slice(0, first), slice(first, total))
+            for span, (t, lo, hi) in zip(spans, parts):
+                nc.scalar.activation(size[:, span], damps[b, t][:, lo:hi], ACT.Abs)
+            for span in spans:
+                nc.scalar.activation(root[:, span], size[:, span], ACT.Abs_reciprocal_sqrt, bias=one[:])
+            for span in spans:
+                nc.scalar.activation(root[:, span], root[:, span], ACT.Square)
+            for span, (t, lo, hi) in zip(spans, parts):
+                nc.scalar.activation(damps[b, t][:, lo:hi], root[:, span], ACT.Copy, scale=gain_sb[:, b, t : t + 1])
 
-        def fetch_nodes(b, lo, hi, tag):
-            z = work.tile([P, PACK, hi - lo], F32, name="z", tag=tag, align_bytes=64)
+        def fetch_nodes(b, lo, hi, z):
             for t in range(PACK):
                 nc.vector.tensor_tensor(
                     z[:, t], pages[b, t][:].indirect(entries(idx3, lo, hi)), damps[b, t][:, lo:hi], MULT
                 )
-            return z
 
-        def quantize_z(b, z, lo, hi, copy, tag, bufs=1):
-            rounded = work.tile([P, PACK * (hi - lo)], BF16, name="rounded", tag=tag, bufs=bufs, align_bytes=64)
+        def quantize_z(b, z, lo, hi, copy, rounded):
             copy(
-                rounded[:].rearrange("p (c i t) -> p c t i", i=4, t=PACK),
-                z[:].rearrange("p t (c i) -> p c t i", i=4),
+                rounded.rearrange("p (c i t) -> p c t i", i=4, t=PACK),
+                z.rearrange("p t (c i) -> p c t i", i=4),
             )
-            nc.vector.quantize_mx(out=z_w[:, b, lo:hi].bitcast(FP8X4), scales=z_s[:, b, lo:hi], in_=rounded[:])
+            nc.vector.quantize_mx(out=z_w[:, b, lo:hi].bitcast(FP8X4), scales=z_s[:, b, lo:hi], in_=rounded)
 
         def scores_pass(b, banks, lo, hi):
             share = N // P // len(banks)
@@ -315,36 +314,44 @@ def tile_list_trie_leak_audit_kernel(
         fetch_link(1, last - 1)
         damping(0, [(2, 0, M), (3, 0, M)], "second0", "page13")
         load_page(1, last)
-        damping(1, [(0, 0, M), (1, 0, M)], "second0")
-        damping(1, [(2, 0, HALF), (2, HALF, M)], "second0")
-        quantize_z(0, fetch_nodes(0, 0, HALF, "rows0"), 0, HALF, nc.scalar.copy, "second0")
+        damping(1, [(0, 0, M), (1, 0, HALF)], "second0")
+        damping(1, [(1, HALF, M), (2, 0, M)], "second0")
+        z = work.tile([P, PACK, HALF], F32, name="z", tag="rows0", align_bytes=64)
+        fetch_nodes(0, 0, HALF, z[:])
+        rounded = work.tile([P, PACK * HALF], BF16, name="rounded", tag="second0", align_bytes=64)
+        quantize_z(0, z[:], 0, HALF, nc.scalar.copy, rounded[:])
         scatter(1, last, h1, 0, S)
         fetch_link(1, last)
         damping(1, [(last, 0, HALF), (last, HALF, M)], "rows0", "wide1")
-        quantize_z(0, fetch_nodes(0, HALF, M, "rows1"), HALF, M, nc.scalar.copy, "rows0")
+        odd = work.tile([P, PACK, HALF], F32, name="odd", tag="rows1", align_bytes=64)
+        fetch_nodes(0, HALF, M, odd[:])
+        rounded = work.tile([P, 2, PACK * CHUNK], BF16, name="rounded", tag="rows0", align_bytes=64)
+        for k in range(2):
+            lo = HALF + k * CHUNK
+            quantize_z(0, odd[:, :, k * CHUNK : (k + 1) * CHUNK], lo, lo + CHUNK, nc.scalar.copy, rounded[:, k])
 
         staged = work.tile([P, N // P, M], F32, name="staged", tag="damp00", align_bytes=64)
         out_rows = out.rearrange("(n p) m -> p n m", p=P)
+        even = work.tile([P, PACK, CHUNK], F32, name="even", tag="wide0", align_bytes=64)
         banks = []
         for i, (lo, hi) in enumerate(PIECES):
-            count = 1 if i == len(PIECES) - 2 else 2
-            used = sum(map(len, banks))
-            banks.append([bank([P, N // P // count, hi - lo], (used + e) % 8, "scores") for e in range(count)])
+            banks.append([bank([P, 2, hi - lo], (2 * i + e) % 8, "scores") for e in range(2)])
 
         def finish(i):
             lo, hi = PIECES[i]
-            final = i == len(PIECES) - 1
             share = N // P // len(banks[i])
             for e, sums in enumerate(banks[i]):
                 rows = slice(e * share, (e + 1) * share)
-                copy = nc.vector.tensor_copy if final and e == 0 else nc.scalar.copy
+                copy = nc.vector.tensor_copy if hi - lo == P and e == 0 else nc.scalar.copy
                 copy(staged[:, rows, lo:hi], sums[:])
                 nc.sync.dma_start(out=out_rows[:, rows, lo:hi], in_=staged[:, rows, lo:hi])
 
         for i, (lo, hi) in enumerate(PIECES):
-            z = fetch_nodes(1, lo, hi, ("wide0", "rows1")[i % 2])
+            z = (even, odd)[i % 2][:, :, : hi - lo]
+            fetch_nodes(1, lo, hi, z)
             scores_pass(0, banks[i], lo, hi)
-            quantize_z(1, z, lo, hi, nc.vector.tensor_copy if hi - lo == P else nc.scalar.copy, "rounded", 2)
+            rounded = work.tile([P, PACK * (hi - lo)], BF16, name="rounded", tag="rounded", bufs=2, align_bytes=64)
+            quantize_z(1, z, lo, hi, nc.vector.tensor_copy if i == len(PIECES) - 1 else nc.scalar.copy, rounded[:])
             scores_pass(1, banks[i], lo, hi)
             if i > 0:
                 finish(i - 1)

@@ -251,10 +251,10 @@ def tile_list_trie_leak_audit_kernel(
                     z[:, t], pages[b, t][:].indirect(entries(idx3, lo, hi)), damps[b, t][:, lo:hi], MULT
                 )
 
-        def quantize_z(b, z, lo, hi, copy, rounded):
+        def quantize_z(b, z, lo, hi, copy, rounded, run=2):
             copy(
-                rounded.rearrange("p (c i t) -> p c t i", i=4, t=PACK),
-                z.rearrange("p t (c i) -> p c t i", i=4),
+                rounded.rearrange("p (c i t) -> p c t i", i=run, t=PACK),
+                z.rearrange("p t (c i) -> p c t i", i=run),
             )
             nc.vector.quantize_mx(out=z_w[:, b, lo:hi].bitcast(FP8X4), scales=z_s[:, b, lo:hi], in_=rounded)
 
@@ -351,7 +351,10 @@ def tile_list_trie_leak_audit_kernel(
             fetch_nodes(1, lo, hi, z)
             scores_pass(0, banks[i], lo, hi)
             rounded = work.tile([P, PACK * (hi - lo)], BF16, name="rounded", tag="rounded", bufs=2, align_bytes=64)
-            quantize_z(1, z, lo, hi, nc.vector.tensor_copy if i == len(PIECES) - 1 else nc.scalar.copy, rounded[:])
+            if i == len(PIECES) - 1:
+                quantize_z(1, z, lo, hi, nc.vector.tensor_copy, rounded[:], 4)
+            else:
+                quantize_z(1, z, lo, hi, nc.scalar.copy, rounded[:])
             scores_pass(1, banks[i], lo, hi)
             if i > 0:
                 finish(i - 1)

@@ -216,9 +216,8 @@ def tile_list_trie_leak_audit_kernel(
             nc.scalar.copy(h[:, t, lo : lo + HALF], turned[:].rearrange("p u j -> p (u j)"))
 
         def scatter(b, t, h, lo, hi):
-            nc.vector.tensor_tensor(
-                pages[b, t][:].indirect(entries(idx2, lo, hi)), h[:, t, lo:hi], wg[:, t, lo:hi], MULT
-            )
+            nc.vector.tensor_tensor(h[:, t, lo:hi], h[:, t, lo:hi], wg[:, t, lo:hi], MULT)
+            nc.vector.tensor_copy(pages[b, t][:].indirect(entries(idx2, lo, hi)), h[:, t, lo:hi])
 
         damps = {}
 

@@ -42,95 +42,241 @@ def tile_list_trie_leak_audit_kernel(
         work = ctx.enter_context(tc.tile_pool(name="work", bufs=1))
         psum = ctx.enter_context(tc.psum_pool(name="psum", bufs=1))
 
+        def scratch(shape, dtype, tag):
+            return work.tile(shape, dtype, name=tag, tag=tag, align_bytes=64)
+
+        def bank(shape, number):
+            return psum.tile(shape, F32, name="bank%d" % number, tag="bank%d" % number)
+
         idx = lists.tile([P, S // 16], U16)
         idx2 = lists.tile([P, S // 16], U16)
         idx3 = lists.tile([P, M // 16], U16)
         idx4 = lists.tile([P, M // 16], U16)
 
-        tab_w = keep.tile([P, T], I32, align_bytes=64)
-        tab_s = work.tile([P, T], U8, tag="page00", align_bytes=64)
+        tab_w = scratch([P, T], I32, "table")
+        tab_s = scratch([P, T], U8, "page0")
         v_w = keep.tile([P, S], U32, align_bytes=64)
         v_s_spread = keep.tile([P, S], U8, align_bytes=64)
         v_s = keep.tile([P, S], U8, align_bytes=64)
-        w1_w_in = keep.tile([P, 2 * H], U8)
-        w1_s_in = keep.tile([P, H], U8)
-        w1_w = keep.tile([P, BLOCKS, PACK, 2 * P], U8, align_bytes=64)
-        w1_s = keep.tile([P, BLOCKS, PACK, P], U8, align_bytes=64)
-        w2_w = keep.tile([P, BLOCKS, PACK, P], U32, align_bytes=64)
-        w2_s = keep.tile([P, BLOCKS, PACK, P], U8, align_bytes=64)
+        w1_w = keep.tile([P, 2 * H], U8, align_bytes=64)
+        w1_s = keep.tile([P, H], U8, align_bytes=64)
+        w2_w = keep.tile([P, H], U32, align_bytes=64)
+        w2_s = keep.tile([P, H], U8, align_bytes=64)
         w3_w = keep.tile([P, BLOCKS * N], I32, align_bytes=64)
         w3_s = keep.tile([P, BLOCKS * N], U8, align_bytes=64)
-        z_w = keep.tile([P, BLOCKS, M], U32, align_bytes=64)
-        z_s = keep.tile([P, BLOCKS, M], U8, align_bytes=64)
-        wg = keep.tile([P, PACK, S], F32)
-        gain_sb = keep.tile([P, BLOCKS, PACK], F32)
+        z_w = keep.tile([P, BLOCKS * M], U32, align_bytes=64)
+        z_s = keep.tile([P, BLOCKS * M], U8, align_bytes=64)
+        wg = keep.tile([P, S], F32)
+        wg_dealt = keep.tile([P, PACK, S], F32)
+        gains = [keep.tile([P, PACK], F32, name="gain%d" % b) for b in range(BLOCKS)]
         ident = keep.tile([P, P], F32)
         one = keep.tile([P, 1], F32)
 
         nc.vector.memset(tab_s[:].bitcast(I32), 0)
-        nc.gpsimd.memset(w1_s_in[:].bitcast(I32), 0)
+        nc.gpsimd.memset(w1_s[:].bitcast(I32), 0)
         nc.vector.memset(v_s[:].bitcast(I32), 0)
         nc.gpsimd.memset(w3_s[:].bitcast(I32), 0)
         nc.gpsimd.memset(one[:], 1.0)
         make_identity(nc, ident[:])
 
-        def load_w2(b):
-            raw = work.tile([P, PACK, PASS], F32, name="raw", tag="wide%d" % b, align_bytes=64)
-            nc.sync.dma_start(
-                out=raw[:], in_=w2.rearrange("(p j) c -> p j c", j=PACK)[:, :, b * PASS : (b + 1) * PASS]
-            )
+        def load_w2(lo, hi):
+            raw = scratch([P, PACK, hi - lo], F32, "raw%d" % lo)
+            nc.sync.dma_start(out=raw[:], in_=w2.rearrange("(p j) c -> p j c", j=PACK)[:, :, lo:hi])
             return raw
-
-        def load_wg(t0, t1, lo, hi):
-            rows = wgs.rearrange("(i t) c -> i t c", t=PACK)
-            for quadrant in (0, 2, 1, 3):
-                nc.sync.dma_start(
-                    out=wg[32 * quadrant : 32 * quadrant + 32, t0:t1, lo:hi], in_=rows[:, t0:t1, lo:hi]
-                )
 
         def load_w1(lo, hi):
             cols = slice(2 * lo, 2 * hi)
-            nc.sync.dma_start(out=w1_w_in[:, cols].bitcast(I32), in_=w1_words[0][:, cols].bitcast(I32))
+            nc.sync.dma_start(out=w1_w[:, cols].bitcast(I32), in_=w1_words[0][:, cols].bitcast(I32))
+
+        def load_wg(lo, hi):
+            nc.sync.dma_start(out=wg[:, lo:hi], in_=wgs[:, lo:hi])
+
+        def load_wg_dealt(t0, t1):
+            rows = wgs.rearrange("(i t) c -> i t c", t=PACK)
+            for quadrant in (0, 2, 1, 3):
+                nc.sync.dma_start(out=wg_dealt[32 * quadrant : 32 * quadrant + 32, t0:t1], in_=rows[:, t0:t1])
 
         pages = {}
 
-        def load_page(b, t):
-            pages[b, t] = work.tile([P, T2], F32, name="page%d%d" % (b, t), align_bytes=64)
-            nc.sync.dma_start(
-                out=pages[b, t][:], in_=page0.rearrange("(b p t) c -> b t p c", b=BLOCKS, t=PACK)[b, t]
+        def load_page(s):
+            pages[s] = scratch([P, T2], F32, "page%d" % s)
+            if s < PACK:
+                rows = page0[s * P : (s + 1) * P]
+            else:
+                rows = page0[PASS:].rearrange("(p t) c -> t p c", t=PACK)[s - PACK]
+            nc.sync.dma_start(out=pages[s][:], in_=rows)
+
+        def quantize_w2(raw, lo, hi, cuts=()):
+            rounded = scratch([P, PACK * (hi - lo)], BF16, "rounded_w2_%d" % lo)
+            for c0, c1 in zip((0,) + cuts, cuts + (hi - lo,)):
+                nc.scalar.copy(
+                    rounded[:, PACK * c0 : PACK * c1].rearrange("p (c i j) -> p c j i", i=2, j=PACK),
+                    raw[:, :, c0:c1].rearrange("p j (c i) -> p c j i", i=2),
+                )
+            nc.vector.quantize_mx(out=w2_w[:, lo:hi].bitcast(FP8X4), scales=w2_s[:, lo:hi], in_=rounded[:])
+
+        def weights(lo, hi):
+            return (
+                (w1_w[:, 2 * lo : 2 * hi].bitcast(FP4X4), w1_s[:, lo:hi]),
+                (w2_w[:, lo:hi].bitcast(FP8X4), w2_s[:, lo:hi]),
             )
 
+        def first_features(h, q):
+            cols = slice(q * CHUNK, (q + 1) * CHUNK)
+            sums = [bank([P, CHUNK], 2 * q + e) for e in range(2)]
+            for acc, (codes, scales) in reversed(list(zip(sums, weights(0, P)))):
+                nc.tensor.matmul_mx(
+                    out=acc[:], lhsT=codes, lhsT_scale=scales,
+                    rhs=v_w[:, cols].bitcast(FP8X4), rhs_scale=v_s[:, cols],
+                    start=True, stop=True,
+                )
+            second = scratch([P, CHUNK], F32, "second%d" % q)
+            nc.scalar.activation(second[:], sums[1][:], ACT.Tanh)
+            nc.vector.tensor_tensor(h[:, cols], sums[0][:], second[:], SUBTRACT)
+
+        def turn(unit, sums, view, h, tags, number):
+            tags = tags or ("first%d" % (unit % 2), "second%d" % (unit % 2))
+            first, second = [scratch([P, PACK, P], F32, tag) for tag in tags]
+            nc.scalar.activation(second[:], view(sums[1]), ACT.Tanh, scale=-1.0)
+            nc.scalar.copy(first[:], view(sums[0]))
+            turned = bank([P, PACK, P], number)
+            for e, term in enumerate((second, first)):
+                for u in range(PACK):
+                    nc.tensor.matmul(
+                        turned[:, u], term[:, u], ident[:], is_transpose=True,
+                        start=(e == 0 and u == 0), stop=(e == 1 and u == PACK - 1),
+                    )
+            nc.scalar.copy(h, turned[:])
+
+        def banks_of(unit):
+            return 2 * (unit % 2), 2 * (unit % 2) + 1, 4 + unit % 4
+
+        def features(unit, s, lo, h, tags=None, numbers=None):
+            numbers = numbers or banks_of(unit)
+            sums = [bank([P, PACK, P], number) for number in numbers[:2]]
+            for acc, (codes, scales) in reversed(list(zip(sums, weights(s * P, (s + 1) * P)))):
+                for u in range(PACK):
+                    cols = slice(lo + u * P, lo + (u + 1) * P)
+                    nc.tensor.matmul_mx(
+                        out=acc[:, u], lhsT=v_w[:, cols].bitcast(FP8X4), lhsT_scale=v_s[:, cols],
+                        rhs=codes, rhs_scale=scales, start=True, stop=True,
+                    )
+            turn(unit, sums, lambda acc: acc[:], h.rearrange("p (u j) -> p u j", u=PACK), tags, numbers[2])
+
+        def dealt_features(unit, lo, h, tags=None):
+            sums = [bank([P, PASS], number) for number in banks_of(unit)[:2]]
+            cols = slice(lo, lo + P)
+            for acc, (codes, scales) in reversed(list(zip(sums, weights(PASS, H)))):
+                nc.tensor.matmul_mx(
+                    out=acc[:], lhsT=v_w[:, cols].bitcast(FP8X4), lhsT_scale=v_s[:, cols],
+                    rhs=codes, rhs_scale=scales, start=True, stop=True,
+                )
+            turn(unit, sums, lambda acc: acc[:].rearrange("j (p t) -> j t p", t=PACK), h[:, :, cols], tags, banks_of(unit)[2])
+
+        def scatter(s, h, lo, hi):
+            factor = wg[:, lo:hi] if s < PACK else wg_dealt[:, s - PACK, lo:hi]
+            nc.vector.tensor_tensor(pages[s][:].indirect(entries(idx2, lo, hi)), h, factor, MULT)
+
+        damps = {}
+
+        def damp_tile(s0, s1, tag):
+            tile = scratch([P, s1 - s0, M], F32, tag)
+            for s in range(s0, s1):
+                damps[s] = tile[:, s - s0]
+
+        def fetch_link(s):
+            nc.vector.tensor_copy(damps[s], pages[s][:].indirect(idx4[:]))
+
+        def damping(parts, tags, last_tag=None):
+            values = [damps[s][:, lo:hi] for s, lo, hi in parts]
+            sizes = [scratch([P, hi - lo], F32, tag) for (s, lo, hi), tag in zip(parts, tags)]
+            roots = list(values)
+            if last_tag is not None:
+                roots[1] = scratch([P, parts[1][2] - parts[1][1]], F32, last_tag)[:]
+            for size, value in zip(sizes, values):
+                nc.scalar.activation(size[:], value, ACT.Abs)
+            for root, size in zip(roots, sizes):
+                nc.scalar.activation(root, size[:], ACT.Abs_reciprocal_sqrt, bias=one[:])
+            for root in roots:
+                nc.scalar.activation(root, root, ACT.Square)
+            for value, root, (s, lo, hi) in zip(values, roots, parts):
+                nc.scalar.activation(value, root, ACT.Copy, scale=gains[s // PACK][:, s % PACK : s % PACK + 1])
+
+        def fetch_nodes(b, lo, hi, z):
+            for t in range(PACK):
+                s = PACK * b + t
+                nc.vector.tensor_tensor(z[:, t], pages[s][:].indirect(entries(idx3, lo, hi)), damps[s][:, lo:hi], MULT)
+
+        def quantize_z(b, lo, hi, rounded):
+            cols = slice(b * M + lo, b * M + hi)
+            nc.vector.quantize_mx(out=z_w[:, cols].bitcast(FP8X4), scales=z_s[:, cols], in_=rounded)
+
+        def regroup(z):
+            units = HALF // P
+            lying = []
+            for u in range(units):
+                turned = bank([P, PACK, P], u)
+                for s in range(PACK):
+                    nc.tensor.transpose(turned[:, s], z[:, s, u * P : (u + 1) * P], ident[:])
+                rows = scratch([P, PASS], BF16, "lying%d" % u)
+                nc.scalar.copy(
+                    rows[:].rearrange("m (h p e) -> m h p e", h=2, e=2),
+                    turned[:].rearrange("m s i -> m (s i)").rearrange("m (p h e) -> m h p e", h=2, e=2),
+                )
+                lying.append(rows)
+            rounded = scratch([P, PACK * HALF], BF16, "rounded_w2_%d" % PASS)
+            words = rounded[:].bitcast(F32).rearrange("p (v u m h) -> p v u m h", u=2, m=P, h=2)
+            for v in range(units // 2):
+                back = bank([P, 2, 2, P], 4 + v)
+                for u in range(2):
+                    for h in range(2):
+                        pairs = lying[2 * v + u][:].bitcast(F32)[:, h * P : (h + 1) * P]
+                        nc.tensor.transpose(back[:, u, h], pairs, ident[:])
+                nc.scalar.copy(words[:, v], back[:].rearrange("p u h m -> p u m h"))
+            return rounded
+
+        def scores_pass(b, banks, lo, hi):
+            share = N // P // len(banks)
+            moving = slice(b * M + lo, b * M + hi)
+            for n in range(N // P):
+                cols = slice(b * N + n * P, b * N + (n + 1) * P)
+                nc.tensor.matmul_mx(
+                    out=banks[n // share][:, n % share],
+                    lhsT=w3_w[:, cols].bitcast(FP8X4), lhsT_scale=w3_s[:, cols],
+                    rhs=z_w[:, moving].bitcast(FP8X4), rhs_scale=z_s[:, moving],
+                    start=(b == 0 and n % share == 0), stop=(b == BLOCKS - 1 and n % share == share - 1),
+                )
+
         nc.sync.dma_start(idx[:], offs)
-        w2_raw = [load_w2(0)]
+        raw0 = load_w2(0, P)
         nc.sync.dma_start(out=tab_s[0:P:8, :].bitcast(I32), in_=tab_scales[0].bitcast(I32))
         for r in range(4):
-            nc.sync.dma_start(out=w1_s_in[r:P:32, :].bitcast(I32), in_=w1_scales[0, r:16:4, :].bitcast(I32))
-        load_w1(0, PASS)
+            nc.sync.dma_start(out=w1_s[r:P:32, :].bitcast(I32), in_=w1_scales[0, r:16:4, :].bitcast(I32))
         nc.sync.dma_start(out=tab_w[:], in_=tab_words[0].rearrange("p n t -> p (n t)").bitcast(I32))
+        load_w1(0, P)
         nc.vector.tensor_copy(v_s_spread[:], tab_s[:].indirect(idx[:]))
         for r in range(4):
             nc.sync.dma_start(out=v_s[r:P:32, :].bitcast(I32), in_=v_s_spread[8 * r : P : 32, :].bitcast(I32))
-        load_page(0, 0)
+        load_page(0)
         nc.sync.dma_start(idx2[:], offs2)
-        load_wg(0, 1, 0, CHUNK)
-        load_w1(PASS, PASS + CHUNK)
-        load_wg(0, 1, CHUNK, HALF)
-        load_w1(PASS + CHUNK, H)
-        load_wg(0, 1, HALF, S)
-        load_page(0, 1)
-        load_wg(1, 2, 0, HALF)
+        load_wg(0, CHUNK)
+        raw1 = load_w2(P, 2 * P)
+        load_w1(P, H)
+        load_wg(CHUNK, HALF)
+        raw2 = load_w2(2 * P, PASS)
+        load_wg(HALF, S)
+        load_page(1)
+        raw4 = load_w2(PASS, H)
         nc.sync.dma_start(idx4[:], offs4)
-        w2_raw.append(load_w2(1))
-        load_wg(1, 2, HALF, S)
-        load_page(0, 2)
-        load_wg(2, 3, 0, HALF)
-        load_page(0, 3)
-        load_wg(3, 4, 0, HALF)
-        load_wg(2, 4, HALF, S)
-        for t in range(PACK - 1):
-            load_page(1, t)
+        for s in range(2, 6):
+            load_page(s)
+        load_wg_dealt(0, 2)
+        load_page(6)
+        load_wg_dealt(2, 4)
         nc.sync.dma_start(idx3[:], offs3)
-        nc.sync.dma_start(out=gain_sb[:], in_=gain.rearrange("(b p t) -> p b t", b=BLOCKS, t=PACK))
+        with nc.allow_non_contiguous_dma(reason="one gain a partition and slice"):
+            nc.sync.dma_start(out=gains[0][:], in_=gain[:PASS].rearrange("(s p) -> p s", p=P))
+        nc.sync.dma_start(out=gains[1][:], in_=gain[PASS:].rearrange("(p t) -> p t", t=PACK))
         for b in range(BLOCKS):
             nc.sync.dma_start(
                 out=w3_w[:, b * N : (b + 1) * N],
@@ -142,199 +288,72 @@ def tile_list_trie_leak_audit_kernel(
                 in_=w3_scales[:, 4 * quadrant : 4 * quadrant + 4, :].bitcast(I32).rearrange("b r n -> r b n"),
             )
 
-        def quantize_w2(b, span):
-            rounded = work.tile([P, PACK, P, PACK], BF16, name="rounded_w2", align_bytes=64)
-            for t in range(0, PACK, span):
-                slots = slice(t, t + span)
-                nc.scalar.copy(
-                    rounded[:, slots].rearrange("p t m j -> p m j t"),
-                    w2_raw[b][:].rearrange("p j (m t) -> p m j t", t=PACK)[:, :, :, slots],
-                )
-                nc.vector.quantize_mx(
-                    out=w2_w[:, b, slots].rearrange("p t m -> p (t m)").bitcast(FP8X4),
-                    scales=w2_s[:, b, slots].rearrange("p t m -> p (t m)"),
-                    in_=rounded[:, slots].rearrange("p t m j -> p (t m j)"),
-                )
-
-        nc.vector.tensor_copy(w1_s[:], w1_s_in[:].rearrange("p (b m t) -> p b t m", b=BLOCKS, t=PACK))
-        quantize_w2(0, PACK)
-
-        def deal_w1(lo, hi):
-            rows = slice(lo % PASS // PACK, (hi - 1) % PASS // PACK + 1)
-            nc.vector.tensor_copy(
-                w1_w[:, lo // PASS].rearrange("p t (m e) -> p t m e", e=2)[:, :, rows],
-                w1_w_in[:, 2 * lo : 2 * hi].rearrange("p (m t e) -> p t m e", t=PACK, e=2),
-            )
-
-        deal_w1(0, PASS)
-        for lo in range(0, S, HALF):
-            nc.vector.tensor_copy(
-                v_w[:, lo : lo + HALF], tab_w[:].bitcast(U32).indirect(entries(idx, lo, lo + HALF))
-            )
-
-        def weights(b, t):
-            return (
-                (w1_w[:, b, t].bitcast(FP4X4), w1_s[:, b, t]),
-                (w2_w[:, b, t].bitcast(FP8X4), w2_s[:, b, t]),
-            )
-
-        def bank(shape, number, name):
-            return psum.tile(shape, F32, name=name, tag="bank%d" % number)
-
-        def first_features(h, q):
-            cols = slice(q * CHUNK, (q + 1) * CHUNK)
-            sums = [bank([P, CHUNK], 2 * q + e, "sums") for e in range(2)]
-            for acc, (codes, scales) in reversed(list(zip(sums, weights(0, 0)))):
-                nc.tensor.matmul_mx(
-                    out=acc[:], lhsT=codes, lhsT_scale=scales,
-                    rhs=v_w[:, cols].bitcast(FP8X4), rhs_scale=v_s[:, cols],
-                    start=True, stop=True,
-                )
-            second = work.tile([P, CHUNK], F32, name="second", tag="second%d" % q, align_bytes=64)
-            nc.scalar.activation(second[:], sums[1][:], ACT.Tanh)
-            nc.vector.tensor_tensor(h[:, 0, cols], sums[0][:], second[:], SUBTRACT)
-
-        def features(unit, b, t, lo, h, first=None, second=None, spare=0):
-            sums = [bank([P, PACK, P], spare + 2 * (unit % 2) + e, "sums") for e in range(2)]
-            for acc, (codes, scales) in zip(sums, weights(b, t)):
-                for u in range(PACK):
-                    cols = slice(lo + u * P, lo + (u + 1) * P)
-                    nc.tensor.matmul_mx(
-                        out=acc[:, u], lhsT=v_w[:, cols].bitcast(FP8X4), lhsT_scale=v_s[:, cols],
-                        rhs=codes, rhs_scale=scales, start=True, stop=True,
-                    )
-            if first is None:
-                first = work.tile([P, PACK, P], F32, name="first", tag="first", bufs=2)
-            if second is None:
-                second = work.tile([P, PACK, P], F32, name="second", tag="second%d" % (unit % 2), align_bytes=64)
-            nc.scalar.copy(first[:], sums[0][:])
-            nc.scalar.activation(second[:], sums[1][:], ACT.Tanh, scale=-1.0)
-            turned = bank([P, PACK, P], (4 + spare + unit % 4) % 8, "turned")
-            for u in range(PACK):
-                nc.tensor.matmul(turned[:, u], second[:, u], ident[:], start=True, stop=False, is_transpose=True)
-                nc.tensor.matmul(turned[:, u], first[:, u], ident[:], start=False, stop=True, is_transpose=True)
-            nc.scalar.copy(h[:, t, lo : lo + HALF], turned[:].rearrange("p u j -> p (u j)"))
-
-        def scatter(b, t, h, lo, hi):
-            nc.vector.tensor_tensor(h[:, t, lo:hi], h[:, t, lo:hi], wg[:, t, lo:hi], MULT)
-            nc.vector.tensor_copy(pages[b, t][:].indirect(entries(idx2, lo, hi)), h[:, t, lo:hi])
-
-        damps = {}
-
-        def damp_tile(b, t0, t1):
-            tile = work.tile([P, t1 - t0, M], F32, name="damp%d%d" % (b, t0), align_bytes=64)
-            for t in range(t0, t1):
-                damps[b, t] = tile[:, t - t0]
-
-        def fetch_link(b, t):
-            nc.vector.tensor_copy(damps[b, t], pages[b, t][:].indirect(idx4[:]))
-
-        def damping(b, parts, tag, tag2=None):
-            total = sum(hi - lo for _, lo, hi in parts)
-            size = work.tile([P, total], F32, name="size", tag=tag, align_bytes=64)
-            root = size if tag2 is None else work.tile([P, total], F32, name="root", tag=tag2, align_bytes=64)
-            first = parts[0][2] - parts[0][1]
-            spans = (slice(0, first), slice(first, total))
-            for span, (t, lo, hi) in zip(spans, parts):
-                nc.scalar.activation(size[:, span], damps[b, t][:, lo:hi], ACT.Abs)
-            for span in spans:
-                nc.scalar.activation(root[:, span], size[:, span], ACT.Abs_reciprocal_sqrt, bias=one[:])
-            for span in spans:
-                nc.scalar.activation(root[:, span], root[:, span], ACT.Square)
-            for span, (t, lo, hi) in zip(spans, parts):
-                nc.scalar.activation(damps[b, t][:, lo:hi], root[:, span], ACT.Copy, scale=gain_sb[:, b, t : t + 1])
-
-        def fetch_nodes(b, lo, hi, z):
-            for t in range(PACK):
-                nc.vector.tensor_tensor(
-                    z[:, t], pages[b, t][:].indirect(entries(idx3, lo, hi)), damps[b, t][:, lo:hi], MULT
-                )
-
-        def quantize_z(b, z, lo, hi, copy, rounded, run=2):
-            copy(
-                rounded.rearrange("p (c i t) -> p c t i", i=run, t=PACK),
-                z.rearrange("p t (c i) -> p c t i", i=run),
-            )
-            nc.vector.quantize_mx(out=z_w[:, b, lo:hi].bitcast(FP8X4), scales=z_s[:, b, lo:hi], in_=rounded)
-
-        def scores_pass(b, banks, lo, hi):
-            share = N // P // len(banks)
-            for n in range(N // P):
-                cols = slice(b * N + n * P, b * N + (n + 1) * P)
-                nc.tensor.matmul_mx(
-                    out=banks[n // share][:, n % share],
-                    lhsT=w3_w[:, cols].bitcast(FP8X4), lhsT_scale=w3_s[:, cols],
-                    rhs=z_w[:, b, lo:hi].bitcast(FP8X4), rhs_scale=z_s[:, b, lo:hi],
-                    start=(b == 0 and n % share == 0), stop=(b == BLOCKS - 1 and n % share == share - 1),
-                )
-
-        h0 = work.tile([P, PACK, S], F32, name="h0", tag="rows0", align_bytes=64)
+        quantize_w2(raw0, 0, P)
+        for lo, hi in ((0, CHUNK), (CHUNK, HALF), (HALF, S)):
+            nc.vector.tensor_copy(v_w[:, lo:hi], tab_w[:].bitcast(U32).indirect(entries(idx, lo, hi)))
+        opening = scratch([P, HALF], F32, "opening")
         for q in range(2):
-            first_features(h0, q)
-        for q in range(2):
-            scatter(0, 0, h0, q * CHUNK, (q + 1) * CHUNK)
-            deal_w1(PASS + q * CHUNK, PASS + (q + 1) * CHUNK)
-        features(0, 0, 0, HALF, h0, spare=4)
-        scatter(0, 0, h0, HALF, S)
-        damp_tile(0, 0, PACK)
-        features(1, 0, 1, 0, h0)
-        scatter(0, 1, h0, 0, HALF)
-        fetch_link(0, 0)
-        features(2, 0, 1, HALF, h0)
-        scatter(0, 1, h0, HALF, S)
-        features(3, 0, 2, 0, h0)
-        quantize_w2(1, 2)
-        fetch_link(0, 1)
-        held = work.tile([P, 2, PACK, P], F32, name="held", tag="wide1", align_bytes=64)
-        features(4, 0, 3, 0, h0, second=held[:, 0])
-        features(5, 0, 2, HALF, h0, second=held[:, 1])
-        features(6, 0, 3, HALF, h0)
-        for lo in range(0, S, HALF):
-            for t in range(2, PACK):
-                scatter(0, t, h0, lo, lo + HALF)
-        for t in range(2, PACK):
-            fetch_link(0, t)
-        h1 = work.tile([P, PACK, S], F32, name="h1", tag="rows1", align_bytes=64)
-        last = PACK - 1
-        for t in range(PACK):
-            for k in range(2):
-                first = None
-                if (t, k) == (last, 1):
-                    first = work.tile([P, PACK, P], F32, name="first", tag="damp10", align_bytes=64)
-                features(2 * t + k + 1, 1, t, k * HALF, h1, first=first)
-        damp_tile(1, 0, 2)
-        for t in range(last):
-            scatter(1, t, h1, 0, S)
-            if t > 0:
-                fetch_link(1, t - 1)
-
-        damping(0, [(0, 0, M), (1, 0, M)], "second0", "damp12")
-        damp_tile(1, 2, PACK)
-        fetch_link(1, last - 1)
-        damping(0, [(2, 0, M), (3, 0, M)], "second0", "page13")
-        load_page(1, last)
-        damping(1, [(0, 0, M), (1, 0, HALF)], "second0")
-        damping(1, [(1, HALF, M), (2, 0, M)], "second0")
-        z = work.tile([P, PACK, HALF], F32, name="z", tag="rows0", align_bytes=64)
-        fetch_nodes(0, 0, HALF, z[:])
-        rounded = work.tile([P, PACK * HALF], BF16, name="rounded", tag="second0", align_bytes=64)
-        quantize_z(0, z[:], 0, HALF, nc.scalar.copy, rounded[:])
-        scatter(1, last, h1, 0, S)
-        fetch_link(1, last)
-        damping(1, [(last, 0, HALF), (last, HALF, M)], "rows0", "wide1")
-        odd = work.tile([P, PACK, HALF], F32, name="odd", tag="rows1", align_bytes=64)
-        fetch_nodes(0, HALF, M, odd[:])
-        rounded = work.tile([P, 2, PACK * CHUNK], BF16, name="rounded", tag="rows0", align_bytes=64)
+            first_features(opening, q)
+        scatter(0, opening[:, :CHUNK], 0, CHUNK)
+        quantize_w2(raw1, P, 2 * P)
+        scatter(0, opening[:, CHUNK:], CHUNK, HALF)
+        rest = scratch([P, HALF], F32, "raw%d" % P)
+        features(0, 0, HALF, rest[:], numbers=(4, 5, 0))
+        scatter(0, rest[:], HALF, S)
+        h0 = scratch([P, PACK - 1, S], F32, "rows")
+        features(1, 1, 0, h0[:, 0, :HALF])
+        features(2, 1, HALF, h0[:, 0, HALF:], tags=("rounded_w2_%d" % PASS, "second0"))
+        quantize_w2(raw2, 2 * P, PASS)
+        scatter(1, h0[:, 0], 0, S)
+        quantize_w2(raw4, PASS, H, cuts=(P,))
+        features(3, 2, 0, h0[:, 1, :HALF], numbers=(7, 6, 2))
+        damp_tile(0, 2, "raw%d" % PASS)
+        for s in range(2):
+            fetch_link(s)
+        features(4, 2, HALF, h0[:, 1, HALF:])
+        scatter(2, h0[:, 1], 0, S)
         for k in range(2):
-            lo = HALF + k * CHUNK
-            quantize_z(0, odd[:, :, k * CHUNK : (k + 1) * CHUNK], lo, lo + CHUNK, nc.scalar.copy, rounded[:, k])
+            features(5 + k, 3, k * HALF, h0[:, 2, k * HALF : (k + 1) * HALF])
+        scatter(3, h0[:, 2], 0, S)
+        h1 = scratch([P, PACK, S], F32, "table")
+        held = {3: ("first0", "damp2"), 7: ("size0", "size1")}
+        for u in range(S // P):
+            dealt_features(u + 7, u * P, h1, held.get(u))
+        damp_tile(2, PACK, "damp2")
+        for s in range(2, PACK):
+            fetch_link(s)
+        for lo in range(0, S, HALF):
+            for s in range(4, 6):
+                scatter(s, h1[:, s - PACK, lo : lo + HALF], lo, lo + HALF)
+        damp_tile(4, 6, "damp4")
+        for s in range(4, 6):
+            fetch_link(s)
+        scatter(6, h1[:, 2], 0, S)
 
-        staged = work.tile([P, N // P, M], F32, name="staged", tag="damp00", align_bytes=64)
+        damping([(0, 0, M), (1, 0, M)], ("size0", "size1"))
+        damping([(2, 0, M), (3, 0, M)], ("size0", "size1"))
+        early = scratch([P, PACK, HALF], F32, "rows")
+        fetch_nodes(0, 0, HALF, early[:])
+        damping([(4, 0, M), (5, 0, M)], ("size0", "page7"))
+        damp_tile(6, 7, "size0")
+        fetch_link(6)
+        load_page(7)
+        scatter(7, h1[:, 3], 0, S)
+        quantize_z(0, 0, HALF, regroup(early[:])[:])
+        damping([(6, 0, HALF), (6, HALF, M)], ("size1", "late"))
+        damp_tile(7, 8, "size1")
+        fetch_link(7)
+        late = scratch([P, PACK, HALF], F32, "late")
+        fetch_nodes(0, HALF, M, late[:])
+        damping([(7, 0, HALF), (7, HALF, M)], ("even", "rows"), "odd")
+        late_rounded = regroup(late[:])
+
+        staged = scratch([P, N // P, M], F32, "table")
         out_rows = out.rearrange("(n p) m -> p n m", p=P)
-        even = work.tile([P, PACK, CHUNK], F32, name="even", tag="wide0", align_bytes=64)
+        pair = [scratch([P, PACK, CHUNK], F32, tag) for tag in ("even", "odd")]
         banks = []
         for i, (lo, hi) in enumerate(PIECES):
-            banks.append([bank([P, 2, hi - lo], (2 * i + e) % 8, "scores") for e in range(2)])
+            banks.append([bank([P, 2, hi - lo], (2 * i + 6 + e) % 8) for e in range(2)])
 
         def finish(i):
             lo, hi = PIECES[i]
@@ -346,14 +365,19 @@ def tile_list_trie_leak_audit_kernel(
                 nc.sync.dma_start(out=out_rows[:, rows, lo:hi], in_=staged[:, rows, lo:hi])
 
         for i, (lo, hi) in enumerate(PIECES):
-            z = (even, odd)[i % 2][:, :, : hi - lo]
+            z = pair[i % 2][:, :, : hi - lo]
             fetch_nodes(1, lo, hi, z)
+            if i == 1:
+                quantize_z(0, HALF, M, late_rounded[:])
             scores_pass(0, banks[i], lo, hi)
             rounded = work.tile([P, PACK * (hi - lo)], BF16, name="rounded", tag="rounded", bufs=2, align_bytes=64)
-            if i == len(PIECES) - 1:
-                quantize_z(1, z, lo, hi, nc.vector.tensor_copy, rounded[:], 4)
-            else:
-                quantize_z(1, z, lo, hi, nc.scalar.copy, rounded[:])
+            last = i == len(PIECES) - 1
+            copy, run = (nc.vector.tensor_copy, 4) if last else (nc.scalar.copy, 2)
+            copy(
+                rounded[:].rearrange("p (c i t) -> p c t i", i=run, t=PACK),
+                z.rearrange("p t (c i) -> p c t i", i=run),
+            )
+            quantize_z(1, lo, hi, rounded[:])
             scores_pass(1, banks[i], lo, hi)
             if i > 0:
                 finish(i - 1)

@@ -106,8 +106,8 @@ def tile_list_trie_leak_audit_kernel(
                 rows = page0[PASS:].rearrange("(p t) c -> t p c", t=PACK)[s - PACK]
             nc.sync.dma_start(out=pages[s][:], in_=rows)
 
-        def quantize_w2(raw, lo, hi, cuts=()):
-            rounded = scratch([P, PACK * (hi - lo)], BF16, "rounded_w2_%d" % lo)
+        def quantize_w2(raw, lo, hi, tag, cuts=()):
+            rounded = scratch([P, PACK * (hi - lo)], BF16, tag)
             for c0, c1 in zip((0,) + cuts, cuts + (hi - lo,)):
                 nc.scalar.copy(
                     rounded[:, PACK * c0 : PACK * c1].rearrange("p (c i j) -> p c j i", i=2, j=PACK),
@@ -134,11 +134,16 @@ def tile_list_trie_leak_audit_kernel(
             nc.scalar.activation(second[:], sums[1][:], ACT.Tanh)
             nc.vector.tensor_tensor(h[:, cols], sums[0][:], second[:], SUBTRACT)
 
-        def turn(unit, sums, view, h, tags, number):
-            tags = tags or ("first%d" % (unit % 2), "second%d" % (unit % 2))
-            first, second = [scratch([P, PACK, P], F32, tag) for tag in tags]
-            nc.scalar.activation(second[:], view(sums[1]), ACT.Tanh, scale=-1.0)
-            nc.scalar.copy(first[:], view(sums[0]))
+        def terms_on(tags):
+            return [scratch([P, PACK, P], F32, tag)[:] for tag in tags]
+
+        def turn(unit, sums, view, h, terms, number):
+            first, second = terms or terms_on(("first%d" % (unit % 2), "second%d" % (unit % 2)))
+            nc.scalar.activation(second, view(sums[1]), ACT.Tanh, scale=-1.0)
+            nc.scalar.copy(first, view(sums[0]))
+            return first, second, h, number
+
+        def turn_back(first, second, h, number):
             turned = bank([P, PACK, P], number)
             for e, term in enumerate((second, first)):
                 for u in range(PACK):
@@ -151,7 +156,7 @@ def tile_list_trie_leak_audit_kernel(
         def banks_of(unit):
             return 2 * (unit % 2), 2 * (unit % 2) + 1, 4 + unit % 4
 
-        def features(unit, s, lo, h, tags=None, numbers=None):
+        def features(unit, s, lo, h, terms=None, numbers=None):
             numbers = numbers or banks_of(unit)
             sums = [bank([P, PACK, P], number) for number in numbers[:2]]
             for acc, (codes, scales) in reversed(list(zip(sums, weights(s * P, (s + 1) * P)))):
@@ -161,9 +166,9 @@ def tile_list_trie_leak_audit_kernel(
                         out=acc[:, u], lhsT=v_w[:, cols].bitcast(FP8X4), lhsT_scale=v_s[:, cols],
                         rhs=codes, rhs_scale=scales, start=True, stop=True,
                     )
-            turn(unit, sums, lambda acc: acc[:], h.rearrange("p (u j) -> p u j", u=PACK), tags, numbers[2])
+            return turn(unit, sums, lambda acc: acc[:], h.rearrange("p (u j) -> p u j", u=PACK), terms, numbers[2])
 
-        def dealt_features(unit, lo, h, tags=None):
+        def dealt_features(unit, lo, h, terms=None):
             sums = [bank([P, PASS], number) for number in banks_of(unit)[:2]]
             cols = slice(lo, lo + P)
             for acc, (codes, scales) in reversed(list(zip(sums, weights(PASS, H)))):
@@ -171,7 +176,7 @@ def tile_list_trie_leak_audit_kernel(
                     out=acc[:], lhsT=v_w[:, cols].bitcast(FP8X4), lhsT_scale=v_s[:, cols],
                     rhs=codes, rhs_scale=scales, start=True, stop=True,
                 )
-            turn(unit, sums, lambda acc: acc[:].rearrange("j (p t) -> j t p", t=PACK), h[:, :, cols], tags, banks_of(unit)[2])
+            return turn(unit, sums, lambda acc: acc[:].rearrange("j (p t) -> j t p", t=PACK), h[:, :, cols], terms, banks_of(unit)[2])
 
         def scatter(s, h, lo, hi):
             factor = wg[:, lo:hi] if s < PACK else wg_dealt[:, s - PACK, lo:hi]
@@ -184,54 +189,49 @@ def tile_list_trie_leak_audit_kernel(
             for s in range(s0, s1):
                 damps[s] = tile[:, s - s0]
 
-        def fetch_link(s):
-            nc.vector.tensor_copy(damps[s], pages[s][:].indirect(idx4[:]))
+        def fetch_link(s, lo=0, hi=M):
+            nc.vector.tensor_copy(damps[s][:, lo:hi], pages[s][:].indirect(entries(idx4, lo, hi)))
 
         def damping(parts, tags, last_tag=None):
             values = [damps[s][:, lo:hi] for s, lo, hi in parts]
-            sizes = [scratch([P, hi - lo], F32, tag) for (s, lo, hi), tag in zip(parts, tags)]
+            sizes = [scratch([P, hi - lo], F32, tag)[:] for (s, lo, hi), tag in zip(parts, tags)]
             roots = list(values)
             if last_tag is not None:
                 roots[1] = scratch([P, parts[1][2] - parts[1][1]], F32, last_tag)[:]
             for size, value in zip(sizes, values):
-                nc.scalar.activation(size[:], value, ACT.Abs)
+                nc.scalar.activation(size, value, ACT.Abs)
             for root, size in zip(roots, sizes):
-                nc.scalar.activation(root, size[:], ACT.Abs_reciprocal_sqrt, bias=one[:])
+                nc.scalar.activation(root, size, ACT.Abs_reciprocal_sqrt, bias=one[:])
             for root in roots:
                 nc.scalar.activation(root, root, ACT.Square)
             for value, root, (s, lo, hi) in zip(values, roots, parts):
                 nc.scalar.activation(value, root, ACT.Copy, scale=gains[s // PACK][:, s % PACK : s % PACK + 1])
 
-        def fetch_nodes(b, lo, hi, z):
-            for t in range(PACK):
-                s = PACK * b + t
-                nc.vector.tensor_tensor(z[:, t], pages[s][:].indirect(entries(idx3, lo, hi)), damps[s][:, lo:hi], MULT)
+        def fetch_nodes(s, lo, hi, z):
+            nc.vector.tensor_tensor(z, pages[s][:].indirect(entries(idx3, lo, hi)), damps[s][:, lo:hi], MULT)
 
         def quantize_z(b, lo, hi, rounded):
             cols = slice(b * M + lo, b * M + hi)
             nc.vector.quantize_mx(out=z_w[:, cols].bitcast(FP8X4), scales=z_s[:, cols], in_=rounded)
 
-        def regroup(z):
-            units = HALF // P
-            lying = []
-            for u in range(units):
-                turned = bank([P, PACK, P], u)
-                for s in range(PACK):
-                    nc.tensor.transpose(turned[:, s], z[:, s, u * P : (u + 1) * P], ident[:])
-                rows = scratch([P, PASS], BF16, "lying%d" % u)
-                nc.scalar.copy(
-                    rows[:].rearrange("m (h p e) -> m h p e", h=2, e=2),
-                    turned[:].rearrange("m s i -> m (s i)").rearrange("m (p h e) -> m h p e", h=2, e=2),
-                )
-                lying.append(rows)
-            rounded = scratch([P, PACK * HALF], BF16, "rounded_w2_%d" % PASS)
+        def lay_down(z, s, half, lying):
+            turned = bank([P, PACK, P], s)
+            for u in range(PACK):
+                nc.tensor.transpose(turned[:, u], z[:, u * P : (u + 1) * P], ident[:])
+            nc.scalar.copy(
+                lying[half][:].rearrange("m (u h s p e) -> m s u h p e", u=PACK, h=2, s=PACK, e=2)[:, s],
+                turned[:].rearrange("m u (p h e) -> m u h p e", h=2, e=2),
+            )
+
+        def stand_up(lying, tag):
+            pairs = lying[:].bitcast(F32).rearrange("m (u h p) -> m u h p", u=PACK, h=2)
+            rounded = scratch([P, PACK * HALF], BF16, tag)
             words = rounded[:].bitcast(F32).rearrange("p (v u m h) -> p v u m h", u=2, m=P, h=2)
-            for v in range(units // 2):
+            for v in range(2):
                 back = bank([P, 2, 2, P], 4 + v)
                 for u in range(2):
                     for h in range(2):
-                        pairs = lying[2 * v + u][:].bitcast(F32)[:, h * P : (h + 1) * P]
-                        nc.tensor.transpose(back[:, u, h], pairs, ident[:])
+                        nc.tensor.transpose(back[:, u, h], pairs[:, 2 * v + u, h], ident[:])
                 nc.scalar.copy(words[:, v], back[:].rearrange("p u h m -> p u m h"))
             return rounded
 
@@ -253,30 +253,30 @@ def tile_list_trie_leak_audit_kernel(
         for r in range(4):
             nc.sync.dma_start(out=w1_s[r:P:32, :].bitcast(I32), in_=w1_scales[0, r:16:4, :].bitcast(I32))
         nc.sync.dma_start(out=tab_w[:], in_=tab_words[0].rearrange("p n t -> p (n t)").bitcast(I32))
-        load_w1(0, P)
+        load_w1(0, 2 * P)
         nc.vector.tensor_copy(v_s_spread[:], tab_s[:].indirect(idx[:]))
         for r in range(4):
             nc.sync.dma_start(out=v_s[r:P:32, :].bitcast(I32), in_=v_s_spread[8 * r : P : 32, :].bitcast(I32))
+        raw1 = load_w2(P, 2 * P)
         load_page(0)
         nc.sync.dma_start(idx2[:], offs2)
-        load_wg(0, CHUNK)
-        raw1 = load_w2(P, 2 * P)
-        load_w1(P, H)
-        load_wg(CHUNK, HALF)
+        load_wg(0, HALF)
         raw2 = load_w2(2 * P, PASS)
         load_wg(HALF, S)
         load_page(1)
+        load_w1(2 * P, H)
         raw4 = load_w2(PASS, H)
         nc.sync.dma_start(idx4[:], offs4)
-        for s in range(2, 6):
-            load_page(s)
-        load_wg_dealt(0, 2)
-        load_page(6)
-        load_wg_dealt(2, 4)
         nc.sync.dma_start(idx3[:], offs3)
         with nc.allow_non_contiguous_dma(reason="one gain a partition and slice"):
             nc.sync.dma_start(out=gains[0][:], in_=gain[:PASS].rearrange("(s p) -> p s", p=P))
         nc.sync.dma_start(out=gains[1][:], in_=gain[PASS:].rearrange("(p t) -> p t", t=PACK))
+        for s in range(2, 6):
+            load_page(s)
+        load_wg_dealt(0, 2)
+        load_page(6)
+        load_wg_dealt(2, 3)
+        load_wg_dealt(3, 4)
         for b in range(BLOCKS):
             nc.sync.dma_start(
                 out=w3_w[:, b * N : (b + 1) * N],
@@ -288,37 +288,46 @@ def tile_list_trie_leak_audit_kernel(
                 in_=w3_scales[:, 4 * quadrant : 4 * quadrant + 4, :].bitcast(I32).rearrange("b r n -> r b n"),
             )
 
-        quantize_w2(raw0, 0, P)
+        quantize_w2(raw0, 0, P, "rounded0")
         for lo, hi in ((0, CHUNK), (CHUNK, HALF), (HALF, S)):
             nc.vector.tensor_copy(v_w[:, lo:hi], tab_w[:].bitcast(U32).indirect(entries(idx, lo, hi)))
         opening = scratch([P, HALF], F32, "opening")
         for q in range(2):
             first_features(opening, q)
-        scatter(0, opening[:, :CHUNK], 0, CHUNK)
-        quantize_w2(raw1, P, 2 * P)
-        scatter(0, opening[:, CHUNK:], CHUNK, HALF)
-        rest = scratch([P, HALF], F32, "raw%d" % P)
-        features(0, 0, HALF, rest[:], numbers=(4, 5, 0))
-        scatter(0, rest[:], HALF, S)
+        quantize_w2(raw1, P, 2 * P, "rounded1")
+        scatter(0, opening[:], 0, HALF)
+        quantize_w2(raw2, 2 * P, PASS, "rounded2")
+        behind = scratch([P, 5, PACK, P], F32, "raw%d" % (2 * P))
+        rest = behind[:, 4].rearrange("p u j -> p (u j)")
+        turn_back(*features(0, 0, HALF, rest, numbers=(4, 5, 0)))
+        scatter(0, rest, HALF, S)
         h0 = scratch([P, PACK - 1, S], F32, "rows")
-        features(1, 1, 0, h0[:, 0, :HALF])
-        features(2, 1, HALF, h0[:, 0, HALF:], tags=("rounded_w2_%d" % PASS, "second0"))
-        quantize_w2(raw2, 2 * P, PASS)
+        halves = [
+            features(1 + k, 1, k * HALF, h0[:, 0, k * HALF : (k + 1) * HALF], (behind[:, 2 * k], behind[:, 2 * k + 1]))
+            for k in range(2)
+        ]
+        for unit in halves:
+            turn_back(*unit)
         scatter(1, h0[:, 0], 0, S)
-        quantize_w2(raw4, PASS, H, cuts=(P,))
-        features(3, 2, 0, h0[:, 1, :HALF], numbers=(7, 6, 2))
+        quantize_w2(raw4, PASS, H, "raw%d" % (2 * P), cuts=(P,))
         damp_tile(0, 2, "raw%d" % PASS)
         for s in range(2):
             fetch_link(s)
-        features(4, 2, HALF, h0[:, 1, HALF:])
-        scatter(2, h0[:, 1], 0, S)
-        for k in range(2):
-            features(5 + k, 3, k * HALF, h0[:, 2, k * HALF : (k + 1) * HALF])
-        scatter(3, h0[:, 2], 0, S)
         h1 = scratch([P, PACK, S], F32, "table")
-        held = {3: ("first0", "damp2"), 7: ("size0", "size1")}
-        for u in range(S // P):
-            dealt_features(u + 7, u * P, h1, held.get(u))
+        held = {10: ("first0", "damp2"), 14: ("size0", "page7")}
+        pending = features(3, 2, 0, h0[:, 1, :HALF], numbers=(7, 6, 4))
+        for unit in range(4, 16):
+            ahead = None
+            if unit < 7:
+                s, k = divmod(unit + 1, 2)
+                ahead = features(unit, s, k * HALF, h0[:, s - 1, k * HALF : (k + 1) * HALF])
+            elif unit < 15:
+                ahead = dealt_features(unit, (unit - 7) * P, h1, terms_on(held[unit]) if unit in held else None)
+            turn_back(*pending)
+            if unit in (5, 7):
+                s = (unit - 1) // 2
+                scatter(s, h0[:, s - 1], 0, S)
+            pending = ahead
         damp_tile(2, PACK, "damp2")
         for s in range(2, PACK):
             fetch_link(s)
@@ -330,30 +339,35 @@ def tile_list_trie_leak_audit_kernel(
             fetch_link(s)
         scatter(6, h1[:, 2], 0, S)
 
-        damping([(0, 0, M), (1, 0, M)], ("size0", "size1"))
-        damping([(2, 0, M), (3, 0, M)], ("size0", "size1"))
+        for s in range(0, PACK, 2):
+            damping([(s, 0, M), (s + 1, 0, M)], ("size0", "page7"))
         early = scratch([P, PACK, HALF], F32, "rows")
-        fetch_nodes(0, 0, HALF, early[:])
+        for s in range(PACK):
+            fetch_nodes(s, 0, HALF, early[:, s])
         damping([(4, 0, M), (5, 0, M)], ("size0", "page7"))
         damp_tile(6, 7, "size0")
         fetch_link(6)
         load_page(7)
         scatter(7, h1[:, 3], 0, S)
-        quantize_z(0, 0, HALF, regroup(early[:])[:])
-        damping([(6, 0, HALF), (6, HALF, M)], ("size1", "late"))
-        damp_tile(7, 8, "size1")
-        fetch_link(7)
+        lying = [scratch([P, PACK * PASS], BF16, tag) for tag in ("raw%d" % (2 * P), "raw0")]
+        for s in range(PACK):
+            lay_down(early[:, s], s, 0, lying)
+        quantize_z(0, 0, HALF, stand_up(lying[0], "rounded0")[:])
+        damping([(6, 0, HALF), (6, HALF, M)], ("link7", "late"))
+        damp_tile(7, 8, "link7")
+        for lo in range(0, M, HALF):
+            fetch_link(7, lo, lo + HALF)
         late = scratch([P, PACK, HALF], F32, "late")
-        fetch_nodes(0, HALF, M, late[:])
-        damping([(7, 0, HALF), (7, HALF, M)], ("even", "rows"), "odd")
-        late_rounded = regroup(late[:])
+        for s in range(PACK):
+            fetch_nodes(s, HALF, M, late[:, s])
+        damping([(7, 0, HALF), (7, HALF, M)], ("even", "opening"), "odd")
+        for s in range(PACK):
+            lay_down(late[:, s], s, 1, lying)
 
         staged = scratch([P, N // P, M], F32, "table")
         out_rows = out.rearrange("(n p) m -> p n m", p=P)
         pair = [scratch([P, PACK, CHUNK], F32, tag) for tag in ("even", "odd")]
-        banks = []
-        for i, (lo, hi) in enumerate(PIECES):
-            banks.append([bank([P, 2, hi - lo], (2 * i + 6 + e) % 8) for e in range(2)])
+        banks = {}
 
         def finish(i):
             lo, hi = PIECES[i]
@@ -366,9 +380,9 @@ def tile_list_trie_leak_audit_kernel(
 
         for i, (lo, hi) in enumerate(PIECES):
             z = pair[i % 2][:, :, : hi - lo]
-            fetch_nodes(1, lo, hi, z)
-            if i == 1:
-                quantize_z(0, HALF, M, late_rounded[:])
+            for t in range(PACK):
+                fetch_nodes(PACK + t, lo, hi, z[:, t])
+            banks[i] = [bank([P, 2, hi - lo], (2 * i + 6 + e) % 8) for e in range(2)]
             scores_pass(0, banks[i], lo, hi)
             rounded = work.tile([P, PACK * (hi - lo)], BF16, name="rounded", tag="rounded", bufs=2, align_bytes=64)
             last = i == len(PIECES) - 1
@@ -378,6 +392,8 @@ def tile_list_trie_leak_audit_kernel(
                 z.rearrange("p t (c i) -> p c t i", i=run),
             )
             quantize_z(1, lo, hi, rounded[:])
+            if i == 0:
+                quantize_z(0, HALF, M, stand_up(lying[1], "rounded2")[:])
             scores_pass(1, banks[i], lo, hi)
             if i > 0:
                 finish(i - 1)

@@ -143,9 +143,9 @@ def tile_list_trie_leak_audit_kernel(
             nc.scalar.copy(first, view(sums[0]))
             return first, second, h, number
 
-        def turn_back(first, second, h, number):
+        def turn_back(first, second, h, number, tanh_last=False):
             turned = bank([P, PACK, P], number)
-            for e, term in enumerate((second, first)):
+            for e, term in enumerate((first, second) if tanh_last else (second, first)):
                 for u in range(PACK):
                     nc.tensor.matmul(
                         turned[:, u], term[:, u], ident[:], is_transpose=True,
@@ -247,22 +247,26 @@ def tile_list_trie_leak_audit_kernel(
                     start=(b == 0 and n % share == 0), stop=(b == BLOCKS - 1 and n % share == share - 1),
                 )
 
+        def load_table(lo, hi):
+            nc.sync.dma_start(out=tab_w[:, lo:hi], in_=tab_words[0].rearrange("p n t -> p (n t)").bitcast(I32)[:, lo:hi])
+
         nc.sync.dma_start(idx[:], offs)
         raw0 = load_w2(0, P)
+        load_table(0, T // 8)
         nc.sync.dma_start(out=tab_s[0:P:8, :].bitcast(I32), in_=tab_scales[0].bitcast(I32))
         for r in range(4):
             nc.sync.dma_start(out=w1_s[r:P:32, :].bitcast(I32), in_=w1_scales[0, r:16:4, :].bitcast(I32))
-        nc.sync.dma_start(out=tab_w[:], in_=tab_words[0].rearrange("p n t -> p (n t)").bitcast(I32))
+        load_table(T // 8, T)
         load_w1(0, 2 * P)
+        load_wg(0, HALF)
         nc.vector.tensor_copy(v_s_spread[:], tab_s[:].indirect(idx[:]))
         for r in range(4):
             nc.sync.dma_start(out=v_s[r:P:32, :].bitcast(I32), in_=v_s_spread[8 * r : P : 32, :].bitcast(I32))
-        raw1 = load_w2(P, 2 * P)
         load_page(0)
         nc.sync.dma_start(idx2[:], offs2)
-        load_wg(0, HALF)
-        raw2 = load_w2(2 * P, PASS)
+        raw1 = load_w2(P, 2 * P)
         load_wg(HALF, S)
+        raw2 = load_w2(2 * P, PASS)
         load_page(1)
         load_w1(2 * P, H)
         raw4 = load_w2(PASS, H)
@@ -294,36 +298,42 @@ def tile_list_trie_leak_audit_kernel(
         opening = scratch([P, HALF], F32, "opening")
         for q in range(2):
             first_features(opening, q)
-        quantize_w2(raw1, P, 2 * P, "rounded1")
         scatter(0, opening[:], 0, HALF)
-        quantize_w2(raw2, 2 * P, PASS, "rounded2")
-        behind = scratch([P, 5, PACK, P], F32, "raw%d" % (2 * P))
-        rest = behind[:, 4].rearrange("p u j -> p (u j)")
+        quantize_w2(raw1, P, 2 * P, "rounded1")
+        behind = scratch([P, 2, PACK, P], F32, "raw%d" % P)
+        rest = behind[:, 0].rearrange("p u j -> p (u j)")
         turn_back(*features(0, 0, HALF, rest, numbers=(4, 5, 0)))
         scatter(0, rest, HALF, S)
         h0 = scratch([P, PACK - 1, S], F32, "rows")
-        halves = [
-            features(1 + k, 1, k * HALF, h0[:, 0, k * HALF : (k + 1) * HALF], (behind[:, 2 * k], behind[:, 2 * k + 1]))
-            for k in range(2)
-        ]
-        for unit in halves:
-            turn_back(*unit)
-        scatter(1, h0[:, 0], 0, S)
+        turn_back(*features(1, 1, 0, h0[:, 0, :HALF], (behind[:, 1], terms_on(("rounded2",))[0])), tanh_last=True)
+        scatter(1, h0[:, 0, :HALF], 0, HALF)
+        quantize_w2(raw2, 2 * P, PASS, "rounded2", cuts=(P // 2,))
+        damp_tile(0, 1, "rounded2")
+        fetch_link(0)
+        both = scratch([P, 2, PACK, P], F32, "raw%d" % (2 * P))
+        turn_back(*features(2, 1, HALF, h0[:, 0, HALF:], (both[:, 0], both[:, 1])))
+        scatter(1, h0[:, 0, HALF:], HALF, S)
         quantize_w2(raw4, PASS, H, "raw%d" % (2 * P), cuts=(P,))
-        damp_tile(0, 2, "raw%d" % PASS)
-        for s in range(2):
-            fetch_link(s)
+        ring = scratch([P, 2, 2, PACK, P], F32, "raw%d" % PASS)
         h1 = scratch([P, PACK, S], F32, "table")
-        held = {10: ("first0", "damp2"), 14: ("size0", "page7")}
-        pending = features(3, 2, 0, h0[:, 1, :HALF], numbers=(7, 6, 4))
-        for unit in range(4, 16):
+        held = {3: "damp1", 10: "damp2", 14: "page7"}
+        numbers = {3: (7, 6, 4), 4: (0, 7, 5), 5: (3, 6, 4), 6: (1, 0, 5)}
+        pending = None
+        for unit in range(3, 16):
             ahead = None
+            if unit < 15:
+                first = terms_on(("size0",))[0] if unit == 14 else ring[:, unit % 2, 0]
+                second = terms_on((held[unit],))[0] if unit in held else ring[:, unit % 2, 1]
             if unit < 7:
                 s, k = divmod(unit + 1, 2)
-                ahead = features(unit, s, k * HALF, h0[:, s - 1, k * HALF : (k + 1) * HALF])
+                ahead = features(unit, s, k * HALF, h0[:, s - 1, k * HALF : (k + 1) * HALF], (first, second), numbers[unit])
             elif unit < 15:
-                ahead = dealt_features(unit, (unit - 7) * P, h1, terms_on(held[unit]) if unit in held else None)
-            turn_back(*pending)
+                ahead = dealt_features(unit, (unit - 7) * P, h1, (first, second))
+            if pending is not None:
+                turn_back(*pending)
+            if unit == 4:
+                damp_tile(1, 2, "damp1")
+                fetch_link(1)
             if unit in (5, 7):
                 s = (unit - 1) // 2
                 scatter(s, h0[:, s - 1], 0, S)

@@ -106,13 +106,17 @@ def tile_list_trie_leak_audit_kernel(
                 rows = page0[PASS:].rearrange("(p t) c -> t p c", t=PACK)[s - PACK]
             nc.sync.dma_start(out=pages[s][:], in_=rows)
 
-        def quantize_w2(raw, lo, hi, tag, cuts=()):
+        def quantize_w2(raws, lo, hi, tag, cuts=()):
             rounded = scratch([P, PACK * (hi - lo)], BF16, tag)
-            for c0, c1 in zip((0,) + cuts, cuts + (hi - lo,)):
-                nc.scalar.copy(
-                    rounded[:, PACK * c0 : PACK * c1].rearrange("p (c i j) -> p c j i", i=2, j=PACK),
-                    raw[:, :, c0:c1].rearrange("p j (c i) -> p c j i", i=2),
-                )
+            width = (hi - lo) // len(raws)
+            for n, raw in enumerate(raws):
+                for c0, c1 in zip((0,) + cuts, cuts + (width,)):
+                    nc.scalar.copy(
+                        rounded[:, PACK * (n * width + c0) : PACK * (n * width + c1)].rearrange(
+                            "p (c i j) -> p c j i", i=2, j=PACK
+                        ),
+                        raw[:, :, c0:c1].rearrange("p j (c i) -> p c j i", i=2),
+                    )
             nc.vector.quantize_mx(out=w2_w[:, lo:hi].bitcast(FP8X4), scales=w2_s[:, lo:hi], in_=rounded[:])
 
         def weights(lo, hi):
@@ -137,13 +141,13 @@ def tile_list_trie_leak_audit_kernel(
         def terms_on(tags):
             return [scratch([P, PACK, P], F32, tag)[:] for tag in tags]
 
-        def turn(unit, sums, view, h, terms, number):
+        def turn(unit, sums, view, terms, number):
             first, second = terms or terms_on(("first%d" % (unit % 2), "second%d" % (unit % 2)))
             nc.scalar.activation(second, view(sums[1]), ACT.Tanh, scale=-1.0)
             nc.scalar.copy(first, view(sums[0]))
-            return first, second, h, number
+            return first, second, number
 
-        def turn_back(first, second, h, number, tanh_last=False):
+        def turn_back(first, second, number, h, tanh_last=False):
             turned = bank([P, PACK, P], number)
             for e, term in enumerate((first, second) if tanh_last else (second, first)):
                 for u in range(PACK):
@@ -151,12 +155,12 @@ def tile_list_trie_leak_audit_kernel(
                         turned[:, u], term[:, u], ident[:], is_transpose=True,
                         start=(e == 0 and u == 0), stop=(e == 1 and u == PACK - 1),
                     )
-            nc.scalar.copy(h, turned[:])
+            nc.scalar.copy(h, turned[:] if len(h.shape) == 3 else turned[:].rearrange("p u j -> p (u j)"))
 
         def banks_of(unit):
             return 2 * (unit % 2), 2 * (unit % 2) + 1, 4 + unit % 4
 
-        def features(unit, s, lo, h, terms=None, numbers=None):
+        def features(unit, s, lo, terms=None, numbers=None):
             numbers = numbers or banks_of(unit)
             sums = [bank([P, PACK, P], number) for number in numbers[:2]]
             for acc, (codes, scales) in reversed(list(zip(sums, weights(s * P, (s + 1) * P)))):
@@ -166,9 +170,9 @@ def tile_list_trie_leak_audit_kernel(
                         out=acc[:, u], lhsT=v_w[:, cols].bitcast(FP8X4), lhsT_scale=v_s[:, cols],
                         rhs=codes, rhs_scale=scales, start=True, stop=True,
                     )
-            return turn(unit, sums, lambda acc: acc[:], h.rearrange("p (u j) -> p u j", u=PACK), terms, numbers[2])
+            return turn(unit, sums, lambda acc: acc[:], terms, numbers[2])
 
-        def dealt_features(unit, lo, h, terms=None):
+        def dealt_features(unit, lo, terms):
             sums = [bank([P, PASS], number) for number in banks_of(unit)[:2]]
             cols = slice(lo, lo + P)
             for acc, (codes, scales) in reversed(list(zip(sums, weights(PASS, H)))):
@@ -176,7 +180,7 @@ def tile_list_trie_leak_audit_kernel(
                     out=acc[:], lhsT=v_w[:, cols].bitcast(FP8X4), lhsT_scale=v_s[:, cols],
                     rhs=codes, rhs_scale=scales, start=True, stop=True,
                 )
-            return turn(unit, sums, lambda acc: acc[:].rearrange("j (p t) -> j t p", t=PACK), h[:, :, cols], terms, banks_of(unit)[2])
+            return turn(unit, sums, lambda acc: acc[:].rearrange("j (p t) -> j t p", t=PACK), terms, banks_of(unit)[2])
 
         def scatter(s, h, lo, hi):
             factor = wg[:, lo:hi] if s < PACK else wg_dealt[:, s - PACK, lo:hi]
@@ -269,7 +273,7 @@ def tile_list_trie_leak_audit_kernel(
         raw2 = load_w2(2 * P, PASS)
         load_page(1)
         load_w1(2 * P, H)
-        raw4 = load_w2(PASS, H)
+        raw4 = [load_w2(lo, lo + CHUNK) for lo in range(PASS, H, CHUNK)]
         nc.sync.dma_start(idx4[:], offs4)
         nc.sync.dma_start(idx3[:], offs3)
         with nc.allow_non_contiguous_dma(reason="one gain a partition and slice"):
@@ -292,32 +296,33 @@ def tile_list_trie_leak_audit_kernel(
                 in_=w3_scales[:, 4 * quadrant : 4 * quadrant + 4, :].bitcast(I32).rearrange("b r n -> r b n"),
             )
 
-        quantize_w2(raw0, 0, P, "rounded0")
+        quantize_w2([raw0], 0, P, "rounded0")
         for lo, hi in ((0, CHUNK), (CHUNK, HALF), (HALF, S)):
             nc.vector.tensor_copy(v_w[:, lo:hi], tab_w[:].bitcast(U32).indirect(entries(idx, lo, hi)))
         opening = scratch([P, HALF], F32, "opening")
         for q in range(2):
             first_features(opening, q)
         scatter(0, opening[:], 0, HALF)
-        quantize_w2(raw1, P, 2 * P, "rounded1")
-        behind = scratch([P, 2, PACK, P], F32, "raw%d" % P)
+        quantize_w2([raw1], P, 2 * P, "rounded1")
+        behind = scratch([P, 3, PACK, P], F32, "raw%d" % P)
         rest = behind[:, 0].rearrange("p u j -> p (u j)")
-        turn_back(*features(0, 0, HALF, rest, numbers=(4, 5, 0)))
+        turn_back(*features(0, 0, HALF, numbers=(4, 5, 0)), rest)
         scatter(0, rest, HALF, S)
-        h0 = scratch([P, PACK - 1, S], F32, "rows")
-        turn_back(*features(1, 1, 0, h0[:, 0, :HALF], (behind[:, 1], terms_on(("rounded2",))[0])), tanh_last=True)
-        scatter(1, h0[:, 0, :HALF], 0, HALF)
-        quantize_w2(raw2, 2 * P, PASS, "rounded2", cuts=(P // 2,))
-        damp_tile(0, 1, "rounded2")
-        fetch_link(0)
-        both = scratch([P, 2, PACK, P], F32, "raw%d" % (2 * P))
-        turn_back(*features(2, 1, HALF, h0[:, 0, HALF:], (both[:, 0], both[:, 1])))
-        scatter(1, h0[:, 0, HALF:], HALF, S)
-        quantize_w2(raw4, PASS, H, "raw%d" % (2 * P), cuts=(P,))
+        h0 = scratch([P, 5, HALF], F32, "rows")
+        units = [
+            features(1 + k, 1, k * HALF, (behind[:, 1 + k], terms_on((tag,))[0]))
+            for k, tag in enumerate(("rounded2", "rounded4"))
+        ]
+        turn_back(*units[0], h0[:, 0], tanh_last=True)
+        scatter(1, h0[:, 0], 0, HALF)
+        quantize_w2([raw2], 2 * P, PASS, "rounded2", cuts=(P // 2,))
+        after = scratch([P, HALF], F32, "raw%d" % (2 * P))
+        turn_back(*units[1], after[:], tanh_last=True)
+        scatter(1, after[:], HALF, S)
+        quantize_w2(raw4, PASS, H, "rounded4")
         ring = scratch([P, 2, 2, PACK, P], F32, "raw%d" % PASS)
         h1 = scratch([P, PACK, S], F32, "table")
-        held = {3: "damp1", 10: "damp2", 14: "page7"}
-        numbers = {3: (7, 6, 4), 4: (0, 7, 5), 5: (3, 6, 4), 6: (1, 0, 5)}
+        held = {3: "raw%d" % (PASS + CHUNK), 10: "damp2", 14: "page7"}
         pending = None
         for unit in range(3, 16):
             ahead = None
@@ -326,24 +331,24 @@ def tile_list_trie_leak_audit_kernel(
                 second = terms_on((held[unit],))[0] if unit in held else ring[:, unit % 2, 1]
             if unit < 7:
                 s, k = divmod(unit + 1, 2)
-                ahead = features(unit, s, k * HALF, h0[:, s - 1, k * HALF : (k + 1) * HALF], (first, second), numbers[unit])
+                ahead = features(unit, s, k * HALF, (first, second)) + (h0[:, unit - 2],)
             elif unit < 15:
-                ahead = dealt_features(unit, (unit - 7) * P, h1, (first, second))
+                lo = (unit - 7) * P
+                ahead = dealt_features(unit, lo, (first, second)) + (h1[:, :, lo : lo + P],)
             if pending is not None:
                 turn_back(*pending)
             if unit == 4:
-                damp_tile(1, 2, "damp1")
-                fetch_link(1)
+                damp_tile(0, 2, held[3])
+                for s in range(2):
+                    fetch_link(s)
             if unit in (5, 7):
-                s = (unit - 1) // 2
-                scatter(s, h0[:, s - 1], 0, S)
+                scatter((unit - 1) // 2, h0[:, unit - 4 : unit - 2].rearrange("p k j -> p (k j)"), 0, S)
             pending = ahead
         damp_tile(2, PACK, "damp2")
         for s in range(2, PACK):
             fetch_link(s)
-        for lo in range(0, S, HALF):
-            for s in range(4, 6):
-                scatter(s, h1[:, s - PACK, lo : lo + HALF], lo, lo + HALF)
+        for s in range(4, 6):
+            scatter(s, h1[:, s - PACK], 0, S)
         damp_tile(4, 6, "damp4")
         for s in range(4, 6):
             fetch_link(s)
@@ -359,7 +364,7 @@ def tile_list_trie_leak_audit_kernel(
         fetch_link(6)
         load_page(7)
         scatter(7, h1[:, 3], 0, S)
-        lying = [scratch([P, PACK * PASS], BF16, tag) for tag in ("raw%d" % (2 * P), "raw0")]
+        lying = [scratch([P, PACK * PASS], BF16, tag) for tag in ("rounded4", "raw0")]
         for s in range(PACK):
             lay_down(early[:, s], s, 0, lying)
         quantize_z(0, 0, HALF, stand_up(lying[0], "rounded0")[:])

@@ -347,8 +347,9 @@ def tile_list_trie_leak_audit_kernel(
         damp_tile(2, PACK, "damp2")
         for s in range(2, PACK):
             fetch_link(s)
-        for s in range(4, 6):
-            scatter(s, h1[:, s - PACK], 0, S)
+        for lo in range(0, S, HALF):
+            for s in range(4, 6):
+                scatter(s, h1[:, s - PACK, lo : lo + HALF], lo, lo + HALF)
         damp_tile(4, 6, "damp4")
         for s in range(4, 6):
             fetch_link(s)

@@ -25,6 +25,7 @@ BLOCKS = H // PASS
 CHUNK = 256
 HALF = 512
 PIECES = ((0, 256), (256, 512), (512, 768), (768, 896), (896, 1024))
+PIECE_BANKS = (6, 0, 2, 6, 0)
 
 
 def entries(offsets, lo, hi):
@@ -227,17 +228,16 @@ def tile_list_trie_leak_audit_kernel(
                 turned[:].rearrange("m u (p h e) -> m u h p e", h=2, e=2),
             )
 
-        def stand_up(lying, tag):
+        def stand_up(lying, v, rounded):
             pairs = lying[:].bitcast(F32).rearrange("m (u h p) -> m u h p", u=PACK, h=2)
-            rounded = scratch([P, PACK * HALF], BF16, tag)
-            words = rounded[:].bitcast(F32).rearrange("p (v u m h) -> p v u m h", u=2, m=P, h=2)
-            for v in range(2):
-                back = bank([P, 2, 2, P], 4 + v)
-                for u in range(2):
-                    for h in range(2):
-                        nc.tensor.transpose(back[:, u, h], pairs[:, 2 * v + u, h], ident[:])
-                nc.scalar.copy(words[:, v], back[:].rearrange("p u h m -> p u m h"))
-            return rounded
+            back = bank([P, 2, 2, P], 4 + v)
+            for u in range(2):
+                for h in range(2):
+                    nc.tensor.transpose(back[:, u, h], pairs[:, 2 * v + u, h], ident[:])
+            nc.scalar.copy(
+                rounded.bitcast(F32).rearrange("p (u m h) -> p u m h", u=2, h=2),
+                back[:].rearrange("p u h m -> p u m h"),
+            )
 
         def scores_pass(b, banks, lo, hi):
             share = N // P // len(banks)
@@ -304,14 +304,14 @@ def tile_list_trie_leak_audit_kernel(
             first_features(opening, q)
         scatter(0, opening[:], 0, HALF)
         quantize_w2([raw1], P, 2 * P, "rounded1")
-        behind = scratch([P, 3, PACK, P], F32, "raw%d" % P)
+        behind = scratch([P, 2, PACK, P], F32, "raw%d" % P)
         rest = behind[:, 0].rearrange("p u j -> p (u j)")
         turn_back(*features(0, 0, HALF, numbers=(4, 5, 0)), rest)
         scatter(0, rest, HALF, S)
         h0 = scratch([P, 5, HALF], F32, "rows")
         units = [
-            features(1 + k, 1, k * HALF, (behind[:, 1 + k], terms_on((tag,))[0]))
-            for k, tag in enumerate(("rounded2", "rounded4"))
+            features(1, 1, 0, terms_on(("first1", "rounded2"))),
+            features(2, 1, HALF, (behind[:, 1], terms_on(("rounded4",))[0])),
         ]
         turn_back(*units[0], h0[:, 0], tanh_last=True)
         scatter(1, h0[:, 0], 0, HALF)
@@ -368,7 +368,10 @@ def tile_list_trie_leak_audit_kernel(
         lying = [scratch([P, PACK * PASS], BF16, tag) for tag in ("rounded4", "raw0")]
         for s in range(PACK):
             lay_down(early[:, s], s, 0, lying)
-        quantize_z(0, 0, HALF, stand_up(lying[0], "rounded0")[:])
+        upright = scratch([P, PACK * HALF], BF16, "rounded0")
+        for v in range(2):
+            stand_up(lying[0], v, upright[:, v * PACK * CHUNK : (v + 1) * PACK * CHUNK])
+        quantize_z(0, 0, HALF, upright[:])
         damping([(6, 0, HALF), (6, HALF, M)], ("link7", "late"))
         damp_tile(7, 8, "link7")
         for lo in range(0, M, HALF):
@@ -398,7 +401,7 @@ def tile_list_trie_leak_audit_kernel(
             z = pair[i % 2][:, :, : hi - lo]
             for t in range(PACK):
                 fetch_nodes(PACK + t, lo, hi, z[:, t])
-            banks[i] = [bank([P, 2, hi - lo], (2 * i + 6 + e) % 8) for e in range(2)]
+            banks[i] = [bank([P, 2, hi - lo], PIECE_BANKS[i] + e) for e in range(2)]
             scores_pass(0, banks[i], lo, hi)
             rounded = work.tile([P, PACK * (hi - lo)], BF16, name="rounded", tag="rounded", bufs=2, align_bytes=64)
             last = i == len(PIECES) - 1
@@ -409,7 +412,10 @@ def tile_list_trie_leak_audit_kernel(
             )
             quantize_z(1, lo, hi, rounded[:])
             if i == 0:
-                quantize_z(0, HALF, M, stand_up(lying[1], "rounded2")[:])
+                for v in range(2):
+                    upright = scratch([P, PACK * CHUNK], BF16, "rounded%d" % (1 + v))
+                    stand_up(lying[1], v, upright[:])
+                    quantize_z(0, HALF + v * CHUNK, HALF + (v + 1) * CHUNK, upright[:])
             scores_pass(1, banks[i], lo, hi)
             if i > 0:
                 finish(i - 1)

@@ -76,9 +76,10 @@ def tile_list_trie_leak_audit_kernel(
         nc.vector.memset(tab_s[:].bitcast(I32), 0)
         nc.gpsimd.memset(w1_s[:].bitcast(I32), 0)
         nc.vector.memset(v_s[:].bitcast(I32), 0)
-        nc.gpsimd.memset(w3_s[:].bitcast(I32), 0)
-        nc.gpsimd.memset(one[:], 1.0)
-        make_identity(nc, ident[:])
+        nc.vector.memset(w3_s[:].bitcast(I32), 0)
+        nc.vector.memset(one[:], 1.0)
+        nc.vector.memset(ident[:], 0.0)
+        make_identity(nc, ident[:], nomemset=True)
 
         def load_w2(lo, hi):
             raw = scratch([P, PACK, hi - lo], F32, "raw%d" % lo)

@@ -221,7 +221,7 @@ def tile_list_trie_leak_audit_kernel(
             nc.vector.quantize_mx(out=z_w[:, cols].bitcast(FP8X4), scales=z_s[:, cols], in_=rounded)
 
         def lay_down(z, s, half, lying):
-            turned = bank([P, PACK, P], s)
+            turned = bank([P, PACK, P], (2 * s + half) % PACK)
             for u in range(PACK):
                 nc.tensor.transpose(turned[:, u], z[:, u * P : (u + 1) * P], ident[:])
             nc.scalar.copy(
@@ -358,9 +358,9 @@ def tile_list_trie_leak_audit_kernel(
 
         for s in range(0, PACK, 2):
             damping([(s, 0, M), (s + 1, 0, M)], ("size0", "page7"))
-        early = scratch([P, PACK, HALF], F32, "rows")
+        nodes = [scratch([P, 2, M], F32, tag) for tag in ("rows", "late")]
         for s in range(PACK):
-            fetch_nodes(s, 0, HALF, early[:, s])
+            fetch_nodes(s, 0, M, nodes[s // 2][:, s % 2])
         damping([(4, 0, M), (5, 0, M)], ("size0", "page7"))
         damp_tile(6, 7, "size0")
         fetch_link(6)
@@ -368,21 +368,19 @@ def tile_list_trie_leak_audit_kernel(
         scatter(7, h1[:, 3], 0, S)
         lying = [scratch([P, PACK * PASS], BF16, tag) for tag in ("rounded4", "raw0")]
         for s in range(PACK):
-            lay_down(early[:, s], s, 0, lying)
-        upright = scratch([P, PACK * HALF], BF16, "rounded0")
-        for v in range(2):
-            stand_up(lying[0], v, upright[:, v * PACK * CHUNK : (v + 1) * PACK * CHUNK])
-        quantize_z(0, 0, HALF, upright[:])
+            for half in range(2):
+                lay_down(nodes[s // 2][:, s % 2, half * HALF : (half + 1) * HALF], s, half, lying)
+        for half, tag in enumerate(("rounded0", "raw%d" % (2 * P))):
+            upright = scratch([P, PACK * HALF], BF16, tag)
+            for v in range(2):
+                stand_up(lying[half], v, upright[:, v * PACK * CHUNK : (v + 1) * PACK * CHUNK])
+            quantize_z(0, half * HALF, (half + 1) * HALF, upright[:])
         damping([(6, 0, HALF), (6, HALF, M)], ("link7", "late"))
         damp_tile(7, 8, "link7")
         for lo in range(0, M, HALF):
             fetch_link(7, lo, lo + HALF)
-        late = scratch([P, PACK, HALF], F32, "late")
-        for s in range(PACK):
-            fetch_nodes(s, HALF, M, late[:, s])
-        damping([(7, 0, HALF), (7, HALF, M)], ("even", "opening"), "odd")
-        for s in range(PACK):
-            lay_down(late[:, s], s, 1, lying)
+        damping([(7, 0, CHUNK), (7, CHUNK, HALF)], ("even", "opening"), "odd")
+        damping([(7, HALF, HALF + CHUNK), (7, HALF + CHUNK, M)], ("rounded1", "rounded2"))
 
         staged = scratch([P, N // P, M], F32, "table")
         out_rows = out.rearrange("(n p) m -> p n m", p=P)
@@ -412,11 +410,6 @@ def tile_list_trie_leak_audit_kernel(
                 z.rearrange("p t (c i) -> p c t i", i=run),
             )
             quantize_z(1, lo, hi, rounded[:])
-            if i == 0:
-                for v in range(2):
-                    upright = scratch([P, PACK * CHUNK], BF16, "rounded%d" % (1 + v))
-                    stand_up(lying[1], v, upright[:])
-                    quantize_z(0, HALF + v * CHUNK, HALF + (v + 1) * CHUNK, upright[:])
             scores_pass(1, banks[i], lo, hi)
             if i > 0:
                 finish(i - 1)

@@ -74,7 +74,7 @@ def tile_list_trie_leak_audit_kernel(
         one = keep.tile([P, 1], F32)
 
         nc.vector.memset(tab_s[:].bitcast(I32), 0)
-        nc.gpsimd.memset(w1_s[:].bitcast(I32), 0)
+        nc.vector.memset(w1_s[:].bitcast(I32), 0)
         nc.vector.memset(v_s[:].bitcast(I32), 0)
         nc.vector.memset(w3_s[:].bitcast(I32), 0)
         nc.vector.memset(one[:], 1.0)
@@ -259,9 +259,10 @@ def tile_list_trie_leak_audit_kernel(
         raw0 = load_w2(0, P)
         load_table(0, T // 8)
         nc.sync.dma_start(out=tab_s[0:P:8, :].bitcast(I32), in_=tab_scales[0].bitcast(I32))
+        load_table(T // 8, T // 2)
         for r in range(4):
             nc.sync.dma_start(out=w1_s[r:P:32, :].bitcast(I32), in_=w1_scales[0, r:16:4, :].bitcast(I32))
-        load_table(T // 8, T)
+        load_table(T // 2, T)
         load_w1(0, 2 * P)
         load_wg(0, HALF)
         nc.vector.tensor_copy(v_s_spread[:], tab_s[:].indirect(idx[:]))

@@ -257,9 +257,9 @@ def tile_list_trie_leak_audit_kernel(
 
         nc.sync.dma_start(idx[:], offs)
         raw0 = load_w2(0, P)
-        load_table(0, T // 8)
+        load_table(0, T // 16)
         nc.sync.dma_start(out=tab_s[0:P:8, :].bitcast(I32), in_=tab_scales[0].bitcast(I32))
-        load_table(T // 8, T // 2)
+        load_table(T // 16, T // 2)
         for r in range(4):
             nc.sync.dma_start(out=w1_s[r:P:32, :].bitcast(I32), in_=w1_scales[0, r:16:4, :].bitcast(I32))
         load_table(T // 2, T)

@@ -73,8 +73,8 @@ def tile_list_trie_leak_audit_kernel(
         ident = keep.tile([P, P], F32)
         one = keep.tile([P, 1], F32)
 
-        nc.vector.memset(tab_s[:].bitcast(I32), 0)
         nc.vector.memset(w1_s[:].bitcast(I32), 0)
+        nc.vector.memset(tab_s[: P - 16].bitcast(I32), 0)
         nc.vector.memset(v_s[:].bitcast(I32), 0)
         nc.vector.memset(w3_s[:].bitcast(I32), 0)
         nc.vector.memset(one[:], 1.0)
@@ -255,11 +255,10 @@ def tile_list_trie_leak_audit_kernel(
         def load_table(lo, hi):
             nc.sync.dma_start(out=tab_w[:, lo:hi], in_=tab_words[0].rearrange("p n t -> p (n t)").bitcast(I32)[:, lo:hi])
 
+        nc.sync.dma_start(out=tab_s[P - 16 :, :].bitcast(I32), in_=tab_scales[0].bitcast(I32))
         nc.sync.dma_start(idx[:], offs)
         raw0 = load_w2(0, P)
-        load_table(0, T // 16)
-        nc.sync.dma_start(out=tab_s[0:P:8, :].bitcast(I32), in_=tab_scales[0].bitcast(I32))
-        load_table(T // 16, T // 2)
+        load_table(0, T // 2)
         for r in range(4):
             nc.sync.dma_start(out=w1_s[r:P:32, :].bitcast(I32), in_=w1_scales[0, r:16:4, :].bitcast(I32))
         load_table(T // 2, T)
@@ -267,7 +266,7 @@ def tile_list_trie_leak_audit_kernel(
         load_wg(0, HALF)
         nc.vector.tensor_copy(v_s_spread[:], tab_s[:].indirect(idx[:]))
         for r in range(4):
-            nc.sync.dma_start(out=v_s[r:P:32, :].bitcast(I32), in_=v_s_spread[8 * r : P : 32, :].bitcast(I32))
+            nc.sync.dma_start(out=v_s[r:P:32, :].bitcast(I32), in_=v_s_spread[P - 16 + r : P : 4, :].bitcast(I32))
         load_page(0)
         nc.sync.dma_start(idx2[:], offs2)
         raw1 = load_w2(P, 2 * P)
@@ -377,7 +376,7 @@ def tile_list_trie_leak_audit_kernel(
                 stand_up(lying[half], v, upright[:, v * PACK * CHUNK : (v + 1) * PACK * CHUNK])
             quantize_z(0, half * HALF, (half + 1) * HALF, upright[:])
         damping([(6, 0, HALF), (6, HALF, M)], ("link7", "late"))
-        damp_tile(7, 8, "link7")
+        damp_tile(7, 8, "raw0")
         for lo in range(0, M, HALF):
             fetch_link(7, lo, lo + HALF)
         damping([(7, 0, CHUNK), (7, CHUNK, HALF)], ("even", "opening"), "odd")

@@ -25,7 +25,7 @@ BLOCKS = H // PASS
 CHUNK = 256
 HALF = 512
 PIECES = ((0, 256), (256, 512), (512, 768), (768, 896), (896, 1024))
-PIECE_BANKS = (6, 0, 2, 6, 0)
+PIECE_BANKS = (6, 0, 2, 6, 2)
 
 
 def entries(offsets, lo, hi):

@@ -24,6 +24,7 @@ PASS = P * PACK
 BLOCKS = H // PASS
 CHUNK = 256
 HALF = 512
+LEAD = 256
 PIECES = ((0, 256), (256, 512), (512, 768), (768, 896), (896, 1024))
 PIECE_BANKS = (6, 0, 2, 6, 2)
 
@@ -60,7 +61,9 @@ def tile_list_trie_leak_audit_kernel(
         v_s_spread = keep.tile([P, S], U8, align_bytes=64)
         v_s = keep.tile([P, S], U8, align_bytes=64)
         w1_w = keep.tile([P, 2 * H], U8, align_bytes=64)
-        w1_s = keep.tile([P, H], U8, align_bytes=64)
+        w1_s_rows = keep.tile([PACK, 4, LEAD // 4], I32)
+        w1_s_lead = keep.tile([P, LEAD], U8, align_bytes=64)
+        w1_s_rest = keep.tile([P, H - LEAD], U8, align_bytes=64)
         w2_w = keep.tile([P, H], U32, align_bytes=64)
         w2_s = keep.tile([P, H], U8, align_bytes=64)
         w3_w = keep.tile([P, BLOCKS * N], I32, align_bytes=64)
@@ -73,8 +76,9 @@ def tile_list_trie_leak_audit_kernel(
         ident = keep.tile([P, P], F32)
         one = keep.tile([P, 1], F32)
 
-        nc.vector.memset(w1_s[:].bitcast(I32), 0)
         nc.vector.memset(tab_s[: P - 16].bitcast(I32), 0)
+        nc.vector.memset(w1_s_lead[:].bitcast(I32), 0)
+        nc.vector.memset(w1_s_rest[:].bitcast(I32), 0)
         nc.vector.memset(v_s[:].bitcast(I32), 0)
         nc.vector.memset(w3_s[:].bitcast(I32), 0)
         nc.vector.memset(one[:], 1.0)
@@ -122,8 +126,9 @@ def tile_list_trie_leak_audit_kernel(
             nc.vector.quantize_mx(out=w2_w[:, lo:hi].bitcast(FP8X4), scales=w2_s[:, lo:hi], in_=rounded[:])
 
         def weights(lo, hi):
+            w1_s = w1_s_lead[:, lo:hi] if hi <= LEAD else w1_s_rest[:, lo - LEAD : hi - LEAD]
             return (
-                (w1_w[:, 2 * lo : 2 * hi].bitcast(FP4X4), w1_s[:, lo:hi]),
+                (w1_w[:, 2 * lo : 2 * hi].bitcast(FP4X4), w1_s),
                 (w2_w[:, lo:hi].bitcast(FP8X4), w2_s[:, lo:hi]),
             )
 
@@ -257,14 +262,18 @@ def tile_list_trie_leak_audit_kernel(
 
         nc.sync.dma_start(out=tab_s[P - 16 :, :].bitcast(I32), in_=tab_scales[0].bitcast(I32))
         nc.sync.dma_start(idx[:], offs)
+        w1_scale_words = w1_scales[0].bitcast(I32)
+        nc.sync.dma_start(
+            out=w1_s_rows[:], in_=w1_scale_words[:, : LEAD // 4].rearrange("(q i) c -> i q c", q=4)
+        )
         raw0 = load_w2(0, P)
         load_table(0, T // 2)
-        for r in range(4):
-            nc.sync.dma_start(out=w1_s[r:P:32, :].bitcast(I32), in_=w1_scales[0, r:16:4, :].bitcast(I32))
         load_table(T // 2, T)
         load_w1(0, 2 * P)
         load_wg(0, HALF)
         nc.vector.tensor_copy(v_s_spread[:], tab_s[:].indirect(idx[:]))
+        for quadrant in range(4):
+            nc.vector.tensor_copy(w1_s_lead[32 * quadrant : 32 * quadrant + 4].bitcast(I32), w1_s_rows[:, quadrant])
         for r in range(4):
             nc.sync.dma_start(out=v_s[r:P:32, :].bitcast(I32), in_=v_s_spread[P - 16 + r : P : 4, :].bitcast(I32))
         load_page(0)
@@ -276,6 +285,8 @@ def tile_list_trie_leak_audit_kernel(
         load_w1(2 * P, H)
         raw4 = [load_w2(lo, lo + CHUNK) for lo in range(PASS, H, CHUNK)]
         nc.sync.dma_start(idx4[:], offs4)
+        for r in range(4):
+            nc.sync.dma_start(out=w1_s_rest[r:P:32, :].bitcast(I32), in_=w1_scale_words[r:16:4, LEAD // 4 :])
         nc.sync.dma_start(idx3[:], offs3)
         with nc.allow_non_contiguous_dma(reason="one gain a partition and slice"):
             nc.sync.dma_start(out=gains[0][:], in_=gain[:PASS].rearrange("(s p) -> p s", p=P))

@@ -45,7 +45,7 @@ def tile_list_trie_leak_audit_kernel(
         psum = ctx.enter_context(tc.psum_pool(name="psum", bufs=1))
 
         def scratch(shape, dtype, tag):
-            return work.tile(shape, dtype, name=tag, tag=tag, align_bytes=64)
+            return work.tile(shape, dtype, name=tag, tag=tag, align_bytes=256)
 
         def bank(shape, number):
             return psum.tile(shape, F32, name="bank%d" % number, tag="bank%d" % number)
@@ -57,21 +57,21 @@ def tile_list_trie_leak_audit_kernel(
 
         tab_w = scratch([P, T], I32, "table")
         tab_s = scratch([P, T], U8, "page0")
-        v_w = keep.tile([P, S], U32, align_bytes=64)
-        v_s_spread = keep.tile([P, S], U8, align_bytes=64)
-        v_s = keep.tile([P, S], U8, align_bytes=64)
-        w1_w = keep.tile([P, 2 * H], U8, align_bytes=64)
-        w1_s_rows = keep.tile([PACK, 4, LEAD // 4], I32)
-        w1_s_lead = keep.tile([P, LEAD], U8, align_bytes=64)
-        w1_s_rest = keep.tile([P, H - LEAD], U8, align_bytes=64)
-        w2_w = keep.tile([P, H], U32, align_bytes=64)
-        w2_s = keep.tile([P, H], U8, align_bytes=64)
-        w3_w = keep.tile([P, BLOCKS * N], I32, align_bytes=64)
-        w3_s = keep.tile([P, BLOCKS * N], U8, align_bytes=64)
-        z_w = keep.tile([P, BLOCKS * M], U32, align_bytes=64)
-        z_s = keep.tile([P, BLOCKS * M], U8, align_bytes=64)
-        wg = keep.tile([P, S], F32)
-        wg_dealt = keep.tile([P, PACK, S], F32)
+        v_w = keep.tile([P, S], U32, align_bytes=256)
+        v_s_spread = scratch([P, S], U8, "damp4")
+        v_s = keep.tile([P, S], U8, align_bytes=256)
+        w1_w = keep.tile([P, 2 * H], U8, align_bytes=256)
+        w1_s_rows = scratch([PACK, 4, LEAD // 4], I32, "link7")
+        w1_s_lead = keep.tile([P, LEAD], U8, align_bytes=256)
+        w1_s_rest = keep.tile([P, H - LEAD], U8, align_bytes=256)
+        w2_w = keep.tile([P, H], U32, align_bytes=256)
+        w2_s = keep.tile([P, H], U8, align_bytes=256)
+        w3_w = keep.tile([P, BLOCKS * N], I32, align_bytes=256)
+        w3_s = keep.tile([P, BLOCKS * N], U8, align_bytes=256)
+        z_w = keep.tile([P, BLOCKS * M], U32, align_bytes=256)
+        z_s = keep.tile([P, BLOCKS * M], U8, align_bytes=256)
+        wg = keep.tile([P, S], F32, align_bytes=256)
+        wg_dealt = keep.tile([P, PACK, S], F32, align_bytes=256)
         gains = [keep.tile([P, PACK], F32, name="gain%d" % b) for b in range(BLOCKS)]
         ident = keep.tile([P, P], F32)
         one = keep.tile([P, 1], F32)
@@ -413,7 +413,7 @@ def tile_list_trie_leak_audit_kernel(
                 fetch_nodes(PACK + t, lo, hi, z[:, t])
             banks[i] = [bank([P, 2, hi - lo], PIECE_BANKS[i] + e) for e in range(2)]
             scores_pass(0, banks[i], lo, hi)
-            rounded = work.tile([P, PACK * (hi - lo)], BF16, name="rounded", tag="rounded", bufs=2, align_bytes=64)
+            rounded = work.tile([P, PACK * (hi - lo)], BF16, name="rounded", tag="rounded", bufs=2, align_bytes=256)
             last = i == len(PIECES) - 1
             copy, run = (nc.vector.tensor_copy, 4) if last else (nc.scalar.copy, 2)
             copy(

@@ -85,9 +85,9 @@ def tile_list_trie_leak_audit_kernel(
         nc.vector.memset(ident[:], 0.0)
         make_identity(nc, ident[:], nomemset=True)
 
-        def load_w2(lo, hi):
+        def load_w2(lo, hi, queue=nc.sync):
             raw = scratch([P, PACK, hi - lo], F32, "raw%d" % lo)
-            nc.sync.dma_start(out=raw[:], in_=w2.rearrange("(p j) c -> p j c", j=PACK)[:, :, lo:hi])
+            queue.dma_start(out=raw[:], in_=w2.rearrange("(p j) c -> p j c", j=PACK)[:, :, lo:hi])
             return raw
 
         def load_w1(lo, hi):
@@ -266,7 +266,7 @@ def tile_list_trie_leak_audit_kernel(
         nc.sync.dma_start(
             out=w1_s_rows[:], in_=w1_scale_words[:, : LEAD // 4].rearrange("(q i) c -> i q c", q=4)
         )
-        raw0 = load_w2(0, P)
+        raw0 = load_w2(0, P, nc.scalar)
         load_table(0, T // 2)
         load_table(T // 2, T)
         load_w1(0, 2 * P)

from contextlib import ExitStack

import concourse.mybir as mybir
from concourse.masks import make_identity

K, T, S, H, T2, M, N = 512, 4096, 1024, 1024, 2048, 1024, 512
FLOPS = 2 * K * H * S * 2 + 2 * H * N * M

F32 = mybir.dt.float32
BF16 = mybir.dt.bfloat16
I32 = mybir.dt.int32
U32 = mybir.dt.uint32
U16 = mybir.dt.uint16
U8 = mybir.dt.uint8
FP8X4 = mybir.dt.float8_e4m3fn_x4
FP4X4 = mybir.dt.float4_e2m1fn_x4
ACT = mybir.ActivationFunctionType
MULT = mybir.AluOpType.mult
SUBTRACT = mybir.AluOpType.subtract

P = 128
PACK = 4
PASS = P * PACK
BLOCKS = H // PASS
CHUNK = 256
HALF = 512
LEAD = 256
PIECES = ((0, 256), (256, 512), (512, 768), (768, 896), (896, 1024))
PIECE_BANKS = (6, 0, 2, 6, 2)


def entries(offsets, lo, hi):
    return offsets[:, lo // 16 : hi // 16]


def tile_list_trie_leak_audit_kernel(
    tc, tab_words, tab_scales, offs, offs2, offs3, offs4, page0, wgs,
    w1_words, w1_scales, w2, gain, w3_words, w3_scales, out,
):
    nc = tc.nc
    with ExitStack() as ctx:
        lists = ctx.enter_context(tc.tile_pool(name="lists", bufs=1))
        keep = ctx.enter_context(tc.tile_pool(name="keep", bufs=1))
        work = ctx.enter_context(tc.tile_pool(name="work", bufs=1))
        psum = ctx.enter_context(tc.psum_pool(name="psum", bufs=1))

        def scratch(shape, dtype, tag):
            return work.tile(shape, dtype, name=tag, tag=tag, align_bytes=256)

        def bank(shape, number):
            return psum.tile(shape, F32, name="bank%d" % number, tag="bank%d" % number)

        idx = lists.tile([P, S // 16], U16)
        idx2 = lists.tile([P, S // 16], U16)
        idx3 = lists.tile([P, M // 16], U16)
        idx4 = lists.tile([P, M // 16], U16)

        tab_w = scratch([P, T], I32, "table")
        tab_s = scratch([P, T], U8, "page0")
        v_w = keep.tile([P, S], U32, align_bytes=256)
        v_s_spread = scratch([P, S], U8, "damp4")
        v_s = keep.tile([P, S], U8, align_bytes=256)
        w1_w = keep.tile([P, 2 * H], U8, align_bytes=256)
        w1_s_rows = scratch([PACK, 4, LEAD // 4], I32, "link7")
        w1_s_lead = keep.tile([P, LEAD], U8, align_bytes=256)
        w1_s_rest = keep.tile([P, H - LEAD], U8, align_bytes=256)
        w2_w = keep.tile([P, H], U32, align_bytes=256)
        w2_s = keep.tile([P, H], U8, align_bytes=256)
        w3_w = keep.tile([P, BLOCKS * N], I32, align_bytes=256)
        w3_s = keep.tile([P, BLOCKS * N], U8, align_bytes=256)
        z_w = keep.tile([P, BLOCKS * M], U32, align_bytes=256)
        z_s = keep.tile([P, BLOCKS * M], U8, align_bytes=256)
        wg = keep.tile([P, S], F32, align_bytes=256)
        wg_dealt = keep.tile([P, PACK, S], F32, align_bytes=256)
        gains = [keep.tile([P, PACK], F32, name="gain%d" % b) for b in range(BLOCKS)]
        ident = keep.tile([P, P], F32)
        one = keep.tile([P, 1], F32)

        nc.vector.memset(tab_s[: P - 16].bitcast(I32), 0)
        nc.vector.memset(w1_s_lead[:].bitcast(I32), 0)
        nc.vector.memset(w1_s_rest[:].bitcast(I32), 0)
        nc.vector.memset(v_s[:].bitcast(I32), 0)
        nc.vector.memset(w3_s[:].bitcast(I32), 0)
        nc.vector.memset(one[:], 1.0)
        nc.vector.memset(ident[:], 0.0)
        make_identity(nc, ident[:], nomemset=True)

        def load_w2(lo, hi, queue=nc.sync):
            raw = scratch([P, PACK, hi - lo], F32, "raw%d" % lo)
            queue.dma_start(out=raw[:], in_=w2.rearrange("(p j) c -> p j c", j=PACK)[:, :, lo:hi])
            return raw

        def load_w1(lo, hi):
            cols = slice(2 * lo, 2 * hi)
            nc.sync.dma_start(out=w1_w[:, cols].bitcast(I32), in_=w1_words[0][:, cols].bitcast(I32))

        def load_wg(lo, hi):
            nc.sync.dma_start(out=wg[:, lo:hi], in_=wgs[:, lo:hi])

        def load_wg_dealt(t0, t1):
            rows = wgs.rearrange("(i t) c -> i t c", t=PACK)
            for quadrant in (0, 2, 1, 3):
                nc.sync.dma_start(out=wg_dealt[32 * quadrant : 32 * quadrant + 32, t0:t1], in_=rows[:, t0:t1])

        pages = {}

        def load_page(s):
            pages[s] = scratch([P, T2], F32, "page%d" % s)
            if s < PACK:
                rows = page0[s * P : (s + 1) * P]
            else:
                rows = page0[PASS:].rearrange("(p t) c -> t p c", t=PACK)[s - PACK]
            nc.sync.dma_start(out=pages[s][:], in_=rows)

        def quantize_w2(raws, lo, hi, tag, cuts=()):
            rounded = scratch([P, PACK * (hi - lo)], BF16, tag)
            width = (hi - lo) // len(raws)
            for n, raw in enumerate(raws):
                for c0, c1 in zip((0,) + cuts, cuts + (width,)):
                    nc.scalar.copy(
                        rounded[:, PACK * (n * width + c0) : PACK * (n * width + c1)].rearrange(
                            "p (c i j) -> p c j i", i=2, j=PACK
                        ),
                        raw[:, :, c0:c1].rearrange("p j (c i) -> p c j i", i=2),
                    )
            nc.vector.quantize_mx(out=w2_w[:, lo:hi].bitcast(FP8X4), scales=w2_s[:, lo:hi], in_=rounded[:])

        def weights(lo, hi):
            w1_s = w1_s_lead[:, lo:hi] if hi <= LEAD else w1_s_rest[:, lo - LEAD : hi - LEAD]
            return (
                (w1_w[:, 2 * lo : 2 * hi].bitcast(FP4X4), w1_s),
                (w2_w[:, lo:hi].bitcast(FP8X4), w2_s[:, lo:hi]),
            )

        def first_features(h, q):
            cols = slice(q * CHUNK, (q + 1) * CHUNK)
            sums = [bank([P, CHUNK], 2 * q + e) for e in range(2)]
            for acc, (codes, scales) in reversed(list(zip(sums, weights(0, P)))):
                nc.tensor.matmul_mx(
                    out=acc[:], lhsT=codes, lhsT_scale=scales,
                    rhs=v_w[:, cols].bitcast(FP8X4), rhs_scale=v_s[:, cols],
                    start=True, stop=True,
                )
            second = scratch([P, CHUNK], F32, "second%d" % q)
            nc.scalar.activation(second[:], sums[1][:], ACT.Tanh)
            nc.vector.tensor_tensor(h[:, cols], sums[0][:], second[:], SUBTRACT)

        def terms_on(tags):
            return [scratch([P, PACK, P], F32, tag)[:] for tag in tags]

        def turn(unit, sums, view, terms, number):
            first, second = terms or terms_on(("first%d" % (unit % 2), "second%d" % (unit % 2)))
            nc.scalar.activation(second, view(sums[1]), ACT.Tanh, scale=-1.0)
            nc.scalar.copy(first, view(sums[0]))
            return first, second, number

        def turn_back(first, second, number, h, tanh_last=False):
            turned = bank([P, PACK, P], number)
            for e, term in enumerate((first, second) if tanh_last else (second, first)):
                for u in range(PACK):
                    nc.tensor.matmul(
                        turned[:, u], term[:, u], ident[:], is_transpose=True,
                        start=(e == 0 and u == 0), stop=(e == 1 and u == PACK - 1),
                    )
            nc.scalar.copy(h, turned[:] if len(h.shape) == 3 else turned[:].rearrange("p u j -> p (u j)"))

        def banks_of(unit):
            return 2 * (unit % 2), 2 * (unit % 2) + 1, 4 + unit % 4

        def features(unit, s, lo, terms=None, numbers=None):
            numbers = numbers or banks_of(unit)
            sums = [bank([P, PACK, P], number) for number in numbers[:2]]
            for acc, (codes, scales) in reversed(list(zip(sums, weights(s * P, (s + 1) * P)))):
                for u in range(PACK):
                    cols = slice(lo + u * P, lo + (u + 1) * P)
                    nc.tensor.matmul_mx(
                        out=acc[:, u], lhsT=v_w[:, cols].bitcast(FP8X4), lhsT_scale=v_s[:, cols],
                        rhs=codes, rhs_scale=scales, start=True, stop=True,
                    )
            return turn(unit, sums, lambda acc: acc[:], terms, numbers[2])

        def dealt_features(unit, lo, terms):
            sums = [bank([P, PASS], number) for number in banks_of(unit)[:2]]
            cols = slice(lo, lo + P)
            for acc, (codes, scales) in reversed(list(zip(sums, weights(PASS, H)))):
                nc.tensor.matmul_mx(
                    out=acc[:], lhsT=v_w[:, cols].bitcast(FP8X4), lhsT_scale=v_s[:, cols],
                    rhs=codes, rhs_scale=scales, start=True, stop=True,
                )
            return turn(unit, sums, lambda acc: acc[:].rearrange("j (p t) -> j t p", t=PACK), terms, banks_of(unit)[2])

        def scatter(s, h, lo, hi):
            factor = wg[:, lo:hi] if s < PACK else wg_dealt[:, s - PACK, lo:hi]
            nc.vector.tensor_tensor(pages[s][:].indirect(entries(idx2, lo, hi)), h, factor, MULT)

        damps = {}

        def damp_tile(s0, s1, tag):
            tile = scratch([P, s1 - s0, M], F32, tag)
            for s in range(s0, s1):
                damps[s] = tile[:, s - s0]

        def fetch_link(s, lo=0, hi=M):
            nc.vector.tensor_copy(damps[s][:, lo:hi], pages[s][:].indirect(entries(idx4, lo, hi)))

        def damping(parts, tags, last_tag=None):
            values = [damps[s][:, lo:hi] for s, lo, hi in parts]
            sizes = [scratch([P, hi - lo], F32, tag)[:] for (s, lo, hi), tag in zip(parts, tags)]
            roots = list(values)
            if last_tag is not None:
                roots[1] = scratch([P, parts[1][2] - parts[1][1]], F32, last_tag)[:]
            for size, value in zip(sizes, values):
                nc.scalar.activation(size, value, ACT.Abs)
            for root, size in zip(roots, sizes):
                nc.scalar.activation(root, size, ACT.Abs_reciprocal_sqrt, bias=one[:])
            for root in roots:
                nc.scalar.activation(root, root, ACT.Square)
            for value, root, (s, lo, hi) in zip(values, roots, parts):
                nc.scalar.activation(value, root, ACT.Copy, scale=gains[s // PACK][:, s % PACK : s % PACK + 1])

        def fetch_nodes(s, lo, hi, z):
            nc.vector.tensor_tensor(z, pages[s][:].indirect(entries(idx3, lo, hi)), damps[s][:, lo:hi], MULT)

        def quantize_z(b, lo, hi, rounded):
            cols = slice(b * M + lo, b * M + hi)
            nc.vector.quantize_mx(out=z_w[:, cols].bitcast(FP8X4), scales=z_s[:, cols], in_=rounded)

        def lay_down(z, s, half, lying):
            turned = bank([P, PACK, P], (2 * s + half) % PACK)
            for u in range(PACK):
                nc.tensor.transpose(turned[:, u], z[:, u * P : (u + 1) * P], ident[:])
            nc.scalar.copy(
                lying[half][:].rearrange("m (u h s p e) -> m s u h p e", u=PACK, h=2, s=PACK, e=2)[:, s],
                turned[:].rearrange("m u (p h e) -> m u h p e", h=2, e=2),
            )

        def stand_up(lying, v, rounded):
            pairs = lying[:].bitcast(F32).rearrange("m (u h p) -> m u h p", u=PACK, h=2)
            back = bank([P, 2, 2, P], 4 + v)
            for u in range(2):
                for h in range(2):
                    nc.tensor.transpose(back[:, u, h], pairs[:, 2 * v + u, h], ident[:])
            nc.scalar.copy(
                rounded.bitcast(F32).rearrange("p (u m h) -> p u m h", u=2, h=2),
                back[:].rearrange("p u h m -> p u m h"),
            )

        def scores_pass(b, banks, lo, hi):
            share = N // P // len(banks)
            moving = slice(b * M + lo, b * M + hi)
            for n in range(N // P):
                cols = slice(b * N + n * P, b * N + (n + 1) * P)
                nc.tensor.matmul_mx(
                    out=banks[n // share][:, n % share],
                    lhsT=w3_w[:, cols].bitcast(FP8X4), lhsT_scale=w3_s[:, cols],
                    rhs=z_w[:, moving].bitcast(FP8X4), rhs_scale=z_s[:, moving],
                    start=(b == 0 and n % share == 0), stop=(b == BLOCKS - 1 and n % share == share - 1),
                )

        def load_table(lo, hi):
            nc.sync.dma_start(out=tab_w[:, lo:hi], in_=tab_words[0].rearrange("p n t -> p (n t)").bitcast(I32)[:, lo:hi])

        nc.sync.dma_start(out=tab_s[P - 16 :, :].bitcast(I32), in_=tab_scales[0].bitcast(I32))
        nc.sync.dma_start(idx[:], offs)
        w1_scale_words = w1_scales[0].bitcast(I32)
        nc.sync.dma_start(
            out=w1_s_rows[:], in_=w1_scale_words[:, : LEAD // 4].rearrange("(q i) c -> i q c", q=4)
        )
        raw0 = load_w2(0, P, nc.scalar)
        load_table(0, T // 2)
        load_table(T // 2, T)
        load_w1(0, 2 * P)
        load_wg(0, HALF)
        nc.vector.tensor_copy(v_s_spread[:], tab_s[:].indirect(idx[:]))
        for quadrant in range(4):
            nc.vector.tensor_copy(w1_s_lead[32 * quadrant : 32 * quadrant + 4].bitcast(I32), w1_s_rows[:, quadrant])
        for r in range(4):
            nc.sync.dma_start(out=v_s[r:P:32, :].bitcast(I32), in_=v_s_spread[P - 16 + r : P : 4, :].bitcast(I32))
        load_page(0)
        nc.sync.dma_start(idx2[:], offs2)
        raw1 = load_w2(P, 2 * P)
        load_wg(HALF, S)
        raw2 = load_w2(2 * P, PASS)
        load_page(1)
        load_w1(2 * P, H)
        raw4 = [load_w2(lo, lo + CHUNK) for lo in range(PASS, H, CHUNK)]
        nc.sync.dma_start(idx4[:], offs4)
        for r in range(4):
            nc.sync.dma_start(out=w1_s_rest[r:P:32, :].bitcast(I32), in_=w1_scale_words[r:16:4, LEAD // 4 :])
        nc.sync.dma_start(idx3[:], offs3)
        with nc.allow_non_contiguous_dma(reason="one gain a partition and slice"):
            nc.sync.dma_start(out=gains[0][:], in_=gain[:PASS].rearrange("(s p) -> p s", p=P))
        nc.sync.dma_start(out=gains[1][:], in_=gain[PASS:].rearrange("(p t) -> p t", t=PACK))
        for s in range(2, 6):
            load_page(s)
        load_wg_dealt(0, 2)
        load_page(6)
        load_wg_dealt(2, 3)
        load_wg_dealt(3, 4)
        for b in range(BLOCKS):
            nc.sync.dma_start(
                out=w3_w[:, b * N : (b + 1) * N],
                in_=w3_words[b].rearrange("p n t -> p (n t)").bitcast(I32),
            )
        for quadrant in range(4):
            nc.sync.dma_start(
                out=w3_s[32 * quadrant : 32 * quadrant + 4, :].bitcast(I32).rearrange("r (b n) -> r b n", b=BLOCKS),
                in_=w3_scales[:, 4 * quadrant : 4 * quadrant + 4, :].bitcast(I32).rearrange("b r n -> r b n"),
            )

        quantize_w2([raw0], 0, P, "rounded0")
        for lo, hi in ((0, CHUNK), (CHUNK, HALF), (HALF, S)):
            nc.vector.tensor_copy(v_w[:, lo:hi], tab_w[:].bitcast(U32).indirect(entries(idx, lo, hi)))
        opening = scratch([P, HALF], F32, "opening")
        for q in range(2):
            first_features(opening, q)
        scatter(0, opening[:], 0, HALF)
        quantize_w2([raw1], P, 2 * P, "rounded1")
        behind = scratch([P, 2, PACK, P], F32, "raw%d" % P)
        rest = behind[:, 0].rearrange("p u j -> p (u j)")
        turn_back(*features(0, 0, HALF, numbers=(4, 5, 0)), rest)
        scatter(0, rest, HALF, S)
        h0 = scratch([P, 5, HALF], F32, "rows")
        units = [
            features(1, 1, 0, terms_on(("first1", "rounded2"))),
            features(2, 1, HALF, (behind[:, 1], terms_on(("rounded4",))[0])),
        ]
        turn_back(*units[0], h0[:, 0], tanh_last=True)
        scatter(1, h0[:, 0], 0, HALF)
        quantize_w2([raw2], 2 * P, PASS, "rounded2", cuts=(P // 2,))
        after = scratch([P, HALF], F32, "raw%d" % (2 * P))
        turn_back(*units[1], after[:], tanh_last=True)
        scatter(1, after[:], HALF, S)
        quantize_w2(raw4, PASS, H, "rounded4")
        ring = scratch([P, 2, 2, PACK, P], F32, "raw%d" % PASS)
        h1 = scratch([P, PACK, S], F32, "table")
        held = {3: "raw%d" % (PASS + CHUNK), 10: "damp2", 14: "page7"}
        pending = None
        for unit in range(3, 16):
            ahead = None
            if unit < 15:
                first = terms_on(("size0",))[0] if unit == 14 else ring[:, unit % 2, 0]
                second = terms_on((held[unit],))[0] if unit in held else ring[:, unit % 2, 1]
            if unit < 7:
                s, k = divmod(unit + 1, 2)
                ahead = features(unit, s, k * HALF, (first, second)) + (h0[:, unit - 2],)
            elif unit < 15:
                lo = (unit - 7) * P
                ahead = dealt_features(unit, lo, (first, second)) + (h1[:, :, lo : lo + P],)
            if pending is not None:
                turn_back(*pending)
            if unit == 4:
                damp_tile(0, 2, held[3])
                for s in range(2):
                    fetch_link(s)
            if unit in (5, 7):
                scatter((unit - 1) // 2, h0[:, unit - 4 : unit - 2].rearrange("p k j -> p (k j)"), 0, S)
            pending = ahead
        damp_tile(2, PACK, "damp2")
        for s in range(2, PACK):
            fetch_link(s)
        for lo in range(0, S, HALF):
            for s in range(4, 6):
                scatter(s, h1[:, s - PACK, lo : lo + HALF], lo, lo + HALF)
        damp_tile(4, 6, "damp4")
        for s in range(4, 6):
            fetch_link(s)
        scatter(6, h1[:, 2], 0, S)

        for s in range(0, PACK, 2):
            damping([(s, 0, M), (s + 1, 0, M)], ("size0", "page7"))
        nodes = [scratch([P, 2, M], F32, tag) for tag in ("rows", "late")]
        for s in range(PACK):
            fetch_nodes(s, 0, M, nodes[s // 2][:, s % 2])
        damping([(4, 0, M), (5, 0, M)], ("size0", "page7"))
        damp_tile(6, 7, "size0")
        fetch_link(6)
        load_page(7)
        scatter(7, h1[:, 3], 0, S)
        lying = [scratch([P, PACK * PASS], BF16, tag) for tag in ("rounded4", "raw0")]
        for s in range(PACK):
            for half in range(2):
                lay_down(nodes[s // 2][:, s % 2, half * HALF : (half + 1) * HALF], s, half, lying)
        for half, tag in enumerate(("rounded0", "raw%d" % (2 * P))):
            upright = scratch([P, PACK * HALF], BF16, tag)
            for v in range(2):
                stand_up(lying[half], v, upright[:, v * PACK * CHUNK : (v + 1) * PACK * CHUNK])
            quantize_z(0, half * HALF, (half + 1) * HALF, upright[:])
        damping([(6, 0, HALF), (6, HALF, M)], ("link7", "late"))
        damp_tile(7, 8, "raw0")
        for lo in range(0, M, HALF):
            fetch_link(7, lo, lo + HALF)
        damping([(7, 0, CHUNK), (7, CHUNK, HALF)], ("even", "opening"), "odd")
        damping([(7, HALF, HALF + CHUNK), (7, HALF + CHUNK, M)], ("rounded1", "rounded2"))

        staged = scratch([P, N // P, M], F32, "table")
        out_rows = out.rearrange("(n p) m -> p n m", p=P)
        pair = [scratch([P, PACK, CHUNK], F32, tag) for tag in ("even", "odd")]
        banks = {}

        def finish(i):
            lo, hi = PIECES[i]
            share = N // P // len(banks[i])
            for e, sums in enumerate(banks[i]):
                rows = slice(e * share, (e + 1) * share)
                copy = nc.vector.tensor_copy if hi - lo == P and e == 0 else nc.scalar.copy
                copy(staged[:, rows, lo:hi], sums[:])
                nc.sync.dma_start(out=out_rows[:, rows, lo:hi], in_=staged[:, rows, lo:hi])

        for i, (lo, hi) in enumerate(PIECES):
            z = pair[i % 2][:, :, : hi - lo]
            for t in range(PACK):
                fetch_nodes(PACK + t, lo, hi, z[:, t])
            banks[i] = [bank([P, 2, hi - lo], PIECE_BANKS[i] + e) for e in range(2)]
            scores_pass(0, banks[i], lo, hi)
            rounded = work.tile([P, PACK * (hi - lo)], BF16, name="rounded", tag="rounded", bufs=2, align_bytes=256)
            last = i == len(PIECES) - 1
            copy, run = (nc.vector.tensor_copy, 4) if last else (nc.scalar.copy, 2)
            copy(
                rounded[:].rearrange("p (c i t) -> p c t i", i=run, t=PACK),
                z.rearrange("p t (c i) -> p c t i", i=run),
            )
            quantize_z(1, lo, hi, rounded[:])
            scores_pass(1, banks[i], lo, hi)
            if i > 0:
                finish(i - 1)
        finish(len(PIECES) - 1)
